import numpy as np, ml_dtypes
CORES = [5,29,101,125,133,157,229,253]
N = 8
import mx_ref
BF = ml_dtypes.bfloat16
def entries(a):
    return np.ascontiguousarray(a.T).reshape(-1)
def table(e):
    return np.ascontiguousarray(np.reshape(e, (-1, 16)).T).astype(np.int32)
def cols(t, e):
    v = np.concatenate([t.reshape(128, -1, 4), np.zeros((128, 1, 4), BF)], axis=1)
    return np.ascontiguousarray(v[:, e]).reshape(128, -1)
def cut(t, i, w=512):
    return t[:, w * i:w * i + w]
def pick(q, e):
    c = np.concatenate([q[0].reshape(128, -1, 4), np.zeros((128, 1, 4), np.uint8)], axis=1); s = np.concatenate([q[1], np.ones((16, 1), np.uint8)], axis=1)
    return (np.ascontiguousarray(c[:, e].reshape(128, -1)), np.ascontiguousarray(s[:, e]))
def join(*qs):
    return (np.concatenate([q[0] for q in qs], axis=1), np.concatenate([q[1] for q in qs], axis=1))
def put(q, e, v):
    c, s = q[0].reshape(128, -1, 4).copy(), q[1].copy(); c[:, e] = v[0].reshape(128, -1, 4); s[:, e] = v[1]
    return (c.reshape(128, -1), s)
def pk(c, s):
    return (np.ascontiguousarray(c), mx_ref.live(s))
def emit(q):
    return q[0], q[1]
def decode(q):
    o = []
    for b in range(4):
        e = np.zeros((128, 128, 4), np.float32); e[np.arange(128), np.arange(128), b] = 1
        o.append(mx_ref.matmul(mx_ref.quantize(e.reshape(128, 512).astype(BF)), q))
    return np.stack(o, axis=2).reshape(128, -1)
def f(rng, *shape):
    return mx_ref.flush((rng.standard_normal(shape, dtype=np.float32) * np.exp2(rng.integers(-2, 3, shape[:-1] + (1,)))).astype(BF))
def wide(rng, *shape, cols=0):
    v = rng.standard_normal(shape, dtype=np.float32) * np.exp2(rng.integers(-12, 13, shape)).astype(np.float32)
    if cols: v *= np.repeat(np.exp2(rng.integers(-cols, cols + 1, shape[:-2] + (1, shape[-1] // 4))) * (rng.random(shape[:-2] + (1, shape[-1] // 4)) > 0.0625), 4, axis=-1).astype(np.float32)
    return mx_ref.flush(v.astype(BF))
P, A, C, E, KP = 128, 16, 16, 8, 4
LC, M = 48, 5
def clean(v):
    v = np.array(v, np.float32)
    v[np.abs(v) < np.float32(2.0 ** -16)] = 0
    return v.astype(BF)
def lists(rng, full=False, own=False):
    out = []
    for r in range(N):
        pool = np.stack([P * q + rng.permutation(P)[:LC] for q in range(N)])
        must = np.zeros(0, int)
        if full: must = rng.permutation(pool[(r + 1 + rng.permutation(N - 1)[:M]) % N].reshape(-1))
        if own: must = P * r + rng.permutation(P)[:A * (C - 4)]
        rows = []
        for i in range(A):
            a = must[i::A]
            b = rng.permutation(np.setdiff1d(pool, a))[:C - a.size]
            rows.append(rng.permutation(np.concatenate([a, b])))
        out.append(table(np.concatenate(rows)))
    return {"cd": np.stack(out)}
def clusters(rng, n, low, high, noise):
    m = f(rng, 128, 4 * n).astype(np.float32).reshape(128, n, 4)
    h = rng.integers(0, n, (N, P))
    tb = np.stack([m[:, h[q]].reshape(128, -1) for q in range(N)]) + noise * f(rng, N, 128, 4 * P).astype(np.float32)
    a = low + (high - low) * rng.random((N, A, n))
    x = np.einsum("png,rin->rpig", m, a).reshape(N, 128, 4 * A) + noise * f(rng, N, 128, 4 * A).astype(np.float32)
    return {"tb": clean(tb), "x": clean(x), "w": f(rng, N, 128, 512)}
def setup_inputs(rng):
    return {**clusters(rng, 8, 0.2, 1.0, 0.5), **lists(rng)}
def setup_inputs_alike(rng):
    return {**clusters(rng, 3, 0.3, 0.7, 0.25), **lists(rng, full=True)}
def setup_inputs_one(rng):
    o, m, n = 0, min(A, LC // KP), P // KP
    kind = rng.permutation(P) % KP
    part = np.arange(128) // (128 // KP)
    tb = f(rng, N, 128, 4 * P).astype(np.float32).reshape(N, 128, P, 4) * np.float32(0.0625)
    tb[o] = (4 + 4 * rng.random((128, P, 4))) * (part[:, None] == kind[None, :])[:, :, None]
    order = np.stack([rng.permutation(np.flatnonzero(kind == k)) for k in range(KP)])
    out = []
    for r in range(N):
        size, at = (A, 0) if r == o else (m, A + m * (r - int(r > o)))
        big = P * o + order[:, (at + np.arange(A) % size) % n]
        pool = rng.permutation(np.concatenate([P * q + rng.permutation(P)[:LC] for q in range(N) if q != o]))
        rest = pool[:A * (C - KP)].reshape(A, C - KP)
        out.append(table(np.concatenate([rng.permutation(v) for v in np.concatenate([big.T, rest], axis=1)])))
    return {"tb": clean(tb.reshape(N, 128, 4 * P)), "x": clean(1 + rng.random((N, 128, 4 * A))), "w": f(rng, N, 128, 512), "cd": np.stack(out)}
def setup_inputs_ties(rng):
    m = clean(f(rng, 128, 12)).astype(np.float32).reshape(128, 3, 4)
    h = rng.integers(0, 3, (N, P))
    i = np.arange(A)
    k = np.where(i // 3 % 2 == 0, 1.0, 2.0)[None, :, None]
    tb = clean(np.stack([m[:, h[q]].reshape(128, -1) for q in range(N)])).reshape(N, 128, P, 4)
    x = clean(np.stack([(m[:, (i + r) % 3] * k).reshape(128, -1) for r in range(N)])).reshape(N, 128, A, 4)
    cd = lists(rng, own=True)["cd"]
    top = np.arange(128) < 64
    x[:, :, A - 2] = np.where(top, 4.0, 1.0).astype(BF)[None, :, None]
    x[:, :, A - 1] = np.where(top, -1.0, -4.0).astype(BF)[None, :, None]
    for r in range(N):
        g = rng.permutation(P)[:C + 1]
        g[:3] = np.sort(g[:3])
        tb[r][:, g[0]] = BF(-0.0)
        tb[r][:, g[1]] = BF(0.0)
        tb[r][:, g[2]] = np.array([1.0, -1.0, 1.0, -1.0]).astype(BF)[None, :]
        tb[r][:, g[3:]] = clean((1 + rng.random((128, C - 2, 4))) * np.where(top, -1.0, 1.0)[:, None, None])
        e = np.array(entries(cd[r])).reshape(A, C)
        e[A - 2] = P * r + rng.permutation(np.delete(g, 1))
        e[A - 1] = P * r + rng.permutation(np.delete(g, 0))
        cd[r] = table(e)
    return {"tb": tb.reshape(N, 128, 4 * P), "x": x.reshape(N, 128, 4 * A), "w": f(rng, N, 128, 512), "cd": cd}
def setup_inputs_shared(rng):
    place = np.stack([rng.permutation(P) for q in range(N)])
    tb = f(rng, N, 128, 4 * P).astype(np.float32).reshape(N, 128, P, 4) * np.float32(0.0625)
    part = np.arange(128) // (128 // KP)
    big = np.zeros((N, KP), int)
    for g in range(N):
        for k in range(KP):
            o = (g + k) % N
            tb[o, :, place[o, k]] = (4 + 4 * rng.random((128, 4))) * (part == k)[:, None]
            big[g, k] = P * o + place[o, k]
    out = []
    for r in range(N):
        pool = np.concatenate([P * q + rng.permutation(place[q, KP:])[:LC - KP] for q in range(N)])
        at = rng.integers(0, r + 1, A)
        at[0], at[A - 1] = 0, r
        out.append(table(np.concatenate([rng.permutation(np.concatenate([big[g], rng.permutation(pool)[:C - KP]])) for g in at])))
    return {"tb": clean(tb.reshape(N, 128, 4 * P)), "x": clean(1 + rng.random((N, 128, 4 * A))), "w": f(rng, N, 128, 512), "cd": np.stack(out)}
def setup_inputs_spread(rng):
    return {"tb": clean(wide(rng, N, 128, 4 * P, cols=6)), "x": clean(wide(rng, N, 128, 4 * A, cols=6)), "w": f(rng, N, 128, 512), **lists(rng)}
def check_inputs(d):
    b = []
    for k, low in (("tb", -16), ("x", -16), ("w", -30)):
        v = np.abs(d[k].astype(np.float32))
        if not (np.isfinite(v).all() and ((v == 0) | (v >= 2.0 ** low) & (v <= 2.0 ** 30)).all()): b.append("a value of " + k)
    for r in range(N):
        e = entries(d["cd"][r])
        if e.min() < 0 or e.max() >= N * P:
            b.append("cd: a number out of range")
            continue
        if any(len(set(v.tolist())) < C for v in e.reshape(A, C)): b.append("cd: a candidate twice at one point")
        n = np.bincount(np.unique(e) // P, minlength=N)
        n[r] = 0
        if n.max() > LC: b.append("cd: too many columns of one other rank")
    return b
def chosen(every, x, cd):
    kept = np.full((N, A, KP), -1)
    for r in range(N):
        e = entries(cd[r])
        t = cols(every, e)
        v = mx_ref.quantize(t)
        points = mx_ref.quantize(cols(x[r], np.concatenate([np.arange(A), np.full(128 - A, -1)])))
        s = mx_ref.matmul(points, v) + np.float32(0)
        g = np.concatenate([mx_ref.matmul(mx_ref.quantize(np.ascontiguousarray(cut(t, j))), v) for j in range(C * A // 128)]) + np.float32(0)
        for i in range(A):
            at = np.arange(C * i, C * i + C)
            best = at[np.lexsort((e[at], -s[i, at]))[:E]]
            mine = []
            for c in best:
                if len(mine) < KP and all(s[i, c] > g[c, k] for k in mine): mine.append(c)
            kept[r, i, :len(mine)] = e[mine]
    return kept
def reference(tb, x, w, cd):
    every = np.concatenate([tb[q] for q in range(N)], axis=1)
    kept = chosen(every, x, cd)
    y = np.zeros((N, 128, KP * A), np.float32)
    oc, osc = np.zeros((N, 128, 4 * P), np.uint8), np.zeros((N, 16, P), np.uint8)
    for r in range(N):
        y[r] = mx_ref.matmul(mx_ref.quantize(w[r]), mx_ref.quantize(cols(every, kept[r].reshape(-1))))
    dx = [decode(mx_ref.quantize(x[r])).reshape(128, A, 4) for r in range(N)]
    half = np.float32(0.5)
    for q in range(N):
        v = mx_ref.quantize(tb[q])
        m = decode(v).reshape(128, P, 4)
        named = np.zeros(P, bool)
        for r in range(N):
            for i in range(A):
                for c in kept[r, i]:
                    j = c - P * q
                    if 0 <= j < P and not named[j]:
                        m[:, j] = m[:, j] * half + dx[r][:, i] * half
                        named[j] = True
        at = np.flatnonzero(named)
        new = mx_ref.quantize(np.ascontiguousarray(m.reshape(128, -1).astype(BF)))
        oc[q], osc[q] = emit(put(v, at, pick(new, at)))
    return {"y": y, "kp": np.ascontiguousarray(kept.transpose(0, 2, 1)).astype(np.float32), "oc": oc, "osc": osc}

@@ -1,0 +1,472 @@
+from concourse.bass import DstId, RemoteDMATransfer
+from concourse.mybir import dt, AluOpType, AxisListType, ActivationFunctionType
+
+N, P, A, LC = 8, 128, 16, 48
+F32, BF, I32, U16, U8, X4 = "float32", "bfloat16", "int32", "uint16", "uint8", "float8_e4m3fn_x4"
+WCOLS = P + 7 * LC
+SCRATCH = {}
+
+
+def _sb(name, n, d):
+    SCRATCH[name] = ("sbuf", [128, n], d)
+
+
+for _n, _w, _d in [
+    ("cdi", 16, I32), ("cpi", 2, I32), ("tbt", 512, BF), ("xt", 512, BF), ("wt", 512, BF),
+    ("cdu", 32, U16), ("flg", 1024, BF), ("one", 128, BF), ("inc", 1024, BF), ("le", 2688, BF), ("cs", 2688, BF), ("rs", 2688, BF),
+    ("rq", 12, U16), ("rqx", 10, U16), ("rqr", 4, U16), ("rql", 22, U16),
+    ("tbc", 128, X4), ("tbs", 128, U8), ("wc", 480, X4), ("ws", 480, U8), ("fwc", 256, X4), ("fws", 256, U8),
+    ("xc", 128, X4), ("xs", 128, U8), ("wqc", 128, X4), ("wqs", 128, U8), ("pwc", 128, X4), ("pws", 128, U8),
+    ("dcc", 192, X4), ("dcs", 192, U8), ("dsc", 144, X4), ("dss", 144, U8), ("rlc", 96, X4), ("rls", 96, U8),
+    ("rpc", 16, X4), ("rps", 16, U8), ("kc", 288, X4), ("ks", 288, U8), ("ppc", 128, X4), ("pps", 128, U8),
+    ("foc", 128, X4), ("fos", 128, U8), ("ebt", 2048, BF), ("ec", 512, X4), ("es", 512, U8),
+    ("ii", 10, I32), ("fc", 28, F32), ("idx", 1040, F32), ("c16", 256, F32), ("wm", 256, F32), ("wmb", 128, BF), ("r16", 256, F32),
+    ("r16b", 128, BF), ("r64", 256, F32), ("lm", 64, F32), ("r17", 34, F32), ("r8", 32, F32), ("c4", 32, F32), ("zm", 64, F32),
+    ("half", 128, BF), ("hid", 128, BF), ("val", 512, BF), ("lgs", 6, U16), ("low2", 2, U16), ("lrep", 4, U16),
+    ("loc", 1040, F32), ("cdk", 16, U16), ("posr", 256, F32), ("posm", 256, F32), ("posc", 256, F32), ("kpl", 16, U16),
+    ("cpu", 2, U16), ("nr", 32, F32), ("lw", 32, F32),
+    ("pb", 288, F32), ("gs", 96, F32), ("tr", 64, F32), ("sr", 32, F32), ("qa", 192, F32), ("rku", 2, U16), ("ge2", 32, F32),
+    ("bsw", 40, F32), ("pk", 34, F32), ("bc", 64, F32), ("tm", 64, F32), ("own", 32, F32), ("msw", 40, I32), ("ms", 8, I32),
+    ("ui", 64, I32), ("fb", 64, F32), ("tmp", 8, F32), ("r4", 64, F32), ("qb", 192, F32), ("kl", 4, F32),
+    ("kr", 4, F32), ("ku", 4, U16), ("rw", 64, F32), ("rwm", 64, F32), ("eqd", 256, F32), ("scd", 256, F32), ("lf", 4, F32),
+    ("lu", 4, U16), ("lr", 4, U16), ("ll", 28, U16), ("kpf", 64, F32), ("locr", 192, F32), ("yl", 8, U16), ("zb", 480, F32), ("yb", 64, F32),
+    ("wns", 1120, BF), ("wnc", 1120, BF), ("wsm", 384, BF), ("wl", 8, F32), ("wu", 8, U16), ("fl", 8, U16), ("nt", 512, BF),
+]:
+    _sb(_n, _w, _d)
+for _n in ("pg0", "pg1", "pz", "pd0", "pd1", "pd2", "pd3"):
+    SCRATCH[_n] = ("psum", [128, 512], F32)
+SEMAPHORES = ["cv", "ca", "ct", "cg", "dcd", "dcp", "dtb", "dx", "dw", "dkx", "drep", "dy", "dkp", "doc", "ls",
+              "a_rqc", "a_rqs", "a_dt", "a_pt", "a_klc", "a_kls", "r_pt", "r_rq", "r_dt", "r_kl"]
+FILL = ("zm", "ebt", "r16", "r8", "r17", "r64", "rs", "r16b")
+PART = ("sk", "lerq", "lerqx", "lgs", "low2", "lrep", "loc", "cdk", "ui", "eqd", "bc", "yb", "c4")
+
+
+def _bits(es):
+    m = 0
+    for e in es:
+        m |= 1 << e
+    return m
+
+
+def _peers(topo, cores, r):
+    cross = [q for q in range(N) if q != r and not topo.may_write(cores[r], cores[q])]
+    same = [q for q in range(N) if q != r and topo.may_write(cores[r], cores[q])]
+    return cross, same
+
+
+def _relays(topo, cores, r):
+    cross, _ = _peers(topo, cores, r)
+    ok = [c for c in topo.cores_of(cores[r]) if c != cores[r] and topo.may_write(c, cores[cross[0]])]
+    d0 = [c for c in ok if topo.die(c) == topo.die(cores[r])]
+    d1 = [c for c in ok if topo.die(c) != topo.die(cores[r])]
+    return cross, [d0[0], d1[0], d0[1], d1[1]]
+
+
+def _dst(topo, d, s):
+    rid, pid = topo.addr(d, s)
+    return DstId(rid=rid, pnc=pid)
+
+
+def _same_engines(es):
+    return [es[0:4], es[4:6], es[6:8]], [es[0:2], es[2:4], es[4:8]]
+
+
+def _relay_program(g, core, T, topo, cores, r, x):
+    cross, _ = _peers(topo, cores, r)
+    h = x % 2
+    pair = cross[2 * h:2 * h + 2]
+    ids = [_dst(topo, cores[q], core) for q in pair]
+    es = topo.engines(core, cores[pair[0]])
+    place = [_peers(topo, cores, q)[0].index(r) for q in cross]
+    n = [0]
+
+    def fwd(ts):
+        out = []
+        for src, dsts, to, e, sem in ts:
+            out.append(RemoteDMATransfer(dst_ids=to, dma_engine_mask=_bits(e), remote_sem=T.sem[sem], srcs=[src], dsts=dsts))
+            n[0] += len(e)
+        g.remote_dma_fused(out, local_sem=T.sem.ls)
+
+    one = [_dst(topo, cores[cross[x]], core)]
+    non = len(topo.engines(cores[r], core))
+    a = 16 * r
+    w = [P + LC * place[2 * h], P + LC * place[2 * h + 1]]
+    g.wait_ge(T.sem.r_pt, non)
+    if x < 2:
+        fwd([(T.rpc[:].bitcast(dt.uint8), [T.pwc[:, a:a + 16].bitcast(dt.uint8)] * 2, ids, es, "a_pt")])
+    else:
+        fwd([(T.rps[:], [T.pws[:, a:a + 16]] * 2, ids, es, "a_pt")])
+    g.wait_ge(T.sem.r_rq, non // 4)
+    fwd([(T.rqr[:, 0:3], [T.rql[:, 3 * place[x]:3 * place[x] + 3]], one, es, "a_rqc")])
+    g.wait_ge(T.sem.r_dt, non // 2)
+    if x < 2:
+        fwd([(T.rlc[:, LC * k:LC * k + LC].bitcast(dt.uint8), [T.wc[:, w[k]:w[k] + LC].bitcast(dt.uint8)], [ids[k]], es[4 * k:4 * k + 4], "a_dt") for k in range(2)])
+    else:
+        fwd([(T.rls[:, LC * k:LC * k + LC], [T.ws[:, w[k]:w[k] + LC]], [ids[k]], es[4 * k:4 * k + 4], "a_dt") for k in range(2)])
+    g.wait_ge(T.sem.r_kl, non // 4)
+    fwd([(T.lr[:], [T.ll[:, 4 * place[x]:4 * place[x] + 4]], one, es, "a_klc")])
+    g.wait_ge(T.sem.ls, n[0])
+
+
+def rank_program(g, core, T, topo):
+    cores = T.cores
+    r = T.rank_of(core)
+    if r is None:
+        for k in range(N):
+            if cores[k] in topo.cores_of(core):
+                _, rel = _relays(topo, cores, k)
+                if core in rel:
+                    _relay_program(g, core, T, topo, cores, k, rel.index(core))
+        return
+
+    op_ = AluOpType
+    Copy = ActivationFunctionType.Copy
+    cross, rel = _relays(topo, cores, r)
+    _, same = _peers(topo, cores, r)
+    peers = cross + same
+
+    eng = {"v": g.vector, "a": g.scalar, "t": g.tensor, "g": g, "s": g.sync}
+    csem = {"v": "cv", "a": "ca", "t": "ct", "g": "cg"}
+    tot, seen, wr_, rd_, base_ = {}, {e: {} for e in eng}, {}, {}, {}
+
+    def need(e, toks):
+        want = {}
+        for s, c in toks:
+            c = tot[s] if c is None else c
+            want[s] = max(want.get(s, 0), c)
+        for s in want:
+            if seen[e].get(s, 0) < want[s]:
+                eng[e].wait_ge(T.sem[s], want[s])
+                seen[e][s] = want[s]
+
+    def do(e, fn, rd, wr):
+        mine = csem[e]
+        toks = []
+        for k in rd:
+            toks += wr_.get(k, [])
+        for k in wr:
+            old = wr_.get(k, []) + rd_.get(k, [])
+            if k in FILL or k in PART:
+                toks += [t for t in old if t[0] != mine] + base_.get(k, [])
+            else:
+                toks += old
+        need(e, toks)
+        fn(eng[e]).then_inc(T.sem[mine], 1)
+        tot[mine] = tot.get(mine, 0) + 1
+        tok = (mine, tot[mine])
+        for k in wr:
+            if k in FILL and k not in base_:
+                base_[k] = [tok]
+            wr_[k] = [t for t in wr_.get(k, []) if t[0] != mine] + [tok] if k in PART else [tok]
+            rd_[k] = []
+        for k in rd:
+            rd_[k] = [t for t in rd_.get(k, []) if t[0] != mine] + [tok]
+
+    def V(name, wr, rd, *args):
+        def fn(q):
+            f = {"copy": q.tensor_copy, "tt": q.tensor_tensor, "ts": q.tensor_scalar, "set": q.memset,
+                 "scan": q.tensor_tensor_scan, "tr": q.transpose, "qz": q.quantize_mx}[name]
+            return f(*args)
+        do("v", fn, rd.split(), wr.split())
+
+    def dma(e, sem, out, in_, rd, wr):
+        toks = []
+        for k in rd.split():
+            toks += wr_.get(k, [])
+        for k in wr.split():
+            toks += [t for t in wr_.get(k, []) + rd_.get(k, []) if t[0] != sem]
+        need(e, toks)
+        eng[e].dma_start(out, in_).then_inc(T.sem[sem], 16)
+        tot[sem] = tot.get(sem, 0) + 16
+        for k in wr.split():
+            wr_[k] = [(sem, None)]
+        for k in rd.split():
+            rd_[k] = rd_.get(k, []) + [(sem, None)]
+
+    def mm(out, l, ls, m, ms, start, stop, rd, wr):
+        do("t", lambda q: q.matmul_mx(out, l, ls, m, ms, start, stop), rd.split(), wr.split())
+
+    def u8(v):
+        return v.bitcast(dt.uint8)
+
+    def u32(v):
+        return v.bitcast(dt.uint32)
+
+    def send(transfers, rd):
+        need("g", wr_.get(rd, []))
+        ts = []
+        for src, dsts, ids, es, sem in transfers:
+            ts.append(RemoteDMATransfer(dst_ids=ids, dma_engine_mask=_bits(es), remote_sem=T.sem[sem], srcs=[src], dsts=dsts))
+            tot["ls"] = tot.get("ls", 0) + len(es)
+        g.remote_dma_fused(ts, local_sem=T.sem.ls)
+
+    ids_r = [_dst(topo, c, core) for c in rel]
+    ids_s = [_dst(topo, cores[q], core) for q in same]
+    eon = topo.engines(core, rel[0])
+    eoff = topo.engines(core, cores[same[0]])
+    noff = len(eoff)
+    per = len(eon) // 4
+    e_r = [eon[per * x:per * x + per] for x in range(4)]
+    e_h = [eon[0:2 * per], eon[2 * per:4 * per]]
+    e_s, e_s2 = _same_engines(eoff)
+    at_s = []
+    from_s = []
+    for q in same:
+        cq, sq = _peers(topo, cores, q)
+        at_s.append(4 + sq.index(r))
+        from_s.append(sq.index(r))
+
+    pin, ti, gi, oi, o7 = [T.ii[:, 2 * k:2 * k + 2] for k in range(5)]
+    pin1, oi1 = T.ii[:, 0:1], T.ii[:, 6:7]
+    tf = T.fc[:, 0:1]
+    sk = [T.fc[:, 2 + k:3 + k] for k in range(4)]
+    trs = [T.fc[:, 6 + k:7 + k] for k in range(4)]
+    cpf = T.fc[:, 26:28]
+    ge, gt, tt, cmp_, sc, slf = [T.qa[:, 32 * k:32 * k + 32] for k in range(6)]
+    k4, ps, kn, eq, v4, sc8 = [T.qb[:, 32 * k:32 * k + 32] for k in range(6)]
+
+    for k in range(8):
+        dma("s" if k % 2 == 0 else "a", "dcd", T.cdi[16 * k:16 * k + 16, :], T.cd[:], "", "cdi")
+    dma("a", "dx", T.xt[:, 0:64], T.x[:], "", "xt")
+    dma("s", "dtb", T.tbt[:], T.tb[:], "", "tbt")
+    dma("a", "dw", T.wt[:], T.w[:], "", "wt")
+    for k in range(8):
+        dma("s", "dcp", T.cpi[16 * k:16 * k + 16, :], T.cd[:, 2 * k:2 * k + 2], "", "cpi")
+
+    do("g", lambda q: q.iota(pin, [[0, 2]], 0, 1), [], ["pin"])
+    do("g", lambda q: q.iota(T.c16[:], [[0, 16], [1, 16]], 0, 0, allow_small_or_imprecise_dtypes=True), [], ["c16"])
+    do("g", lambda q: q.iota(T.fc[:, 10:18], [[16, 8]], 0, 0, allow_small_or_imprecise_dtypes=True), [], ["k16"])
+
+    V("set", "flg", "", T.flg[:], 0.0)
+    V("set", "one", "", T.one[:], 1.0)
+    V("set", "xtz", "", T.xt[:, 64:512], 0.0)
+    V("ts", "ti", "pin", ti, pin, 15, None, op_.bitwise_and)
+    V("copy", "tf", "ti", T.fc[:, 0:2], ti)
+    for k in range(4):
+        V("ts", "sk", "tf", sk[k], tf, float(16 * k), None, op_.add)
+    V("set", "rs", "", T.rs[:], 1.0)
+    V("set", "rs", "", T.rs[:, 0:2688:128], 0.0)
+
+    V("copy", "cdu", "cdi", T.cdu[:, 0:32:2], T.cdi[:])
+    for i in range(A):
+        V("copy", "flg", "cdu one", T.flg[:].indirect(T.cdu[:, 2 * i:2 * i + 1]), T.one[:, 0:16])
+        if i == 2:
+            V("qz", "xc xs", "xt xtz", T.xc[:], T.xs[:], T.xt[:])
+            send([(u8(T.xc[:, 0:16]), [u8(T.rpc[:])] * 2, ids_r[0:2], eon, "r_pt")], "xc")
+            send([(T.xs[:, 0:16], [T.rps[:]] * 2, ids_r[2:4], eon, "r_pt")], "xs")
+
+    def lists(qs, base, name, out):
+        n = len(qs)
+        for x, q in enumerate(qs):
+            V("scan", "inc%d" % q, "flg one", T.inc[:, P * q:P * q + P], T.one[:], T.flg[:, P * q:P * q + P], 0.0, op_.mult, op_.add)
+        for x, q in enumerate(qs):
+            for k in range(3):
+                a = base + P * (3 * x + k)
+                V("ts", "le" + name, "inc%d sk" % q, T.le[:, a:a + P], T.inc[:, P * q:P * q + P], sk[k], None, op_.is_le)
+        e = base + P * 3 * n
+        V("scan", "cs" + name, "rs le" + name, T.cs[:, base:e], T.rs[:, base:e], T.le[:, base:e], 0.0, op_.mult, op_.add)
+        V("ts", name, "cs" + name, out, T.cs[:, base + P - 1:e:P], float(P - 1), None, op_.min)
+
+    lists(cross, 0, "rq", T.rq[:])
+    send([(T.rq[:, 3 * x:3 * x + 3], [T.rqr[:, 0:3]], [ids_r[x]], e_r[x], "r_rq") for x in range(4)], "rq")
+    lists(same, 1536, "rqx", T.rqx[:, 0:9])
+    send([(T.rqx[:, 3 * y:3 * y + 3], [T.rql[:, 3 * at_s[y]:3 * at_s[y] + 3]], [ids_s[y]], e_s[y], "a_rqs") for y in range(3)], "rqx")
+    do("g", lambda q: q.iota(T.idx[:], [[1, 1040]], 0, 0, allow_small_or_imprecise_dtypes=True), [], ["idx"])
+
+    dma("s", "dkx", u8(T.kc[:, 0:16]), u8(T.xc[:, 0:16]), "xc", "kcx")
+    dma("s", "dkx", u8(T.kc[:, 272:288]), u8(T.xc[:, 0:16]), "xc", "kcx")
+    dma("s", "dkx", u8(T.pwc[:, 16 * r:16 * r + 16]), u8(T.xc[:, 0:16]), "xc", "pwo")
+    dma("s", "dkx", T.ks[:, 0:16], T.xs[:, 0:16], "xs", "ksx")
+    dma("s", "dkx", T.ks[:, 272:288], T.xs[:, 0:16], "xs", "ksx")
+    dma("s", "dkx", T.pws[:, 16 * r:16 * r + 16], T.xs[:, 0:16], "xs", "pwo")
+
+    V("qz", "tbc tbs", "tbt", T.tbc[:], T.tbs[:], T.tbt[:])
+    V("set", "r16", "", T.r16[:], 1.0)
+    V("set", "r16", "", T.r16[:, 0:256:16], 0.0)
+    V("ts", "wm", "c16 tf", T.wm[:], T.c16[:], tf, None, op_.is_equal)
+    for x, q in enumerate(peers):
+        V("ts", "loc", "inc%d" % q, T.loc[:, 1 + P * q:1 + P * q + P], T.inc[:, P * q:P * q + P], float(P + LC * x - 1), None, op_.add)
+    V("set", "loc", "", T.loc[:, 0:1], float(WCOLS))
+    V("set", "loc", "", T.loc[:, 1025:1040], float(WCOLS))
+
+    tot["a_rqc"] = 4 * noff
+    tot["a_rqs"] = sum(len(e_s[f]) for f in from_s)
+    wr_["rqlc"] = [("a_rqc", tot["a_rqc"])]
+    wr_["rqls"] = [("a_rqs", tot["a_rqs"])]
+    do("a", lambda q: q.activation(T.dcs[:], T.tbs[:].indirect(T.rql[:, 0:12]), Copy), ["tbs", "rqlc"], ["dcs"])
+    V("copy", "dcc", "tbc rqlc", u32(T.dcc[:]), u32(T.tbc[:]).indirect(T.rql[:, 0:12]))
+    do("a", lambda q: q.activation(T.dss[:], T.tbs[:].indirect(T.rql[:, 12:21]), Copy), ["tbs", "rqls"], ["dss"])
+    V("copy", "dsc", "tbc rqls", u32(T.dsc[:]), u32(T.tbc[:]).indirect(T.rql[:, 12:21]))
+    send([(u8(T.dcc[:, 96 * h:96 * h + 96]), [u8(T.rlc[:])], [ids_r[h]], e_h[h], "r_dt") for h in range(2)], "dcc")
+    send([(T.dcs[:, 96 * h:96 * h + 96], [T.rls[:]], [ids_r[2 + h]], e_h[h], "r_dt") for h in range(2)], "dcs")
+    ws_ = [P + LC * at_s[y] for y in range(3)]
+    send([(u8(T.dsc[:, LC * y:LC * y + LC]), [u8(T.wc[:, ws_[y]:ws_[y] + LC])], [ids_s[y]], e_s[y], "a_dt") for y in range(3)], "dsc")
+    send([(T.dss[:, LC * y:LC * y + LC], [T.ws[:, ws_[y]:ws_[y] + LC]], [ids_s[y]], e_s2[y], "a_dt") for y in range(3)], "dss")
+    send([(u8(T.xc[:, 0:16]), [u8(T.pwc[:, 16 * r:16 * r + 16])] * 3, ids_s, eoff, "a_pt")], "xc")
+    send([(T.xs[:, 0:16], [T.pws[:, 16 * r:16 * r + 16]] * 3, ids_s, eoff, "a_pt")], "xs")
+
+    V("ts", "loc", "idx", T.loc[:, 1 + P * r:1 + P * r + P], T.idx[:, 0:P], 0.0, None, op_.add)
+    V("ts", "cdk", "cdi", T.cdk[:, 0:8], T.cdi[:, 0:16:2], 1.0, None, op_.add)
+    V("ts", "cdk", "cdi", T.cdk[:, 8:16], T.cdi[:, 1:16:2], 1.0, None, op_.add)
+    V("copy", "posr", "loc cdk", T.posr[:], T.loc[:].indirect(T.cdk[:]))
+    V("tt", "posm", "posr wm", T.posm[:], T.posr[:], T.wm[:], op_.mult)
+    V("scan", "posc", "posm r16", T.posc[:], T.r16[:], T.posm[:], 0.0, op_.mult, op_.add)
+    V("copy", "kpl", "posc", T.kpl[:], T.posc[:, 15:256:16])
+    V("qz", "wco wso", "tbt", T.wc[:, 0:P], T.ws[:, 0:P], T.tbt[:])
+    V("qz", "wqc wqs", "wt", T.wqc[:], T.wqs[:], T.wt[:])
+    V("copy", "cpf", "cpi", cpf, T.cpi[:])
+    V("copy", "cpu", "cpi", T.cpu[:], T.cpi[:])
+    V("copy", "nr", "idx cpu", T.nr[:], T.idx[:].indirect(T.cpu[:]))
+    for j in range(2):
+        V("ts", "lw%d" % j, "nr cpf", T.lw[:, 16 * j:16 * j + 16], T.nr[:, 16 * j:16 * j + 16], T.fc[:, 26 + j:27 + j], None, op_.is_lt)
+        V("ts", "slf%d" % j, "c16 tf", T.qa[:, 160 + 16 * j:176 + 16 * j], T.c16[:, 0:16], tf, float(1 + 17 * j), op_.is_equal, op_.mult)
+    V("tt", "lw", "lw0 lw1 slf0 slf1", T.lw[:], T.lw[:], slf, op_.add)
+    V("ts", "bsw", "cpf", T.bsw[:, 0:34:17], cpf, 1.0, None, op_.add)
+    V("ts", "gi", "pin", gi, pin, 4, None, op_.logical_shift_right)
+    V("ts", "oi", "pin", oi, pin, 31, None, op_.bitwise_and)
+    V("ts", "o7", "pin", o7, pin, 7, None, op_.bitwise_and)
+    V("ts", "lgs", "pin", T.lgs[:, 0:1], pin1, 16.0, None, op_.add)
+    V("ts", "lgs", "pin", T.lgs[:, 1:2], pin1, 144.0, None, op_.add)
+    V("ts", "lgs", "gi", T.lgs[:, 2:4], gi, 2.0, None, op_.mult)
+    V("ts", "lgs", "gi", T.lgs[:, 4:6], gi, 2.0, 273.0, op_.mult, op_.add)
+    V("ts", "low2", "oi", T.low2[:, 0:1], oi1, 0.0, None, op_.add)
+    V("ts", "low2", "oi", T.low2[:, 1:2], oi1, 32.0, None, op_.add)
+    V("ts", "lrep", "o7", T.lrep[:, 0:2], o7, 0.0, None, op_.add)
+    V("ts", "lrep", "o7", T.lrep[:, 2:4], o7, 56.0, None, op_.add)
+    V("set", "r17", "", T.r17[:], 2.0)
+    V("set", "r17", "", T.r17[:, 0:34:17], 0.0)
+    V("set", "zm", "", T.zm[:], 0.0)
+    for a in (0, 16, 40, 56):
+        V("set", "zm", "", T.zm[:, a:a + 8], 1.0)
+    V("set", "r8", "", T.r8[:], 1.0)
+    V("set", "r8", "", T.r8[:, 0:32:8], 0.0)
+    for k in range(4):
+        V("set", "c4", "", T.c4[:, 8 * k:8 * k + 8], float(k + 1))
+    V("set", "fb", "", T.fb[:, 0:1], 0.0)
+    V("set", "half", "", T.half[:], 0.5)
+    do("g", lambda q: q.affine_select(T.hid[:], T.half[:], [[-1, 128]], op_.is_equal, 0.0, 0, 1), ["half"], ["hid"])
+    do("g", lambda q: q.iota(T.val[:], [[16, 8], [0, 4], [1, 16]], 0, 0, allow_small_or_imprecise_dtypes=True), [], ["val"])
+
+    tot["a_dt"] = 4 * noff + sum(len(e_s[f]) + len(e_s2[f]) for f in from_s)
+    wr_["wca"] = [("a_dt", tot["a_dt"])]
+    do("a", lambda q: q.activation(T.ks[:, 16:272], T.ws[:, 0:WCOLS].indirect(T.kpl[:]), Copy), ["wso", "wca", "kpl"], ["ks"])
+    V("copy", "kc", "wco wca kpl", u32(T.kc[:, 16:272]), u32(T.wc[:, 0:WCOLS]).indirect(T.kpl[:]))
+    mm(T.pg0[:, 0:144], T.kc[:, 16:144], T.ks[:, 16:144], T.kc[:, 0:144], T.ks[:, 0:144], True, True, "kc ks kcx ksx", "pg0")
+    mm(T.pg1[:, 0:144], T.kc[:, 144:272], T.ks[:, 144:272], T.kc[:, 144:288], T.ks[:, 144:288], True, True, "kc ks kcx ksx", "pg1")
+    mm(T.pz[:, 0:WCOLS], T.wqc[:], T.wqs[:], T.wc[:, 0:WCOLS], T.ws[:, 0:WCOLS], True, True, "wqc wqs wco wso wca", "pz")
+    V("copy", "pb0", "pg0", T.pb[:, 0:144], T.pg0[:, 0:144])
+    do("a", lambda q: q.activation(T.pb[:, 144:288], T.pg1[:, 0:144], Copy), ["pg1"], ["pb1"])
+    do("a", lambda q: q.activation(T.zb[:, 0:WCOLS], T.pz[:, 0:WCOLS], Copy), ["pz"], ["zb"])
+    V("copy", "gs", "pb0 pb1 lgs", T.gs[:], T.pb[:].indirect(T.lgs[:]))
+    V("tr", "tr", "gs", T.tr[:], T.gs[:, 32:96])
+    V("tt", "ge2", "gs", T.ge2[:], T.gs[:, 0:32], T.gs[:, 48:80], op_.is_ge)
+    V("copy", "sr", "tr low2", T.sr[:], T.tr[:].indirect(T.low2[:]))
+    V("tt", "ge", "sr gs", ge, T.sr[:], T.gs[:, 48:80], op_.is_ge)
+    V("tt", "gt", "sr gs", gt, T.sr[:], T.gs[:, 48:80], op_.is_gt)
+    V("tt", "tt", "ge lw", tt, ge, T.lw[:], op_.mult)
+    V("tt", "cmp", "tt gt", cmp_, tt, gt, op_.max)
+    V("scan", "sc", "cmp r16", sc, T.r16[:, 0:32], cmp_, 0.0, op_.mult, op_.add)
+    V("copy", "rku", "sc", T.rku[:], T.qa[:, 143:160:16])
+    V("copy", "bsw", "ge2 rku", T.bsw[:].indirect(T.rku[:]), T.ge2[:])
+    V("scan", "pk", "bsw r17", T.pk[:], T.r17[:], T.bsw[:, 0:34], 0.0, op_.mult, op_.add)
+    V("ts", "bc", "pk zm", T.bc[:, 0:32], T.zm[:, 0:32], T.pk[:, 8:9], None, op_.mult)
+    V("ts", "bc", "pk zm", T.bc[:, 32:64], T.zm[:, 32:64], T.pk[:, 25:26], None, op_.mult)
+    V("tr", "tm", "bc", T.tm[:], T.bc[:])
+    V("copy", "own", "tm low2", T.own[:], T.tm[:].indirect(T.low2[:]))
+    V("copy", "msw", "own rku", T.msw[:].indirect(T.rku[:]), T.own[:])
+    V("tt", "ms", "msw", T.ms[:], T.msw[:, 1:9], T.msw[:, 18:26], op_.add)
+    for m in range(7):
+        V("ts", "ui", "ms", T.ui[:, 8 * m:8 * m + 8], T.ms[:], 7 - m, 1, op_.logical_shift_right, op_.bitwise_and)
+    V("ts", "ui", "ms", T.ui[:, 56:64], T.ms[:], 8, None, op_.logical_shift_right)
+    V("copy", "fb", "ui", T.fb[:, 1:64], T.ui[:, 1:64])
+    for m in range(1, 7):
+        V("ts", "tmp", "fb", T.tmp[:, 0:7 - m], T.fb[:, 9 * m + 1:8 * m + 8], T.fb[:, m:m + 1], None, op_.subtract)
+        V("tt", "fb", "tmp", T.fb[:, m + 1:8], T.fb[:, m + 1:8], T.tmp[:, 0:7 - m], op_.max)
+    V("copy", "r4", "fb lrep", T.r4[:], T.fb[:].indirect(T.lrep[:]))
+    V("ts", "k4", "r4", k4, T.r4[:, 0:32], 0.0, None, op_.is_equal)
+    V("scan", "ps", "k4 r8", ps, T.r8[:], k4, 0.0, op_.mult, op_.add)
+    V("tt", "kn", "k4 r4", kn, k4, T.r4[:, 32:64], op_.mult)
+    V("tt", "eq", "ps c4", eq, ps, T.c4[:], op_.is_equal)
+    V("tt", "v4", "eq kn", v4, eq, kn, op_.mult)
+    V("scan", "sc8", "v4 r8", sc8, T.r8[:], v4, 0.0, op_.mult, op_.add)
+    V("copy", "kl", "sc8", T.kl[:], T.qb[:, 167:192:8])
+    for k in range(8):
+        dma("s" if k % 2 == 0 else "a", "drep", T.kr[16 * k:16 * k + 16, :], T.kl[0:128:8, :], "kl", "kr")
+    V("ts", "lm", "c16 tf", T.lm[:], T.c16[:, 0:64], tf, None, op_.is_lt)
+    V("ts", "trs", "sk", T.fc[:, 6:10], T.fc[:, 2:6], 1040.0, None, op_.add)
+    V("set", "r64", "", T.r64[:], 1.0)
+    V("set", "r64", "", T.r64[:, 0:256:64], 0.0)
+    V("set", "ebt", "", T.ebt[:], 0.0)
+
+    V("copy", "ku", "kr", T.ku[:], T.kr[:])
+    V("copy", "rw", "idx ku", T.rw[:], T.idx[:].indirect(T.ku[:]))
+    V("tt", "rwm", "rw lm", T.rwm[:], T.rw[:], T.lm[:], op_.mult)
+    for k in range(4):
+        V("ts", "eqd", "rwm kr trs", T.eqd[:, 64 * k:64 * k + 64], T.rwm[:], T.kr[:, k:k + 1], trs[k], op_.is_equal, op_.mult)
+    V("scan", "scd", "eqd r64", T.scd[:], T.r64[:], T.eqd[:], 0.0, op_.mult, op_.max)
+    V("tt", "lf", "scd kr", T.lf[:], T.scd[:, 63:256:64], T.kr[:], op_.max)
+    V("copy", "lu", "lf", T.lu[:], T.lf[:])
+    send([(T.lu[:], [T.lr[:]], [ids_r[x]], e_r[x], "r_kl") for x in range(4)], "lu")
+    send([(T.lu[:], [T.ll[:, 4 * at_s[y]:4 * at_s[y] + 4]], [ids_s[y]], e_s[y], "a_kls") for y in range(3)], "lu")
+
+    for b in range(4):
+        V("copy", "ebt", "hid", T.ebt[:, 512 * b + b:512 * b + 512:4], T.hid[:])
+    V("qz", "ec es", "ebt", T.ec[:], T.es[:], T.ebt[:])
+    for b in range(4):
+        mm(T["pd%d" % b][:, 0:P], T.ec[:, P * b:P * b + P], T.es[:, P * b:P * b + P], T.tbc[:], T.tbs[:], True, False, "ec es tbc tbs", "pd%d" % b)
+    V("ts", "kpf", "rw", T.kpf[:], T.rw[:], -1.0, None, op_.add)
+    dma("s", "dkp", T.kp[:], T.kpf[0:1, :], "kpf", "kp")
+    V("set", "zbz", "", T.zb[:, WCOLS:480], 0.0)
+    V("copy", "locr", "loc ku", T.locr[:, 0:64], T.loc[:].indirect(T.ku[:]))
+    V("tt", "loc2", "locr wm", T.locr[:, 64:128], T.locr[:, 0:64], T.wm[:, 0:64], op_.mult)
+    V("scan", "loc3", "loc2 r16", T.locr[:, 128:192], T.r16[:, 0:64], T.locr[:, 64:128], 0.0, op_.mult, op_.add)
+    V("copy", "yl", "loc3", T.yl[:, 0:8:2], T.locr[:, 143:192:16])
+    for k in range(4):
+        V("copy", "yb", "zb zbz yl", T.yb[:, k:64:4], T.zb[:].indirect(T.yl[:, 2 * k:2 * k + 1]))
+    dma("s", "dy", T.y[:], T.yb[:], "yb", "y")
+    V("set", "wns", "", T.wns[:, P * r:P * r + 136], float(P))
+    V("set", "wnc", "", T.wnc[:, P * r:P * r + 136], float(P))
+    V("ts", "wmb", "c16 tf", T.wmb[:], T.c16[:, 0:P], tf, None, op_.is_equal)
+    V("set", "r16b", "", T.r16b[:], 1.0)
+    V("set", "r16b", "", T.r16b[:, 0:P:16], 0.0)
+    V("ts", "jw", "k16 tf", T.fc[:, 18:26], T.fc[:, 10:18], tf, None, op_.add)
+    V("qz", "fwo fso", "tbt", T.fwc[:, 0:P], T.fws[:, 0:P], T.tbt[:])
+
+    tot["a_kls"] = sum(len(e_s[f]) for f in from_s)
+    tot["a_klc"] = 4 * noff
+    wr_["lls"] = [("a_kls", tot["a_kls"])]
+    wr_["llc"] = [("a_klc", tot["a_klc"])]
+    for q in sorted(same + [r], reverse=True):
+        off = T.lu[:] if q == r else T.ll[:, 4 * peers.index(q):4 * peers.index(q) + 4]
+        V("copy", "wns", "val " + ("lu" if q == r else "lls"), T.wns[:].indirect(off), T.val[:, 64 * q:64 * q + 64])
+    s = P * r + 1
+    V("tt", "wsm0", "wns wmb", T.wsm[:, 0:P], T.wns[:, s:s + P], T.wmb[:], op_.mult)
+    for q in sorted(cross, reverse=True):
+        c = 4 * peers.index(q)
+        V("copy", "wnc", "val llc", T.wnc[:].indirect(T.ll[:, c:c + 4]), T.val[:, 64 * q:64 * q + 64])
+    V("tt", "wsm1", "wsm0 wnc", T.wsm[:, P:2 * P], T.wsm[:, 0:P], T.wnc[:, s:s + P], op_.min)
+    V("scan", "wsm2", "wsm1 r16b", T.wsm[:, 2 * P:3 * P], T.r16b[:], T.wsm[:, P:2 * P], 0.0, op_.mult, op_.add)
+    won = T.wsm[:, 2 * P + 15:3 * P:16]
+    V("ts", "wu", "wsm2", T.wu[:], won, float(P - 1), None, op_.min)
+    tot["a_pt"] = 7 * 2 * noff
+    wr_["pwa"] = [("a_pt", tot["a_pt"])]
+    do("a", lambda q: q.activation(T.pps[:], T.pws[:].indirect(T.wu[:]), Copy), ["pwa", "pwo", "wu"], ["pps"])
+    V("copy", "ppc", "pwa pwo wu", u32(T.ppc[:]), u32(T.pwc[:]).indirect(T.wu[:]))
+    for b in range(4):
+        mm(T["pd%d" % b][:, 0:P], T.ec[:, P * b:P * b + P], T.es[:, P * b:P * b + P], T.ppc[:], T.pps[:], False, True, "ec es ppc pps", "pd%d" % b)
+    V("ts", "wl", "wsm2", T.wl[:], won, float(P), float(P), op_.is_lt, op_.mult)
+    V("tt", "wl", "wl jw", T.wl[:], T.wl[:], T.fc[:, 18:26], op_.add)
+    V("copy", "fl", "wl", T.fl[:], T.wl[:])
+    for b in range(4):
+        o, i = T.nt[:, b:512:4], T["pd%d" % b][:, 0:P]
+        if b % 2 == 0:
+            V("copy", "nt%d" % b, "pd%d" % b, o, i)
+        else:
+            do("a", lambda q: q.activation(o, i, Copy), ["pd%d" % b], ["nt%d" % b])
+    V("qz", "fwn fsn", "nt0 nt1 nt2 nt3", T.fwc[:, P:2 * P], T.fws[:, P:2 * P], T.nt[:])
+    do("a", lambda q: q.activation(T.fos[:], T.fws[:].indirect(T.fl[:]), Copy), ["fso", "fsn", "fl"], ["fos"])
+    V("copy", "foc", "fwo fwn fl", u32(T.foc[:]), u32(T.fwc[:]).indirect(T.fl[:]))
+    dma("s", "doc", T.oc[:], u8(T.foc[:]), "foc", "oc")
+    for k in range(4):
+        dma("a" if k < 3 else "s", "doc", T.osc[4 * k:4 * k + 4, :], T.fos[32 * k:32 * k + 4, :], "fos", "osc")
+    need("g", [(x, tot[x]) for x in tot])

@@ -1,5 +1,5 @@
 from concourse.bass import DstId, RemoteDMATransfer
-from concourse.mybir import dt, AluOpType, AxisListType, ActivationFunctionType
+from concourse.mybir import dt, AluOpType, ActivationFunctionType
 
 N, P, A, LC = 8, 128, 16, 48
 F32, BF, I32, U16, U8, X4 = "float32", "bfloat16", "int32", "uint16", "uint8", "float8_e4m3fn_x4"
@@ -12,33 +12,33 @@ def _sb(name, n, d):
 
 
 for _n, _w, _d in [
-    ("cdi", 16, I32), ("cpi", 2, I32), ("tbt", 512, BF), ("xt", 512, BF), ("wt", 512, BF),
-    ("cdu", 32, U16), ("flg", 1024, BF), ("one", 128, BF), ("inc", 1024, BF), ("le", 2688, BF), ("cs", 2688, BF), ("rs", 2688, BF),
-    ("rq", 12, U16), ("rqx", 10, U16), ("rqr", 4, U16), ("rql", 22, U16),
+    ("cdi", 16, I32), ("cpi", 2, I32), ("tbt", 512, BF), ("xt", 512, BF), ("xu", 512, BF), ("wt", 512, BF),
+    ("cdu", 32, U16), ("flg", 1024, BF), ("one", 128, BF), ("inc", 1024, BF), ("le", 1792, BF), ("cs", 1792, BF), ("rs", 512, BF),
+    ("sgo", 256, BF), ("sga", 16, F32), ("rq", 12, U16), ("rqx", 10, U16), ("rqr", 6, U16), ("rql", 22, U16),
     ("tbc", 128, X4), ("tbs", 128, U8), ("wc", 480, X4), ("ws", 480, U8), ("fwc", 256, X4), ("fws", 256, U8),
     ("xc", 128, X4), ("xs", 128, U8), ("wqc", 128, X4), ("wqs", 128, U8), ("pwc", 128, X4), ("pws", 128, U8),
     ("dcc", 192, X4), ("dcs", 192, U8), ("dsc", 144, X4), ("dss", 144, U8), ("rlc", 96, X4), ("rls", 96, U8),
     ("rpc", 16, X4), ("rps", 16, U8), ("kc", 288, X4), ("ks", 288, U8), ("ppc", 128, X4), ("pps", 128, U8),
     ("foc", 128, X4), ("fos", 128, U8), ("ebt", 2048, BF), ("ec", 512, X4), ("es", 512, U8),
-    ("ii", 10, I32), ("fc", 28, F32), ("idx", 1040, F32), ("c16", 256, F32), ("wm", 256, F32), ("wmb", 128, BF), ("r16", 256, F32),
-    ("r16b", 128, BF), ("r64", 256, F32), ("lm", 64, F32), ("r17", 34, F32), ("r8", 32, F32), ("c4", 32, F32), ("zm", 64, F32),
-    ("half", 128, BF), ("hid", 128, BF), ("val", 512, BF), ("lgs", 6, U16), ("low2", 2, U16), ("lrep", 4, U16),
+    ("ii", 8, I32), ("fc", 36, F32), ("cj", 352, F32), ("idx", 1040, F32), ("c16", 256, F32), ("wm", 256, F32), ("wmb", 128, BF),
+    ("r16", 256, F32), ("r16b", 128, BF), ("r64", 256, BF), ("lm", 64, F32), ("r17", 34, F32), ("r8", 32, F32), ("c4", 32, F32),
+    ("zm", 64, F32), ("hid", 128, BF), ("val", 512, BF), ("lgs", 6, U16), ("low2", 2, U16), ("lrep", 4, U16),
     ("loc", 1040, F32), ("cdk", 16, U16), ("posr", 256, F32), ("posm", 256, F32), ("posc", 256, F32), ("kpl", 16, U16),
     ("cpu", 2, U16), ("nr", 32, F32), ("lw", 32, F32),
     ("pb", 288, F32), ("gs", 96, F32), ("tr", 64, F32), ("sr", 32, F32), ("qa", 192, F32), ("rku", 2, U16), ("ge2", 32, F32),
     ("bsw", 40, F32), ("pk", 34, F32), ("bc", 64, F32), ("tm", 64, F32), ("own", 32, F32), ("msw", 40, I32), ("ms", 8, I32),
     ("ui", 64, I32), ("fb", 64, F32), ("tmp", 8, F32), ("r4", 64, F32), ("qb", 192, F32), ("kl", 4, F32),
-    ("kr", 4, F32), ("ku", 4, U16), ("rw", 64, F32), ("rwm", 64, F32), ("eqd", 256, F32), ("scd", 256, F32), ("lf", 4, F32),
+    ("kr", 4, F32), ("ku", 4, U16), ("rw", 64, F32), ("rwm", 64, F32), ("eqd", 256, BF), ("scd", 256, BF), ("lf", 4, F32),
     ("lu", 4, U16), ("lr", 4, U16), ("ll", 28, U16), ("kpf", 64, F32), ("locr", 192, F32), ("yl", 8, U16), ("zb", 480, F32), ("yb", 64, F32),
-    ("wns", 1120, BF), ("wnc", 1120, BF), ("wsm", 384, BF), ("wl", 8, F32), ("wu", 8, U16), ("fl", 8, U16), ("nt", 512, BF),
+    ("wns", 1552, BF), ("wnc", 1552, BF), ("wsm", 384, BF), ("wl", 8, F32), ("wu", 8, U16), ("fl", 8, U16), ("nt", 512, BF),
 ]:
     _sb(_n, _w, _d)
 for _n in ("pg0", "pg1", "pz", "pd0", "pd1", "pd2", "pd3"):
     SCRATCH[_n] = ("psum", [128, 512], F32)
-SEMAPHORES = ["cv", "ca", "ct", "cg", "dcd", "dcp", "dtb", "dx", "dw", "dkx", "drep", "dy", "dkp", "doc", "ls",
+SEMAPHORES = ["cv", "ca", "ct", "cg", "dcd", "dcp", "dtb", "dx", "dxu", "dw", "dkx", "drep", "dy", "dkp", "doc", "ls",
               "a_rqc", "a_rqs", "a_dt", "a_pt", "a_klc", "a_kls", "r_pt", "r_rq", "r_dt", "r_kl"]
-FILL = ("zm", "ebt", "r16", "r8", "r17", "r64", "rs", "r16b")
-PART = ("sk", "lerq", "lerqx", "lgs", "low2", "lrep", "loc", "cdk", "ui", "eqd", "bc", "yb", "c4")
+PART = ("lerq", "lerqx", "csrq", "csrqx", "lgf", "low2", "lrep", "loc", "cdk", "ui", "eqd", "bc", "yb", "zm", "ebz", "ebt", "slf",
+        "rq", "rqx", "sgarq", "sgarqx")
 
 
 def _bits(es):
@@ -77,7 +77,8 @@ def _relay_program(g, core, T, topo, cores, r, x):
     pair = cross[2 * h:2 * h + 2]
     ids = [_dst(topo, cores[q], core) for q in pair]
     es = topo.engines(core, cores[pair[0]])
-    place = [_peers(topo, cores, q)[0].index(r) for q in cross]
+    half = [es[0:4], es[4:8]]
+    at = [_peers(topo, cores, q)[0].index(r) for q in pair]
     n = [0]
 
     def fwd(ts):
@@ -87,24 +88,22 @@ def _relay_program(g, core, T, topo, cores, r, x):
             n[0] += len(e)
         g.remote_dma_fused(out, local_sem=T.sem.ls)
 
-    one = [_dst(topo, cores[cross[x]], core)]
     non = len(topo.engines(cores[r], core))
     a = 16 * r
-    w = [P + LC * place[2 * h], P + LC * place[2 * h + 1]]
-    g.wait_ge(T.sem.r_pt, non)
+    w = [P + LC * at[0], P + LC * at[1]]
+    g.wait_ge(T.sem.r_pt, non // 2)
     if x < 2:
         fwd([(T.rpc[:].bitcast(dt.uint8), [T.pwc[:, a:a + 16].bitcast(dt.uint8)] * 2, ids, es, "a_pt")])
+        g.wait_ge(T.sem.r_rq, non // 2)
+        fwd([(T.rqr[:, 3 * k:3 * k + 3], [T.rql[:, 3 * at[k]:3 * at[k] + 3]], [ids[k]], half[k], "a_rqc") for k in range(2)])
+        g.wait_ge(T.sem.r_dt, non // 2)
+        fwd([(T.rlc[:, LC * k:LC * k + LC].bitcast(dt.uint8), [T.wc[:, w[k]:w[k] + LC].bitcast(dt.uint8)], [ids[k]], half[k], "a_dt") for k in range(2)])
+        g.wait_ge(T.sem.r_kl, non)
+        fwd([(T.lr[:], [T.ll[:, 4 * at[k]:4 * at[k] + 4]], [ids[k]], half[k], "a_klc") for k in range(2)])
     else:
         fwd([(T.rps[:], [T.pws[:, a:a + 16]] * 2, ids, es, "a_pt")])
-    g.wait_ge(T.sem.r_rq, non // 4)
-    fwd([(T.rqr[:, 0:3], [T.rql[:, 3 * place[x]:3 * place[x] + 3]], one, es, "a_rqc")])
-    g.wait_ge(T.sem.r_dt, non // 2)
-    if x < 2:
-        fwd([(T.rlc[:, LC * k:LC * k + LC].bitcast(dt.uint8), [T.wc[:, w[k]:w[k] + LC].bitcast(dt.uint8)], [ids[k]], es[4 * k:4 * k + 4], "a_dt") for k in range(2)])
-    else:
-        fwd([(T.rls[:, LC * k:LC * k + LC], [T.ws[:, w[k]:w[k] + LC]], [ids[k]], es[4 * k:4 * k + 4], "a_dt") for k in range(2)])
-    g.wait_ge(T.sem.r_kl, non // 4)
-    fwd([(T.lr[:], [T.ll[:, 4 * place[x]:4 * place[x] + 4]], one, es, "a_klc")])
+        g.wait_ge(T.sem.r_dt, non // 2)
+        fwd([(T.rls[:, LC * k:LC * k + LC], [T.ws[:, w[k]:w[k] + LC]], [ids[k]], half[k], "a_dt") for k in range(2)])
     g.wait_ge(T.sem.ls, n[0])
 
 
@@ -120,14 +119,15 @@ def rank_program(g, core, T, topo):
         return
 
     op_ = AluOpType
-    Copy = ActivationFunctionType.Copy
+    AF = ActivationFunctionType
+    Copy, Sign, Ident, Abs, Relu = AF.Copy, AF.Sign, AF.Identity, AF.Abs, AF.Relu
     cross, rel = _relays(topo, cores, r)
     _, same = _peers(topo, cores, r)
     peers = cross + same
 
     eng = {"v": g.vector, "a": g.scalar, "t": g.tensor, "g": g, "s": g.sync}
     csem = {"v": "cv", "a": "ca", "t": "ct", "g": "cg"}
-    tot, seen, wr_, rd_, base_ = {}, {e: {} for e in eng}, {}, {}, {}
+    tot, seen, wr_, rd_ = {}, {e: {} for e in eng}, {}, {}
 
     def need(e, toks):
         want = {}
@@ -145,18 +145,12 @@ def rank_program(g, core, T, topo):
         for k in rd:
             toks += wr_.get(k, [])
         for k in wr:
-            old = wr_.get(k, []) + rd_.get(k, [])
-            if k in FILL or k in PART:
-                toks += [t for t in old if t[0] != mine] + base_.get(k, [])
-            else:
-                toks += old
+            toks += [t for t in wr_.get(k, []) + rd_.get(k, []) if k not in PART or t[0] != mine]
         need(e, toks)
         fn(eng[e]).then_inc(T.sem[mine], 1)
         tot[mine] = tot.get(mine, 0) + 1
         tok = (mine, tot[mine])
         for k in wr:
-            if k in FILL and k not in base_:
-                base_[k] = [tok]
             wr_[k] = [t for t in wr_.get(k, []) if t[0] != mine] + [tok] if k in PART else [tok]
             rd_[k] = []
         for k in rd:
@@ -168,6 +162,12 @@ def rank_program(g, core, T, topo):
                  "scan": q.tensor_tensor_scan, "tr": q.transpose, "qz": q.quantize_mx}[name]
             return f(*args)
         do("v", fn, rd.split(), wr.split())
+
+    def S(f, wr, rd, out, in_, **k):
+        do("a", lambda q: q.activation(out, in_, f, **k), rd.split(), wr.split())
+
+    def iota(out, wr, pattern, base=0, cm=0):
+        do("g", lambda q: q.iota(out, pattern, base, cm, allow_small_or_imprecise_dtypes=True), [], [wr])
 
     def dma(e, sem, out, in_, rd, wr):
         toks = []
@@ -205,9 +205,7 @@ def rank_program(g, core, T, topo):
     eon = topo.engines(core, rel[0])
     eoff = topo.engines(core, cores[same[0]])
     noff = len(eoff)
-    per = len(eon) // 4
-    e_r = [eon[per * x:per * x + per] for x in range(4)]
-    e_h = [eon[0:2 * per], eon[2 * per:4 * per]]
+    e_h = [eon[0:len(eon) // 2], eon[len(eon) // 2:]]
     e_s, e_s2 = _same_engines(eoff)
     at_s = []
     from_s = []
@@ -216,147 +214,163 @@ def rank_program(g, core, T, topo):
         at_s.append(4 + sq.index(r))
         from_s.append(sq.index(r))
 
-    pin, ti, gi, oi, o7 = [T.ii[:, 2 * k:2 * k + 2] for k in range(5)]
-    pin1, oi1 = T.ii[:, 0:1], T.ii[:, 6:7]
+    pin, ti, oi, o7 = [T.ii[:, 2 * k:2 * k + 2] for k in range(4)]
+    oi1 = T.ii[:, 4:5]
     tf = T.fc[:, 0:1]
-    sk = [T.fc[:, 2 + k:3 + k] for k in range(4)]
-    trs = [T.fc[:, 6 + k:7 + k] for k in range(4)]
-    cpf = T.fc[:, 26:28]
+    sk = [T.fc[:, k:k + 1] for k in range(8)]
+    trs = [T.fc[:, 16 + k:17 + k] for k in range(4)]
+    cpf, half2, pf2, n8, n8b = T.fc[:, 20:22], T.fc[:, 22:23], T.fc[:, 30:32], T.fc[:, 32:33], T.fc[:, 33:34]
+    c8, c17, c64 = T.cj[:, 0:32], T.cj[:, 32:66], T.cj[:, 96:352]
     ge, gt, tt, cmp_, sc, slf = [T.qa[:, 32 * k:32 * k + 32] for k in range(6)]
     k4, ps, kn, eq, v4, sc8 = [T.qb[:, 32 * k:32 * k + 32] for k in range(6)]
 
+    dma("a", "dx", T.xt[:, 0:64], T.x[:], "", "xt")
     for k in range(8):
         dma("s" if k % 2 == 0 else "a", "dcd", T.cdi[16 * k:16 * k + 16, :], T.cd[:], "", "cdi")
-    dma("a", "dx", T.xt[:, 0:64], T.x[:], "", "xt")
     dma("s", "dtb", T.tbt[:], T.tb[:], "", "tbt")
-    dma("a", "dw", T.wt[:], T.w[:], "", "wt")
+    dma("s", "dxu", T.xu[:, 448:512], T.x[:], "", "xu")
+    dma("s", "dw", T.wt[:], T.w[:], "", "wt")
     for k in range(8):
         dma("s", "dcp", T.cpi[16 * k:16 * k + 16, :], T.cd[:, 2 * k:2 * k + 2], "", "cpi")
 
     do("g", lambda q: q.iota(pin, [[0, 2]], 0, 1), [], ["pin"])
-    do("g", lambda q: q.iota(T.c16[:], [[0, 16], [1, 16]], 0, 0, allow_small_or_imprecise_dtypes=True), [], ["c16"])
-    do("g", lambda q: q.iota(T.fc[:, 10:18], [[16, 8]], 0, 0, allow_small_or_imprecise_dtypes=True), [], ["k16"])
+    iota(T.fc[:, 8:16], "k16", [[16, 8]])
+    iota(T.c16[:], "c16", [[0, 16], [1, 16]])
+    iota(T.fc[:, 24:26], "lgf", [[128, 2]], 16, 1)
+    iota(pf2, "pf2", [[0, 2]], 0, 1)
 
-    V("set", "flg", "", T.flg[:], 0.0)
-    V("set", "one", "", T.one[:], 1.0)
     V("set", "xtz", "", T.xt[:, 64:512], 0.0)
     V("ts", "ti", "pin", ti, pin, 15, None, op_.bitwise_and)
-    V("copy", "tf", "ti", T.fc[:, 0:2], ti)
-    for k in range(4):
-        V("ts", "sk", "tf", sk[k], tf, float(16 * k), None, op_.add)
+    V("set", "flg", "", T.flg[:], 0.0)
+    V("copy", "tf", "ti", T.fc[:, 34:36], ti)
+    V("set", "one", "", T.one[:], 1.0)
+    V("ts", "sk", "k16 tf", T.fc[:, 0:8], T.fc[:, 8:16], T.fc[:, 34:35], None, op_.add)
     V("set", "rs", "", T.rs[:], 1.0)
-    V("set", "rs", "", T.rs[:, 0:2688:128], 0.0)
+    V("set", "rs", "", T.rs[:, 0:512:128], 0.0)
+
+    S(Ident, "half2", "sk", half2, sk[2], bias=0.5)
+    S(Sign, "r16", "c16", T.r16[:], T.c16[:])
+    S(Abs, "wm", "c16 sk", T.wm[:], T.c16[:], bias=tf, scale=-1.0)
+    S(Relu, "wm", "wm", T.wm[:], T.wm[:], bias=1.0, scale=-1.0)
+    S(Copy, "xuz", "xtz", T.xu[:, 0:448], T.xt[:, 64:512])
+    S(Copy, "n8", "sk", n8, tf, scale=-0.125)
+    S(Ident, "n8b", "n8", n8b, n8, bias=273.0)
+    S(Ident, "lgf", "pf2 n8", T.fc[:, 26:28], pf2, bias=n8, scale=0.125)
+    S(Ident, "lgf", "pf2 n8b", T.fc[:, 28:30], pf2, bias=n8b, scale=0.125)
+
+    V("qz", "xc xs", "xt xtz", T.xc[:], T.xs[:], T.xt[:])
+    send([(u8(T.xc[:, 0:16]), [u8(T.rpc[:])] * 2, ids_r[0:2], e_h[0], "r_pt")], "xc")
+    send([(T.xs[:, 0:16], [T.rps[:]] * 2, ids_r[2:4], e_h[1], "r_pt")], "xs")
 
     V("copy", "cdu", "cdi", T.cdu[:, 0:32:2], T.cdi[:])
     for i in range(A):
         V("copy", "flg", "cdu one", T.flg[:].indirect(T.cdu[:, 2 * i:2 * i + 1]), T.one[:, 0:16])
-        if i == 2:
-            V("qz", "xc xs", "xt xtz", T.xc[:], T.xs[:], T.xt[:])
-            send([(u8(T.xc[:, 0:16]), [u8(T.rpc[:])] * 2, ids_r[0:2], eon, "r_pt")], "xc")
-            send([(T.xs[:, 0:16], [T.rps[:]] * 2, ids_r[2:4], eon, "r_pt")], "xs")
 
     def lists(qs, base, name, out):
         n = len(qs)
+        h0 = base // P
         for x, q in enumerate(qs):
             V("scan", "inc%d" % q, "flg one", T.inc[:, P * q:P * q + P], T.one[:], T.flg[:, P * q:P * q + P], 0.0, op_.mult, op_.add)
         for x, q in enumerate(qs):
-            for k in range(3):
-                a = base + P * (3 * x + k)
+            h = h0 + x
+            b = P * (h % 2)
+            S(Sign, "sgo%d sga%s" % (h % 2, name), "inc%d half2" % q, T.sgo[:, b:b + P - 1], T.inc[:, P * q:P * q + P - 1],
+              bias=half2, scale=-1.0, accum_out=T.sga[:, h:h + 1])
+        for k in range(2):
+            for x, q in enumerate(qs):
+                a = base + P * (n * k + x)
                 V("ts", "le" + name, "inc%d sk" % q, T.le[:, a:a + P], T.inc[:, P * q:P * q + P], sk[k], None, op_.is_le)
-        e = base + P * 3 * n
-        V("scan", "cs" + name, "rs le" + name, T.cs[:, base:e], T.rs[:, base:e], T.le[:, base:e], 0.0, op_.mult, op_.add)
-        V("ts", name, "cs" + name, out, T.cs[:, base + P - 1:e:P], float(P - 1), None, op_.min)
+        for k in range(2):
+            a, e = base + P * n * k, base + P * n * (k + 1)
+            V("scan", "cs" + name, "rs le" + name, T.cs[:, a:e], T.rs[:, 0:P * n], T.le[:, a:e], 0.0, op_.mult, op_.add)
+        V("ts", name, "sga" + name, out[:, 2:3 * n:3], T.sga[:, h0:h0 + n], 0.5, 0.5 * (P - 1), op_.mult, op_.add)
+        for k in range(2):
+            V("copy", name, "cs" + name, out[:, k:3 * n:3], T.cs[:, base + P * n * k + P - 2:base + P * n * (k + 1):P])
 
-    lists(cross, 0, "rq", T.rq[:])
-    send([(T.rq[:, 3 * x:3 * x + 3], [T.rqr[:, 0:3]], [ids_r[x]], e_r[x], "r_rq") for x in range(4)], "rq")
-    lists(same, 1536, "rqx", T.rqx[:, 0:9])
+    lists(cross, 0, "rq", T.rq)
+    send([(T.rq[:, 6 * h:6 * h + 6], [T.rqr[:]], [ids_r[h]], e_h[h], "r_rq") for h in range(2)], "rq")
+    lists(same, 1024, "rqx", T.rqx)
     send([(T.rqx[:, 3 * y:3 * y + 3], [T.rql[:, 3 * at_s[y]:3 * at_s[y] + 3]], [ids_s[y]], e_s[y], "a_rqs") for y in range(3)], "rqx")
-    do("g", lambda q: q.iota(T.idx[:], [[1, 1040]], 0, 0, allow_small_or_imprecise_dtypes=True), [], ["idx"])
-
-    dma("s", "dkx", u8(T.kc[:, 0:16]), u8(T.xc[:, 0:16]), "xc", "kcx")
-    dma("s", "dkx", u8(T.kc[:, 272:288]), u8(T.xc[:, 0:16]), "xc", "kcx")
-    dma("s", "dkx", u8(T.pwc[:, 16 * r:16 * r + 16]), u8(T.xc[:, 0:16]), "xc", "pwo")
-    dma("s", "dkx", T.ks[:, 0:16], T.xs[:, 0:16], "xs", "ksx")
-    dma("s", "dkx", T.ks[:, 272:288], T.xs[:, 0:16], "xs", "ksx")
-    dma("s", "dkx", T.pws[:, 16 * r:16 * r + 16], T.xs[:, 0:16], "xs", "pwo")
+    iota(T.idx[:], "idx", [[1, 1040]])
 
     V("qz", "tbc tbs", "tbt", T.tbc[:], T.tbs[:], T.tbt[:])
-    V("set", "r16", "", T.r16[:], 1.0)
-    V("set", "r16", "", T.r16[:, 0:256:16], 0.0)
-    V("ts", "wm", "c16 tf", T.wm[:], T.c16[:], tf, None, op_.is_equal)
     for x, q in enumerate(peers):
-        V("ts", "loc", "inc%d" % q, T.loc[:, 1 + P * q:1 + P * q + P], T.inc[:, P * q:P * q + P], float(P + LC * x - 1), None, op_.add)
-    V("set", "loc", "", T.loc[:, 0:1], float(WCOLS))
-    V("set", "loc", "", T.loc[:, 1025:1040], float(WCOLS))
+        S(Ident, "loc", "inc%d" % q, T.loc[:, 1 + P * q:1 + P * q + P], T.inc[:, P * q:P * q + P], bias=float(P + LC * x - 1))
+    V("set", "locz", "", T.loc[:, 0:1], float(WCOLS))
+    V("set", "locy", "", T.loc[:, 1025:1040], float(WCOLS))
+    V("ts", "oi", "pin", oi, pin, 31, None, op_.bitwise_and)
+    V("ts", "o7", "pin", o7, pin, 7, None, op_.bitwise_and)
+    V("ts", "cdk", "cdi", T.cdk[:, 0:8], T.cdi[:, 0:16:2], 1.0, None, op_.add)
+    V("ts", "cdk", "cdi", T.cdk[:, 8:16], T.cdi[:, 1:16:2], 1.0, None, op_.add)
+    V("copy", "cpf", "cpi", cpf, T.cpi[:])
+    V("copy", "cpu", "cpi", T.cpu[:], T.cpi[:])
+    V("copy", "lgs", "lgf", T.lgs[:], T.fc[:, 24:30])
+    V("ts", "low2", "oi", T.low2[:, 0:1], oi1, 0.0, None, op_.add)
+    V("ts", "low2", "oi", T.low2[:, 1:2], oi1, 32.0, None, op_.add)
+    V("ts", "lrep", "o7", T.lrep[:, 0:2], o7, 0.0, None, op_.add)
+    V("ts", "lrep", "o7", T.lrep[:, 2:4], o7, 56.0, None, op_.add)
 
-    tot["a_rqc"] = 4 * noff
+    tot["a_rqc"] = 4 * noff // 2
     tot["a_rqs"] = sum(len(e_s[f]) for f in from_s)
     wr_["rqlc"] = [("a_rqc", tot["a_rqc"])]
     wr_["rqls"] = [("a_rqs", tot["a_rqs"])]
-    do("a", lambda q: q.activation(T.dcs[:], T.tbs[:].indirect(T.rql[:, 0:12]), Copy), ["tbs", "rqlc"], ["dcs"])
+    S(Copy, "dcs", "tbs rqlc", T.dcs[:], T.tbs[:].indirect(T.rql[:, 0:12]))
     V("copy", "dcc", "tbc rqlc", u32(T.dcc[:]), u32(T.tbc[:]).indirect(T.rql[:, 0:12]))
-    do("a", lambda q: q.activation(T.dss[:], T.tbs[:].indirect(T.rql[:, 12:21]), Copy), ["tbs", "rqls"], ["dss"])
+    S(Copy, "dss", "tbs rqls", T.dss[:], T.tbs[:].indirect(T.rql[:, 12:21]))
     V("copy", "dsc", "tbc rqls", u32(T.dsc[:]), u32(T.tbc[:]).indirect(T.rql[:, 12:21]))
     send([(u8(T.dcc[:, 96 * h:96 * h + 96]), [u8(T.rlc[:])], [ids_r[h]], e_h[h], "r_dt") for h in range(2)], "dcc")
     send([(T.dcs[:, 96 * h:96 * h + 96], [T.rls[:]], [ids_r[2 + h]], e_h[h], "r_dt") for h in range(2)], "dcs")
     ws_ = [P + LC * at_s[y] for y in range(3)]
     send([(u8(T.dsc[:, LC * y:LC * y + LC]), [u8(T.wc[:, ws_[y]:ws_[y] + LC])], [ids_s[y]], e_s[y], "a_dt") for y in range(3)], "dsc")
     send([(T.dss[:, LC * y:LC * y + LC], [T.ws[:, ws_[y]:ws_[y] + LC]], [ids_s[y]], e_s2[y], "a_dt") for y in range(3)], "dss")
+    iota(c17, "c17", [[0, 2], [1, 17]])
+    iota(c8, "c8", [[0, 4], [1, 8]])
+    iota(T.zm[:, 0:32], "zm", [[0, 2], [-1, 2], [0, 8]], 1)
+    iota(T.zm[:, 32:64], "zm", [[0, 2], [1, 2], [0, 8]])
+    iota(T.c4[:], "c4", [[1, 4], [0, 8]], 1)
     send([(u8(T.xc[:, 0:16]), [u8(T.pwc[:, 16 * r:16 * r + 16])] * 3, ids_s, eoff, "a_pt")], "xc")
     send([(T.xs[:, 0:16], [T.pws[:, 16 * r:16 * r + 16]] * 3, ids_s, eoff, "a_pt")], "xs")
+    iota(c64, "c64", [[0, 4], [1, 64]])
+    do("g", lambda q: q.affine_select(T.hid[:], T.one[:], [[-1, 128]], op_.is_equal, 0.0, 0, 1), ["one"], ["hid"])
+    iota(T.val[:], "val", [[16, 8], [0, 4], [1, 16]])
 
-    V("ts", "loc", "idx", T.loc[:, 1 + P * r:1 + P * r + P], T.idx[:, 0:P], 0.0, None, op_.add)
-    V("ts", "cdk", "cdi", T.cdk[:, 0:8], T.cdi[:, 0:16:2], 1.0, None, op_.add)
-    V("ts", "cdk", "cdi", T.cdk[:, 8:16], T.cdi[:, 1:16:2], 1.0, None, op_.add)
-    V("copy", "posr", "loc cdk", T.posr[:], T.loc[:].indirect(T.cdk[:]))
-    V("tt", "posm", "posr wm", T.posm[:], T.posr[:], T.wm[:], op_.mult)
-    V("scan", "posc", "posm r16", T.posc[:], T.r16[:], T.posm[:], 0.0, op_.mult, op_.add)
-    V("copy", "kpl", "posc", T.kpl[:], T.posc[:, 15:256:16])
-    V("qz", "wco wso", "tbt", T.wc[:, 0:P], T.ws[:, 0:P], T.tbt[:])
-    V("qz", "wqc wqs", "wt", T.wqc[:], T.wqs[:], T.wt[:])
-    V("copy", "cpf", "cpi", cpf, T.cpi[:])
-    V("copy", "cpu", "cpi", T.cpu[:], T.cpi[:])
-    V("copy", "nr", "idx cpu", T.nr[:], T.idx[:].indirect(T.cpu[:]))
+    S(Ident, "loc", "idx", T.loc[:, 1 + P * r:1 + P * r + P], T.idx[:, 0:P], bias=0.0)
     for j in range(2):
-        V("ts", "lw%d" % j, "nr cpf", T.lw[:, 16 * j:16 * j + 16], T.nr[:, 16 * j:16 * j + 16], T.fc[:, 26 + j:27 + j], None, op_.is_lt)
-        V("ts", "slf%d" % j, "c16 tf", T.qa[:, 160 + 16 * j:176 + 16 * j], T.c16[:, 0:16], tf, float(1 + 17 * j), op_.is_equal, op_.mult)
-    V("tt", "lw", "lw0 lw1 slf0 slf1", T.lw[:], T.lw[:], slf, op_.add)
-    V("ts", "bsw", "cpf", T.bsw[:, 0:34:17], cpf, 1.0, None, op_.add)
-    V("ts", "gi", "pin", gi, pin, 4, None, op_.logical_shift_right)
-    V("ts", "oi", "pin", oi, pin, 31, None, op_.bitwise_and)
-    V("ts", "o7", "pin", o7, pin, 7, None, op_.bitwise_and)
-    V("ts", "lgs", "pin", T.lgs[:, 0:1], pin1, 16.0, None, op_.add)
-    V("ts", "lgs", "pin", T.lgs[:, 1:2], pin1, 144.0, None, op_.add)
-    V("ts", "lgs", "gi", T.lgs[:, 2:4], gi, 2.0, None, op_.mult)
-    V("ts", "lgs", "gi", T.lgs[:, 4:6], gi, 2.0, 273.0, op_.mult, op_.add)
-    V("ts", "low2", "oi", T.low2[:, 0:1], oi1, 0.0, None, op_.add)
-    V("ts", "low2", "oi", T.low2[:, 1:2], oi1, 32.0, None, op_.add)
-    V("ts", "lrep", "o7", T.lrep[:, 0:2], o7, 0.0, None, op_.add)
-    V("ts", "lrep", "o7", T.lrep[:, 2:4], o7, 56.0, None, op_.add)
-    V("set", "r17", "", T.r17[:], 2.0)
-    V("set", "r17", "", T.r17[:, 0:34:17], 0.0)
-    V("set", "zm", "", T.zm[:], 0.0)
-    for a in (0, 16, 40, 56):
-        V("set", "zm", "", T.zm[:, a:a + 8], 1.0)
-    V("set", "r8", "", T.r8[:], 1.0)
-    V("set", "r8", "", T.r8[:, 0:32:8], 0.0)
-    for k in range(4):
-        V("set", "c4", "", T.c4[:, 8 * k:8 * k + 8], float(k + 1))
-    V("set", "fb", "", T.fb[:, 0:1], 0.0)
-    V("set", "half", "", T.half[:], 0.5)
-    do("g", lambda q: q.affine_select(T.hid[:], T.half[:], [[-1, 128]], op_.is_equal, 0.0, 0, 1), ["half"], ["hid"])
-    do("g", lambda q: q.iota(T.val[:], [[16, 8], [0, 4], [1, 16]], 0, 0, allow_small_or_imprecise_dtypes=True), [], ["val"])
+        S(Copy, "slf", "wm", T.qa[:, 160 + 16 * j:176 + 16 * j], T.wm[:, 0:16], scale=float(1 + 17 * j))
+    S(Ident, "bsw", "cpf", T.bsw[:, 0:34:17], cpf, bias=1.0)
+    S(Copy, "fb0", "c16", T.fb[:, 0:1], T.c16[:, 0:1])
+    S(Sign, "r17", "c17", T.r17[:], c17)
+    S(Copy, "r17", "r17", T.r17[:], T.r17[:], scale=2.0)
+    S(Sign, "r8", "c8", T.r8[:], c8)
+    V("qz", "wco wso", "tbt", T.wc[:, 0:P], T.ws[:, 0:P], T.tbt[:])
+    V("copy", "posr", "loc locz locy cdk", T.posr[:], T.loc[:].indirect(T.cdk[:]))
+    V("qz", "kcx ksx", "xt xtz", T.kc[:, 0:P], T.ks[:, 0:P], T.xt[:])
+    V("tt", "posm", "posr wm", T.posm[:], T.posr[:], T.wm[:], op_.mult)
+    V("qz", "kcx ksx", "xu xuz", T.kc[:, 160:288], T.ks[:, 160:288], T.xu[:])
+    V("scan", "posc", "posm r16", T.posc[:], T.r16[:], T.posm[:], 0.0, op_.mult, op_.add)
+    V("copy", "nr", "idx cpu", T.nr[:], T.idx[:].indirect(T.cpu[:]))
+    V("copy", "kpl", "posc", T.kpl[:], T.posc[:, 15:256:16])
+    for j in range(2):
+        V("ts", "lw%d" % j, "nr cpf", T.lw[:, 16 * j:16 * j + 16], T.nr[:, 16 * j:16 * j + 16], T.fc[:, 20 + j:21 + j], None, op_.is_lt)
+    V("qz", "wqc wqs", "wt", T.wqc[:], T.wqs[:], T.wt[:])
+    V("tt", "lw", "lw0 lw1 slf", T.lw[:], T.lw[:], slf, op_.add)
 
     tot["a_dt"] = 4 * noff + sum(len(e_s[f]) + len(e_s2[f]) for f in from_s)
     wr_["wca"] = [("a_dt", tot["a_dt"])]
-    do("a", lambda q: q.activation(T.ks[:, 16:272], T.ws[:, 0:WCOLS].indirect(T.kpl[:]), Copy), ["wso", "wca", "kpl"], ["ks"])
-    V("copy", "kc", "wco wca kpl", u32(T.kc[:, 16:272]), u32(T.wc[:, 0:WCOLS]).indirect(T.kpl[:]))
-    mm(T.pg0[:, 0:144], T.kc[:, 16:144], T.ks[:, 16:144], T.kc[:, 0:144], T.ks[:, 0:144], True, True, "kc ks kcx ksx", "pg0")
-    mm(T.pg1[:, 0:144], T.kc[:, 144:272], T.ks[:, 144:272], T.kc[:, 144:288], T.ks[:, 144:288], True, True, "kc ks kcx ksx", "pg1")
+    for j in range(2):
+        a = 16 + P * j
+        S(Copy, "ks%d" % j, "wso wca kpl ksx", T.ks[:, a:a + P], T.ws[:, 0:WCOLS].indirect(T.kpl[:, 8 * j:8 * j + 8]))
+        V("copy", "kc%d" % j, "wco wca kpl kcx", u32(T.kc[:, a:a + P]), u32(T.wc[:, 0:WCOLS]).indirect(T.kpl[:, 8 * j:8 * j + 8]))
+    mm(T.pg0[:, 0:144], T.kc[:, 16:144], T.ks[:, 16:144], T.kc[:, 0:144], T.ks[:, 0:144], True, True, "kc0 ks0 kcx ksx", "pg0")
+    mm(T.pg1[:, 0:144], T.kc[:, 144:272], T.ks[:, 144:272], T.kc[:, 144:288], T.ks[:, 144:288], True, True, "kc1 ks1 kcx ksx", "pg1")
     mm(T.pz[:, 0:WCOLS], T.wqc[:], T.wqs[:], T.wc[:, 0:WCOLS], T.ws[:, 0:WCOLS], True, True, "wqc wqs wco wso wca", "pz")
     V("copy", "pb0", "pg0", T.pb[:, 0:144], T.pg0[:, 0:144])
-    do("a", lambda q: q.activation(T.pb[:, 144:288], T.pg1[:, 0:144], Copy), ["pg1"], ["pb1"])
-    do("a", lambda q: q.activation(T.zb[:, 0:WCOLS], T.pz[:, 0:WCOLS], Copy), ["pz"], ["zb"])
+    S(Copy, "pb1", "pg1", T.pb[:, 144:288], T.pg1[:, 0:144])
+    S(Copy, "zb", "pz", T.zb[:, 0:WCOLS], T.pz[:, 0:WCOLS])
+    S(Sign, "lm", "c16 sk", T.lm[:], T.c16[:, 0:64], bias=tf, scale=-1.0)
+    S(Relu, "lm", "lm", T.lm[:], T.lm[:])
+    S(Ident, "trs", "sk", T.fc[:, 16:20], T.fc[:, 0:4], bias=1032.0, scale=8.0)
+    S(Sign, "r64", "c64", T.r64[:], c64)
     V("copy", "gs", "pb0 pb1 lgs", T.gs[:], T.pb[:].indirect(T.lgs[:]))
     V("tr", "tr", "gs", T.tr[:], T.gs[:, 32:96])
     V("tt", "ge2", "gs", T.ge2[:], T.gs[:, 0:32], T.gs[:, 48:80], op_.is_ge)
@@ -379,10 +393,11 @@ def rank_program(g, core, T, topo):
         V("ts", "ui", "ms", T.ui[:, 8 * m:8 * m + 8], T.ms[:], 7 - m, 1, op_.logical_shift_right, op_.bitwise_and)
     V("ts", "ui", "ms", T.ui[:, 56:64], T.ms[:], 8, None, op_.logical_shift_right)
     V("copy", "fb", "ui", T.fb[:, 1:64], T.ui[:, 1:64])
-    for m in range(1, 7):
+    for m in range(1, 6):
         V("ts", "tmp", "fb", T.tmp[:, 0:7 - m], T.fb[:, 9 * m + 1:8 * m + 8], T.fb[:, m:m + 1], None, op_.subtract)
         V("tt", "fb", "tmp", T.fb[:, m + 1:8], T.fb[:, m + 1:8], T.tmp[:, 0:7 - m], op_.max)
-    V("copy", "r4", "fb lrep", T.r4[:], T.fb[:].indirect(T.lrep[:]))
+    V("ts", "fb", "fb", T.fb[:, 7:8], T.fb[:, 55:56], T.fb[:, 6:7], T.fb[:, 7:8], op_.subtract, op_.max)
+    V("copy", "r4", "fb fb0 lrep", T.r4[:], T.fb[:].indirect(T.lrep[:]))
     V("ts", "k4", "r4", k4, T.r4[:, 0:32], 0.0, None, op_.is_equal)
     V("scan", "ps", "k4 r8", ps, T.r8[:], k4, 0.0, op_.mult, op_.add)
     V("tt", "kn", "k4 r4", kn, k4, T.r4[:, 32:64], op_.mult)
@@ -392,11 +407,18 @@ def rank_program(g, core, T, topo):
     V("copy", "kl", "sc8", T.kl[:], T.qb[:, 167:192:8])
     for k in range(8):
         dma("s" if k % 2 == 0 else "a", "drep", T.kr[16 * k:16 * k + 16, :], T.kl[0:128:8, :], "kl", "kr")
-    V("ts", "lm", "c16 tf", T.lm[:], T.c16[:, 0:64], tf, None, op_.is_lt)
-    V("ts", "trs", "sk", T.fc[:, 6:10], T.fc[:, 2:6], 1040.0, None, op_.add)
-    V("set", "r64", "", T.r64[:], 1.0)
-    V("set", "r64", "", T.r64[:, 0:256:64], 0.0)
-    V("set", "ebt", "", T.ebt[:], 0.0)
+    dma("s", "dkx", u8(T.pwc[:, 16 * r:16 * r + 16]), u8(T.xc[:, 0:16]), "xc", "pwo")
+    dma("s", "dkx", T.pws[:, 16 * r:16 * r + 16], T.xs[:, 0:16], "xs", "pwo")
+    for a in range(0, 2048, 448):
+        w = min(448, 2048 - a)
+        S(Copy, "ebz", "xtz", T.ebt[:, a:a + w], T.xt[:, 64:64 + w])
+    for b in range(4):
+        S(Copy, "ebt", "hid ebz", T.ebt[:, 512 * b + b:512 * b + 512:4], T.hid[:], scale=0.5)
+    S(Copy, "zbz", "xtz", T.zb[:, WCOLS:480], T.xt[:, 64:80])
+    for k in ("wns", "wnc"):
+        S(Copy, k, "one", T[k][:, P * r + 1:P * r + 1 + P], T.one[:], scale=float(P))
+    S(Copy, "wmb", "wm", T.wmb[:], T.wm[:, 0:P])
+    S(Sign, "r16b", "c16", T.r16b[:], T.c16[:, 0:P])
 
     V("copy", "ku", "kr", T.ku[:], T.kr[:])
     V("copy", "rw", "idx ku", T.rw[:], T.idx[:].indirect(T.ku[:]))
@@ -406,34 +428,25 @@ def rank_program(g, core, T, topo):
     V("scan", "scd", "eqd r64", T.scd[:], T.r64[:], T.eqd[:], 0.0, op_.mult, op_.max)
     V("tt", "lf", "scd kr", T.lf[:], T.scd[:, 63:256:64], T.kr[:], op_.max)
     V("copy", "lu", "lf", T.lu[:], T.lf[:])
-    send([(T.lu[:], [T.lr[:]], [ids_r[x]], e_r[x], "r_kl") for x in range(4)], "lu")
+    send([(T.lu[:], [T.lr[:]] * 2, ids_r[0:2], eon, "r_kl")], "lu")
     send([(T.lu[:], [T.ll[:, 4 * at_s[y]:4 * at_s[y] + 4]], [ids_s[y]], e_s[y], "a_kls") for y in range(3)], "lu")
 
-    for b in range(4):
-        V("copy", "ebt", "hid", T.ebt[:, 512 * b + b:512 * b + 512:4], T.hid[:])
-    V("qz", "ec es", "ebt", T.ec[:], T.es[:], T.ebt[:])
+    S(Ident, "kpf", "rw", T.kpf[:], T.rw[:], bias=-1.0)
+    dma("s", "dkp", T.kp[:], T.kpf[0:1, :], "kpf", "kp")
+    V("copy", "locr", "loc locz locy ku", T.locr[:, 0:64], T.loc[:].indirect(T.ku[:]))
+    V("qz", "fwo fso", "tbt", T.fwc[:, 0:P], T.fws[:, 0:P], T.tbt[:])
+    V("tt", "loc2", "locr wm", T.locr[:, 64:128], T.locr[:, 0:64], T.wm[:, 0:64], op_.mult)
+    V("qz", "ec es", "ebt ebz", T.ec[:], T.es[:], T.ebt[:])
     for b in range(4):
         mm(T["pd%d" % b][:, 0:P], T.ec[:, P * b:P * b + P], T.es[:, P * b:P * b + P], T.tbc[:], T.tbs[:], True, False, "ec es tbc tbs", "pd%d" % b)
-    V("ts", "kpf", "rw", T.kpf[:], T.rw[:], -1.0, None, op_.add)
-    dma("s", "dkp", T.kp[:], T.kpf[0:1, :], "kpf", "kp")
-    V("set", "zbz", "", T.zb[:, WCOLS:480], 0.0)
-    V("copy", "locr", "loc ku", T.locr[:, 0:64], T.loc[:].indirect(T.ku[:]))
-    V("tt", "loc2", "locr wm", T.locr[:, 64:128], T.locr[:, 0:64], T.wm[:, 0:64], op_.mult)
     V("scan", "loc3", "loc2 r16", T.locr[:, 128:192], T.r16[:, 0:64], T.locr[:, 64:128], 0.0, op_.mult, op_.add)
     V("copy", "yl", "loc3", T.yl[:, 0:8:2], T.locr[:, 143:192:16])
     for k in range(4):
         V("copy", "yb", "zb zbz yl", T.yb[:, k:64:4], T.zb[:].indirect(T.yl[:, 2 * k:2 * k + 1]))
     dma("s", "dy", T.y[:], T.yb[:], "yb", "y")
-    V("set", "wns", "", T.wns[:, P * r:P * r + 136], float(P))
-    V("set", "wnc", "", T.wnc[:, P * r:P * r + 136], float(P))
-    V("ts", "wmb", "c16 tf", T.wmb[:], T.c16[:, 0:P], tf, None, op_.is_equal)
-    V("set", "r16b", "", T.r16b[:], 1.0)
-    V("set", "r16b", "", T.r16b[:, 0:P:16], 0.0)
-    V("ts", "jw", "k16 tf", T.fc[:, 18:26], T.fc[:, 10:18], tf, None, op_.add)
-    V("qz", "fwo fso", "tbt", T.fwc[:, 0:P], T.fws[:, 0:P], T.tbt[:])
 
     tot["a_kls"] = sum(len(e_s[f]) for f in from_s)
-    tot["a_klc"] = 4 * noff
+    tot["a_klc"] = 4 * noff // 2
     wr_["lls"] = [("a_kls", tot["a_kls"])]
     wr_["llc"] = [("a_klc", tot["a_klc"])]
     for q in sorted(same + [r], reverse=True):
@@ -450,21 +463,21 @@ def rank_program(g, core, T, topo):
     V("ts", "wu", "wsm2", T.wu[:], won, float(P - 1), None, op_.min)
     tot["a_pt"] = 7 * 2 * noff
     wr_["pwa"] = [("a_pt", tot["a_pt"])]
-    do("a", lambda q: q.activation(T.pps[:], T.pws[:].indirect(T.wu[:]), Copy), ["pwa", "pwo", "wu"], ["pps"])
+    S(Copy, "pps", "pwa pwo wu", T.pps[:], T.pws[:].indirect(T.wu[:]))
     V("copy", "ppc", "pwa pwo wu", u32(T.ppc[:]), u32(T.pwc[:]).indirect(T.wu[:]))
     for b in range(4):
         mm(T["pd%d" % b][:, 0:P], T.ec[:, P * b:P * b + P], T.es[:, P * b:P * b + P], T.ppc[:], T.pps[:], False, True, "ec es ppc pps", "pd%d" % b)
     V("ts", "wl", "wsm2", T.wl[:], won, float(P), float(P), op_.is_lt, op_.mult)
-    V("tt", "wl", "wl jw", T.wl[:], T.wl[:], T.fc[:, 18:26], op_.add)
+    V("tt", "wl", "wl sk", T.wl[:], T.wl[:], T.fc[:, 0:8], op_.add)
     V("copy", "fl", "wl", T.fl[:], T.wl[:])
     for b in range(4):
         o, i = T.nt[:, b:512:4], T["pd%d" % b][:, 0:P]
         if b % 2 == 0:
             V("copy", "nt%d" % b, "pd%d" % b, o, i)
         else:
-            do("a", lambda q: q.activation(o, i, Copy), ["pd%d" % b], ["nt%d" % b])
+            S(Copy, "nt%d" % b, "pd%d" % b, o, i)
     V("qz", "fwn fsn", "nt0 nt1 nt2 nt3", T.fwc[:, P:2 * P], T.fws[:, P:2 * P], T.nt[:])
-    do("a", lambda q: q.activation(T.fos[:], T.fws[:].indirect(T.fl[:]), Copy), ["fso", "fsn", "fl"], ["fos"])
+    S(Copy, "fos", "fso fsn fl", T.fos[:], T.fws[:].indirect(T.fl[:]))
     V("copy", "foc", "fwo fwn fl", u32(T.foc[:]), u32(T.fwc[:]).indirect(T.fl[:]))
     dma("s", "doc", T.oc[:], u8(T.foc[:]), "foc", "oc")
     for k in range(4):

@@ -14,30 +14,30 @@ def _sb(name, n, d):
 for _n, _w, _d in [
     ("cdi", 16, I32), ("cpi", 2, I32), ("tbt", 512, BF), ("xt", 512, BF), ("xu", 512, BF), ("wt", 512, BF),
     ("cdu", 32, U16), ("flg", 1024, BF), ("one", 128, BF), ("inc", 1024, BF), ("le", 1792, BF), ("cs", 1792, BF), ("rs", 512, BF),
-    ("sgo", 256, BF), ("sga", 16, F32), ("rq", 12, U16), ("rqx", 10, U16), ("rqr", 6, U16), ("rql", 22, U16),
+    ("sgo", 512, BF), ("sga", 16, F32), ("rq", 12, U16), ("rqx", 10, U16), ("rqr", 6, U16), ("rql", 22, U16),
     ("tbc", 128, X4), ("tbs", 128, U8), ("wc", 480, X4), ("ws", 480, U8), ("fwc", 256, X4), ("fws", 256, U8),
     ("xc", 128, X4), ("xs", 128, U8), ("wqc", 128, X4), ("wqs", 128, U8), ("pwc", 128, X4), ("pws", 128, U8),
     ("dcc", 192, X4), ("dcs", 192, U8), ("dsc", 144, X4), ("dss", 144, U8), ("rlc", 96, X4), ("rls", 96, U8),
     ("rpc", 16, X4), ("rps", 16, U8), ("kc", 288, X4), ("ks", 288, U8), ("ppc", 128, X4), ("pps", 128, U8),
     ("foc", 128, X4), ("fos", 128, U8), ("ebt", 2048, BF), ("ec", 512, X4), ("es", 512, U8),
-    ("ii", 8, I32), ("fc", 36, F32), ("cj", 352, F32), ("idx", 1040, F32), ("c16", 256, F32), ("wm", 256, F32), ("wmb", 128, BF),
+    ("ii", 8, I32), ("fc", 40, F32), ("cj", 352, F32), ("idx", 1040, F32), ("c16", 256, F32), ("wm", 256, F32), ("wmb", 128, BF),
     ("r16", 256, F32), ("r16b", 128, BF), ("r64", 256, BF), ("lm", 64, F32), ("r17", 34, F32), ("r8", 32, F32), ("c4", 32, F32),
-    ("zm", 64, F32), ("hid", 128, BF), ("val", 512, BF), ("lgs", 6, U16), ("low2", 2, U16), ("lrep", 4, U16),
+    ("zt", 512, F32), ("nrz", 32, F32), ("hid", 128, BF), ("val", 512, BF), ("lgs", 6, U16), ("low2", 2, U16), ("lrep", 2, U16),
     ("loc", 1040, F32), ("cdk", 16, U16), ("posr", 256, F32), ("posm", 256, F32), ("posc", 256, F32), ("kpl", 16, U16),
     ("cpu", 2, U16), ("nr", 32, F32), ("lw", 32, F32),
-    ("pb", 288, F32), ("gs", 96, F32), ("tr", 64, F32), ("sr", 32, F32), ("qa", 192, F32), ("rku", 2, U16), ("ge2", 32, F32),
-    ("bsw", 40, F32), ("pk", 34, F32), ("bc", 64, F32), ("tm", 64, F32), ("own", 32, F32), ("msw", 40, I32), ("ms", 8, I32),
-    ("ui", 64, I32), ("fb", 64, F32), ("tmp", 8, F32), ("r4", 64, F32), ("qb", 192, F32), ("kl", 4, F32),
-    ("kr", 4, F32), ("ku", 4, U16), ("rw", 64, F32), ("rwm", 64, F32), ("eqd", 256, BF), ("scd", 256, BF), ("lf", 4, F32),
+    ("pb", 288, F32), ("gs", 64, F32), ("tr", 64, F32), ("qa", 128, F32), ("rku", 2, U16), ("ge2", 32, F32),
+    ("bsw", 40, F32), ("pk", 34, F32), ("pku", 2, U16), ("own", 32, F32), ("msw", 40, I32), ("ms", 8, I32), ("nsw", 40, F32),
+    ("ns", 8, F32), ("ui", 56, I32), ("fv", 8, F32), ("tmp", 16, F32), ("qb", 192, F32), ("klu", 4, U16),
+    ("kr", 4, F32), ("kru", 4, U16), ("rwm", 64, F32), ("eqd", 256, BF), ("scd", 256, BF), ("lf", 4, F32),
     ("lu", 4, U16), ("lr", 4, U16), ("ll", 28, U16), ("kpf", 64, F32), ("locr", 192, F32), ("yl", 8, U16), ("zb", 480, F32), ("yb", 64, F32),
-    ("wns", 1552, BF), ("wnc", 1552, BF), ("wsm", 384, BF), ("wl", 8, F32), ("wu", 8, U16), ("fl", 8, U16), ("nt", 512, BF),
+    ("wns", 1552, BF), ("wnc", 1552, BF), ("wno", 1552, BF), ("wsm", 512, BF), ("wl", 8, F32), ("wu", 8, U16), ("fl", 8, U16), ("nt", 512, BF),
 ]:
     _sb(_n, _w, _d)
 for _n in ("pg0", "pg1", "pz", "pd0", "pd1", "pd2", "pd3"):
     SCRATCH[_n] = ("psum", [128, 512], F32)
 SEMAPHORES = ["cv", "ca", "ct", "cg", "dcd", "dcp", "dtb", "dx", "dxu", "dw", "dkx", "drep", "dy", "dkp", "doc", "ls",
               "a_rqc", "a_rqs", "a_dt", "a_pt", "a_klc", "a_kls", "r_pt", "r_rq", "r_dt", "r_kl"]
-PART = ("lerq", "lerqx", "csrq", "csrqx", "lgf", "low2", "lrep", "loc", "cdk", "ui", "eqd", "bc", "yb", "zm", "ebz", "ebt", "slf",
+PART = ("lerq", "lerqx", "csrq", "csrqx", "lgf", "low2", "lrep", "loc", "cdk", "eqd", "yb", "ebz", "ebt", "rs1", "idxs",
         "rq", "rqx", "sgarq", "sgarqx")
 
 
@@ -220,8 +220,9 @@ def rank_program(g, core, T, topo):
     sk = [T.fc[:, k:k + 1] for k in range(8)]
     trs = [T.fc[:, 16 + k:17 + k] for k in range(4)]
     cpf, half2, pf2, n8, n8b = T.fc[:, 20:22], T.fc[:, 22:23], T.fc[:, 30:32], T.fc[:, 32:33], T.fc[:, 33:34]
+    lo, hi, half1 = T.fc[:, 36:37], T.fc[:, 37:38], T.fc[:, 38:39]
     c8, c17, c64 = T.cj[:, 0:32], T.cj[:, 32:66], T.cj[:, 96:352]
-    ge, gt, tt, cmp_, sc, slf = [T.qa[:, 32 * k:32 * k + 32] for k in range(6)]
+    eqt, gt, el = [T.qa[:, 32 * k:32 * k + 32] for k in range(3)]
     k4, ps, kn, eq, v4, sc8 = [T.qb[:, 32 * k:32 * k + 32] for k in range(6)]
 
     dma("a", "dx", T.xt[:, 0:64], T.x[:], "", "xt")
@@ -240,58 +241,67 @@ def rank_program(g, core, T, topo):
     iota(pf2, "pf2", [[0, 2]], 0, 1)
 
     V("set", "xtz", "", T.xt[:, 64:512], 0.0)
-    V("ts", "ti", "pin", ti, pin, 15, None, op_.bitwise_and)
-    V("set", "flg", "", T.flg[:], 0.0)
-    V("copy", "tf", "ti", T.fc[:, 34:36], ti)
     V("set", "one", "", T.one[:], 1.0)
-    V("ts", "sk", "k16 tf", T.fc[:, 0:8], T.fc[:, 8:16], T.fc[:, 34:35], None, op_.add)
-    V("set", "rs", "", T.rs[:], 1.0)
-    V("set", "rs", "", T.rs[:, 0:512:128], 0.0)
+    V("set", "flg", "", T.flg[:], 0.0)
 
-    S(Ident, "half2", "sk", half2, sk[2], bias=0.5)
+    for k in range(4):
+        S(Copy, "rs1", "one", T.rs[:, P * k:P * k + P], T.one[:])
+    S(Copy, "rs", "rs1 xtz", T.rs[:, 0:512:128], T.xt[:, 64:68])
     S(Sign, "r16", "c16", T.r16[:], T.c16[:])
-    S(Abs, "wm", "c16 sk", T.wm[:], T.c16[:], bias=tf, scale=-1.0)
-    S(Relu, "wm", "wm", T.wm[:], T.wm[:], bias=1.0, scale=-1.0)
     S(Copy, "xuz", "xtz", T.xu[:, 0:448], T.xt[:, 64:512])
-    S(Copy, "n8", "sk", n8, tf, scale=-0.125)
-    S(Ident, "n8b", "n8", n8b, n8, bias=273.0)
-    S(Ident, "lgf", "pf2 n8", T.fc[:, 26:28], pf2, bias=n8, scale=0.125)
-    S(Ident, "lgf", "pf2 n8b", T.fc[:, 28:30], pf2, bias=n8b, scale=0.125)
 
     V("qz", "xc xs", "xt xtz", T.xc[:], T.xs[:], T.xt[:])
     send([(u8(T.xc[:, 0:16]), [u8(T.rpc[:])] * 2, ids_r[0:2], e_h[0], "r_pt")], "xc")
     send([(T.xs[:, 0:16], [T.rps[:]] * 2, ids_r[2:4], e_h[1], "r_pt")], "xs")
+    iota(T.idx[:, 0:256], "idx", [[1, 256]])
 
     V("copy", "cdu", "cdi", T.cdu[:, 0:32:2], T.cdi[:])
     for i in range(A):
         V("copy", "flg", "cdu one", T.flg[:].indirect(T.cdu[:, 2 * i:2 * i + 1]), T.one[:, 0:16])
+        if i == 0:
+            V("ts", "ti", "pin", ti, pin, 15, None, op_.bitwise_and)
+        elif i == 1:
+            V("copy", "tf", "ti", T.fc[:, 34:36], ti)
+        elif i == 2:
+            V("ts", "sk", "k16 tf", T.fc[:, 0:8], T.fc[:, 8:16], T.fc[:, 34:35], None, op_.add)
+    S(Ident, "half2", "sk", half2, sk[2], bias=0.5)
+    S(Ident, "half1", "sk", half1, sk[1], bias=0.5)
+    S(Copy, "n8", "sk", n8, tf, scale=-0.125)
+    S(Copy, "lhc", "sk", T.fc[:, 39:40], tf, scale=-1.0)
+    S(Ident, "hi", "sk", hi, tf, bias=-7.5)
+    S(Ident, "n8b", "n8", n8b, n8, bias=273.0)
+    S(Ident, "lo", "lhc", lo, T.fc[:, 39:40], bias=7.5)
+    S(Ident, "lgf", "pf2 n8", T.fc[:, 26:28], pf2, bias=n8, scale=0.125)
+    S(Ident, "lgf", "pf2 n8b", T.fc[:, 28:30], pf2, bias=n8b, scale=0.125)
 
-    def lists(qs, base, name, out):
+    def lists(qs, base, name, out, more):
         n = len(qs)
         h0 = base // P
+        nk = [n, n - more]
+        todo = [(x, half2, h0 + x) for x in range(n)] + [(x, half1, h0 + 4 + x) for x in range(n - more, n)]
         for x, q in enumerate(qs):
             V("scan", "inc%d" % q, "flg one", T.inc[:, P * q:P * q + P], T.one[:], T.flg[:, P * q:P * q + P], 0.0, op_.mult, op_.add)
-        for x, q in enumerate(qs):
-            h = h0 + x
-            b = P * (h % 2)
-            S(Sign, "sgo%d sga%s" % (h % 2, name), "inc%d half2" % q, T.sgo[:, b:b + P - 1], T.inc[:, P * q:P * q + P - 1],
-              bias=half2, scale=-1.0, accum_out=T.sga[:, h:h + 1])
+        for y, (x, half, col) in enumerate(todo):
+            b = P * (y % 4)
+            S(Sign, "sgo%d sga%s" % (y % 4, name), "inc%d half1 half2" % qs[x], T.sgo[:, b:b + P - 1], T.inc[:, P * qs[x]:P * qs[x] + P - 1],
+              bias=half, scale=-1.0, accum_out=T.sga[:, col:col + 1])
         for k in range(2):
-            for x, q in enumerate(qs):
+            for x in range(nk[k]):
                 a = base + P * (n * k + x)
-                V("ts", "le" + name, "inc%d sk" % q, T.le[:, a:a + P], T.inc[:, P * q:P * q + P], sk[k], None, op_.is_le)
+                V("ts", "le" + name, "inc%d sk" % qs[x], T.le[:, a:a + P], T.inc[:, P * qs[x]:P * qs[x] + P], sk[k], None, op_.is_le)
         for k in range(2):
-            a, e = base + P * n * k, base + P * n * (k + 1)
-            V("scan", "cs" + name, "rs le" + name, T.cs[:, a:e], T.rs[:, 0:P * n], T.le[:, a:e], 0.0, op_.mult, op_.add)
+            a, e = base + P * n * k, base + P * (n * k + nk[k])
+            V("scan", "cs" + name, "rs le" + name, T.cs[:, a:e], T.rs[:, 0:P * nk[k]], T.le[:, a:e], 0.0, op_.mult, op_.add)
         V("ts", name, "sga" + name, out[:, 2:3 * n:3], T.sga[:, h0:h0 + n], 0.5, 0.5 * (P - 1), op_.mult, op_.add)
+        if more:
+            V("ts", name, "sga" + name, out[:, 3 * (n - more) + 1:3 * n:3], T.sga[:, h0 + 4 + n - more:h0 + 4 + n], 0.5, 0.5 * (P - 1), op_.mult, op_.add)
         for k in range(2):
-            V("copy", name, "cs" + name, out[:, k:3 * n:3], T.cs[:, base + P * n * k + P - 2:base + P * n * (k + 1):P])
+            V("copy", name, "cs" + name, out[:, k:3 * nk[k]:3], T.cs[:, base + P * n * k + P - 2:base + P * (n * k + nk[k]):P])
 
-    lists(cross, 0, "rq", T.rq)
+    lists(cross, 0, "rq", T.rq, 2)
     send([(T.rq[:, 6 * h:6 * h + 6], [T.rqr[:]], [ids_r[h]], e_h[h], "r_rq") for h in range(2)], "rq")
-    lists(same, 1024, "rqx", T.rqx)
+    lists(same, 1024, "rqx", T.rqx, 0)
     send([(T.rqx[:, 3 * y:3 * y + 3], [T.rql[:, 3 * at_s[y]:3 * at_s[y] + 3]], [ids_s[y]], e_s[y], "a_rqs") for y in range(3)], "rqx")
-    iota(T.idx[:], "idx", [[1, 1040]])
 
     V("qz", "tbc tbs", "tbt", T.tbc[:], T.tbs[:], T.tbt[:])
     for x, q in enumerate(peers):
@@ -307,8 +317,7 @@ def rank_program(g, core, T, topo):
     V("copy", "lgs", "lgf", T.lgs[:], T.fc[:, 24:30])
     V("ts", "low2", "oi", T.low2[:, 0:1], oi1, 0.0, None, op_.add)
     V("ts", "low2", "oi", T.low2[:, 1:2], oi1, 32.0, None, op_.add)
-    V("ts", "lrep", "o7", T.lrep[:, 0:2], o7, 0.0, None, op_.add)
-    V("ts", "lrep", "o7", T.lrep[:, 2:4], o7, 56.0, None, op_.add)
+    V("ts", "lrep", "o7", T.lrep[:], o7, 0.0, None, op_.add)
 
     tot["a_rqc"] = 4 * noff // 2
     tot["a_rqs"] = sum(len(e_s[f]) for f in from_s)
@@ -325,8 +334,6 @@ def rank_program(g, core, T, topo):
     send([(T.dss[:, LC * y:LC * y + LC], [T.ws[:, ws_[y]:ws_[y] + LC]], [ids_s[y]], e_s2[y], "a_dt") for y in range(3)], "dss")
     iota(c17, "c17", [[0, 2], [1, 17]])
     iota(c8, "c8", [[0, 4], [1, 8]])
-    iota(T.zm[:, 0:32], "zm", [[0, 2], [-1, 2], [0, 8]], 1)
-    iota(T.zm[:, 32:64], "zm", [[0, 2], [1, 2], [0, 8]])
     iota(T.c4[:], "c4", [[1, 4], [0, 8]], 1)
     send([(u8(T.xc[:, 0:16]), [u8(T.pwc[:, 16 * r:16 * r + 16])] * 3, ids_s, eoff, "a_pt")], "xc")
     send([(T.xs[:, 0:16], [T.pws[:, 16 * r:16 * r + 16]] * 3, ids_s, eoff, "a_pt")], "xs")
@@ -335,25 +342,33 @@ def rank_program(g, core, T, topo):
     iota(T.val[:], "val", [[16, 8], [0, 4], [1, 16]])
 
     S(Ident, "loc", "idx", T.loc[:, 1 + P * r:1 + P * r + P], T.idx[:, 0:P], bias=0.0)
-    for j in range(2):
-        S(Copy, "slf", "wm", T.qa[:, 160 + 16 * j:176 + 16 * j], T.wm[:, 0:16], scale=float(1 + 17 * j))
-    S(Ident, "bsw", "cpf", T.bsw[:, 0:34:17], cpf, bias=1.0)
-    S(Copy, "fb0", "c16", T.fb[:, 0:1], T.c16[:, 0:1])
+    S(Abs, "wm", "c16 sk", T.wm[:], T.c16[:], bias=tf, scale=-1.0)
+    for k in range(1, 4):
+        S(Ident, "idxs", "idx", T.idx[:, 256 * k:256 * k + 256], T.idx[:, 0:256], bias=float(256 * k))
+    S(Ident, "idxs", "idx", T.idx[:, 1024:1040], T.idx[:, 0:16], bias=1024.0)
+    S(Relu, "wm", "wm", T.wm[:], T.wm[:], bias=1.0, scale=-1.0)
+    S(Sign, "lh", "lo hi", T.fc[:, 36:38], T.fc[:, 36:38])
+    S(Copy, "bsw", "c16", T.bsw[:, 0:34:17], T.c16[:, 0:2])
+    S(Relu, "lh", "lh", T.fc[:, 36:38], T.fc[:, 36:38])
+    S(Copy, "fv0", "c16", T.fv[:, 0:1], T.c16[:, 0:1])
+    S(Ident, "zt1", "idx lh", T.zt[:, 0:256], T.idx[:, 0:256], scale=lo)
+    S(Ident, "zt2", "idx lh", T.zt[:, 256:512], T.idx[:, 0:256], scale=hi)
     S(Sign, "r17", "c17", T.r17[:], c17)
-    S(Copy, "r17", "r17", T.r17[:], T.r17[:], scale=2.0)
     S(Sign, "r8", "c8", T.r8[:], c8)
+    S(Copy, "r17", "r17", T.r17[:], T.r17[:], scale=2.0)
     V("qz", "wco wso", "tbt", T.wc[:, 0:P], T.ws[:, 0:P], T.tbt[:])
     V("copy", "posr", "loc locz locy cdk", T.posr[:], T.loc[:].indirect(T.cdk[:]))
     V("qz", "kcx ksx", "xt xtz", T.kc[:, 0:P], T.ks[:, 0:P], T.xt[:])
     V("tt", "posm", "posr wm", T.posm[:], T.posr[:], T.wm[:], op_.mult)
     V("qz", "kcx ksx", "xu xuz", T.kc[:, 160:288], T.ks[:, 160:288], T.xu[:])
     V("scan", "posc", "posm r16", T.posc[:], T.r16[:], T.posm[:], 0.0, op_.mult, op_.add)
-    V("copy", "nr", "idx cpu", T.nr[:], T.idx[:].indirect(T.cpu[:]))
+    V("copy", "nr", "idx idxs cpu", T.nr[:], T.idx[:].indirect(T.cpu[:]))
     V("copy", "kpl", "posc", T.kpl[:], T.posc[:, 15:256:16])
     for j in range(2):
         V("ts", "lw%d" % j, "nr cpf", T.lw[:, 16 * j:16 * j + 16], T.nr[:, 16 * j:16 * j + 16], T.fc[:, 20 + j:21 + j], None, op_.is_lt)
+        S(Ident, "nrz%d" % j, "nr lh", T.nrz[:, 16 * j:16 * j + 16], T.nr[:, 16 * j:16 * j + 16], bias=[lo, hi][j], scale=[lo, hi][j])
     V("qz", "wqc wqs", "wt", T.wqc[:], T.wqs[:], T.wt[:])
-    V("tt", "lw", "lw0 lw1 slf", T.lw[:], T.lw[:], slf, op_.add)
+    V("qz", "fwo fso", "tbt", T.fwc[:, 0:P], T.fws[:, 0:P], T.tbt[:])
 
     tot["a_dt"] = 4 * noff + sum(len(e_s[f]) + len(e_s2[f]) for f in from_s)
     wr_["wca"] = [("a_dt", tot["a_dt"])]
@@ -368,61 +383,92 @@ def rank_program(g, core, T, topo):
     S(Copy, "pb1", "pg1", T.pb[:, 144:288], T.pg1[:, 0:144])
     S(Copy, "zb", "pz", T.zb[:, 0:WCOLS], T.pz[:, 0:WCOLS])
     S(Sign, "lm", "c16 sk", T.lm[:], T.c16[:, 0:64], bias=tf, scale=-1.0)
-    S(Relu, "lm", "lm", T.lm[:], T.lm[:])
     S(Ident, "trs", "sk", T.fc[:, 16:20], T.fc[:, 0:4], bias=1032.0, scale=8.0)
+    S(Relu, "lm", "lm", T.lm[:], T.lm[:])
     S(Sign, "r64", "c64", T.r64[:], c64)
-    V("copy", "gs", "pb0 pb1 lgs", T.gs[:], T.pb[:].indirect(T.lgs[:]))
-    V("tr", "tr", "gs", T.tr[:], T.gs[:, 32:96])
-    V("tt", "ge2", "gs", T.ge2[:], T.gs[:, 0:32], T.gs[:, 48:80], op_.is_ge)
-    V("copy", "sr", "tr low2", T.sr[:], T.tr[:].indirect(T.low2[:]))
-    V("tt", "ge", "sr gs", ge, T.sr[:], T.gs[:, 48:80], op_.is_ge)
-    V("tt", "gt", "sr gs", gt, T.sr[:], T.gs[:, 48:80], op_.is_gt)
-    V("tt", "tt", "ge lw", tt, ge, T.lw[:], op_.mult)
-    V("tt", "cmp", "tt gt", cmp_, tt, gt, op_.max)
-    V("scan", "sc", "cmp r16", sc, T.r16[:, 0:32], cmp_, 0.0, op_.mult, op_.add)
-    V("copy", "rku", "sc", T.rku[:], T.qa[:, 143:160:16])
+    V("copy", "gs", "pb0 pb1 lgs", T.gs[:], T.pb[:].indirect(T.lgs[:, 2:6]))
+    V("tr", "tr", "gs", T.tr[:], T.gs[:])
+    V("tt", "ge2", "pb0 pb1 lgs gs", T.ge2[:], T.pb[:].indirect(T.lgs[:, 0:2]), T.gs[:, 16:48], op_.is_ge)
+    V("tt", "eqt", "tr low2 gs", eqt, T.tr[:].indirect(T.low2[:]), T.gs[:, 16:48], op_.is_equal)
+    V("tt", "gt", "tr low2 gs", gt, T.tr[:].indirect(T.low2[:]), T.gs[:, 16:48], op_.is_gt)
+    V("tt", "el", "eqt lw0 lw1", el, eqt, T.lw[:], op_.mult)
+    for j in range(2):
+        a = 16 * j
+        V("scan", "sc%d" % j, "gt el", T.qa[:, 96 + a:112 + a], T.qa[:, 32 + a:48 + a], T.qa[:, 64 + a:80 + a], float(1 + 17 * j), op_.add, op_.add)
+    V("copy", "rku", "sc0 sc1", T.rku[:], T.qa[:, 111:128:16])
     V("copy", "bsw", "ge2 rku", T.bsw[:].indirect(T.rku[:]), T.ge2[:])
+    V("copy", "nsw", "nrz0 nrz1 rku", T.nsw[:].indirect(T.rku[:]), T.nrz[:])
     V("scan", "pk", "bsw r17", T.pk[:], T.r17[:], T.bsw[:, 0:34], 0.0, op_.mult, op_.add)
-    V("ts", "bc", "pk zm", T.bc[:, 0:32], T.zm[:, 0:32], T.pk[:, 8:9], None, op_.mult)
-    V("ts", "bc", "pk zm", T.bc[:, 32:64], T.zm[:, 32:64], T.pk[:, 25:26], None, op_.mult)
-    V("tr", "tm", "bc", T.tm[:], T.bc[:])
-    V("copy", "own", "tm low2", T.own[:], T.tm[:].indirect(T.low2[:]))
+    V("tt", "ns", "nsw", T.ns[:], T.nsw[:, 1:9], T.nsw[:, 18:26], op_.add)
+    V("copy", "pku", "pk", T.pku[:], T.pk[:, 8:26:17])
+    V("copy", "own", "zt1 zt2 pku", T.own[:], T.zt[:].indirect(T.pku[:]))
     V("copy", "msw", "own rku", T.msw[:].indirect(T.rku[:]), T.own[:])
     V("tt", "ms", "msw", T.ms[:], T.msw[:, 1:9], T.msw[:, 18:26], op_.add)
-    for m in range(7):
-        V("ts", "ui", "ms", T.ui[:, 8 * m:8 * m + 8], T.ms[:], 7 - m, 1, op_.logical_shift_right, op_.bitwise_and)
-    V("ts", "ui", "ms", T.ui[:, 56:64], T.ms[:], 8, None, op_.logical_shift_right)
-    V("copy", "fb", "ui", T.fb[:, 1:64], T.ui[:, 1:64])
-    for m in range(1, 6):
-        V("ts", "tmp", "fb", T.tmp[:, 0:7 - m], T.fb[:, 9 * m + 1:8 * m + 8], T.fb[:, m:m + 1], None, op_.subtract)
-        V("tt", "fb", "tmp", T.fb[:, m + 1:8], T.fb[:, m + 1:8], T.tmp[:, 0:7 - m], op_.max)
-    V("ts", "fb", "fb", T.fb[:, 7:8], T.fb[:, 55:56], T.fb[:, 6:7], T.fb[:, 7:8], op_.subtract, op_.max)
-    V("copy", "r4", "fb fb0 lrep", T.r4[:], T.fb[:].indirect(T.lrep[:]))
-    V("ts", "k4", "r4", k4, T.r4[:, 0:32], 0.0, None, op_.is_equal)
+
+    def plane(m):
+        V("ts", "ui%d" % m, "ms", T.ui[:, 8 * m:8 * m + 8], T.ms[:], 7 - m, 1, op_.logical_shift_right, op_.bitwise_and)
+
+    def pair(m, j):
+        V("ts", "fv%d" % j, "ui%d fv%d fv%d" % (m, m, j), T.fv[:, j:j + 1], T.ui[:, 8 * m + j:8 * m + j + 1], T.fv[:, m:m + 1],
+          T.fv[:, j:j + 1], op_.subtract, op_.max)
+
+    def far(m):
+        a = m + 3
+        V("ts", "tmp%d" % m, "ui%d fv%d" % (m, m), T.tmp[:, 8 * m - 8 + a:8 * m], T.ui[:, 8 * m + a:8 * m + 8], T.fv[:, m:m + 1], None, op_.subtract)
+
+    def far2(m):
+        a = m + 3
+        k = " ".join("fv%d" % j for j in range(a, 8))
+        V("tt", k, "tmp%d " % m + k, T.fv[:, a:8], T.fv[:, a:8], T.tmp[:, 8 * m - 8 + a:8 * m], op_.max)
+
+    plane(0)
+    plane(1)
+    V("copy", "fv1 fv2 fv3 fv4 fv5 fv6 fv7", "ui0", T.fv[:, 1:8], T.ui[:, 1:8])
+    plane(2)
+    pair(1, 2)
+    pair(1, 3)
+    far(1)
+    plane(3)
+    pair(2, 3)
+    far2(1)
+    plane(4)
+    pair(2, 4)
+    far(2)
+    plane(5)
+    pair(3, 4)
+    far2(2)
+    plane(6)
+    for m in range(3, 7):
+        for j in range(m + 1, 8):
+            if (m, j) != (3, 4):
+                pair(m, j)
+    V("ts", "k4", "fv0 fv1 fv2 fv3 fv4 fv5 fv6 fv7 lrep", k4, T.fv[:].indirect(T.lrep[:]), 0.0, None, op_.is_equal)
     V("scan", "ps", "k4 r8", ps, T.r8[:], k4, 0.0, op_.mult, op_.add)
-    V("tt", "kn", "k4 r4", kn, k4, T.r4[:, 32:64], op_.mult)
+    V("tt", "kn", "ns k4 lrep", kn, T.ns[:].indirect(T.lrep[:]), k4, op_.mult)
     V("tt", "eq", "ps c4", eq, ps, T.c4[:], op_.is_equal)
     V("tt", "v4", "eq kn", v4, eq, kn, op_.mult)
     V("scan", "sc8", "v4 r8", sc8, T.r8[:], v4, 0.0, op_.mult, op_.add)
-    V("copy", "kl", "sc8", T.kl[:], T.qb[:, 167:192:8])
-    for k in range(8):
-        dma("s" if k % 2 == 0 else "a", "drep", T.kr[16 * k:16 * k + 16, :], T.kl[0:128:8, :], "kl", "kr")
-    dma("s", "dkx", u8(T.pwc[:, 16 * r:16 * r + 16]), u8(T.xc[:, 0:16]), "xc", "pwo")
-    dma("s", "dkx", T.pws[:, 16 * r:16 * r + 16], T.xs[:, 0:16], "xs", "pwo")
+    V("copy", "klu", "sc8", T.klu[:], T.qb[:, 167:192:8])
     for a in range(0, 2048, 448):
         w = min(448, 2048 - a)
         S(Copy, "ebz", "xtz", T.ebt[:, a:a + w], T.xt[:, 64:64 + w])
     for b in range(4):
         S(Copy, "ebt", "hid ebz", T.ebt[:, 512 * b + b:512 * b + 512:4], T.hid[:], scale=0.5)
+    for k in range(8):
+        dma("s" if k % 2 == 0 else "a", "drep", T.kru[16 * k:16 * k + 16, :], T.klu[0:128:8, :], "klu", "kru")
+    dma("s", "dkx", u8(T.pwc[:, 16 * r:16 * r + 16]), u8(T.xc[:, 0:16]), "xc", "pwo")
+    dma("s", "dkx", T.pws[:, 16 * r:16 * r + 16], T.xs[:, 0:16], "xs", "pwo")
+    V("qz", "ec es", "ebt ebz", T.ec[:], T.es[:], T.ebt[:])
+    for b in range(4):
+        mm(T["pd%d" % b][:, 0:P], T.ec[:, P * b:P * b + P], T.es[:, P * b:P * b + P], T.tbc[:], T.tbs[:], True, False, "ec es tbc tbs", "pd%d" % b)
     S(Copy, "zbz", "xtz", T.zb[:, WCOLS:480], T.xt[:, 64:80])
-    for k in ("wns", "wnc"):
+    for k in ("wno", "wns", "wnc"):
         S(Copy, k, "one", T[k][:, P * r + 1:P * r + 1 + P], T.one[:], scale=float(P))
     S(Copy, "wmb", "wm", T.wmb[:], T.wm[:, 0:P])
     S(Sign, "r16b", "c16", T.r16b[:], T.c16[:, 0:P])
 
-    V("copy", "ku", "kr", T.ku[:], T.kr[:])
-    V("copy", "rw", "idx ku", T.rw[:], T.idx[:].indirect(T.ku[:]))
-    V("tt", "rwm", "rw lm", T.rwm[:], T.rw[:], T.lm[:], op_.mult)
+    V("copy", "kr", "kru", T.kr[:], T.kru[:])
+    V("tt", "rwm", "idx idxs kru lm", T.rwm[:], T.idx[:].indirect(T.kru[:]), T.lm[:], op_.mult)
     for k in range(4):
         V("ts", "eqd", "rwm kr trs", T.eqd[:, 64 * k:64 * k + 64], T.rwm[:], T.kr[:, k:k + 1], trs[k], op_.is_equal, op_.mult)
     V("scan", "scd", "eqd r64", T.scd[:], T.r64[:], T.eqd[:], 0.0, op_.mult, op_.max)
@@ -431,29 +477,27 @@ def rank_program(g, core, T, topo):
     send([(T.lu[:], [T.lr[:]] * 2, ids_r[0:2], eon, "r_kl")], "lu")
     send([(T.lu[:], [T.ll[:, 4 * at_s[y]:4 * at_s[y] + 4]], [ids_s[y]], e_s[y], "a_kls") for y in range(3)], "lu")
 
-    S(Ident, "kpf", "rw", T.kpf[:], T.rw[:], bias=-1.0)
+    S(Copy, "locr", "loc locz locy kru", T.locr[:, 0:64], T.loc[:].indirect(T.kru[:]))
+    S(Ident, "kpf", "idx idxs kru", T.kpf[:], T.idx[:].indirect(T.kru[:]), bias=-1.0)
     dma("s", "dkp", T.kp[:], T.kpf[0:1, :], "kpf", "kp")
-    V("copy", "locr", "loc locz locy ku", T.locr[:, 0:64], T.loc[:].indirect(T.ku[:]))
-    V("qz", "fwo fso", "tbt", T.fwc[:, 0:P], T.fws[:, 0:P], T.tbt[:])
+    s = P * r + 1
+    V("copy", "wno", "val lu", T.wno[:].indirect(T.lu[:]), T.val[:, 64 * r:64 * r + 64])
     V("tt", "loc2", "locr wm", T.locr[:, 64:128], T.locr[:, 0:64], T.wm[:, 0:64], op_.mult)
-    V("qz", "ec es", "ebt ebz", T.ec[:], T.es[:], T.ebt[:])
-    for b in range(4):
-        mm(T["pd%d" % b][:, 0:P], T.ec[:, P * b:P * b + P], T.es[:, P * b:P * b + P], T.tbc[:], T.tbs[:], True, False, "ec es tbc tbs", "pd%d" % b)
+    V("tt", "wsmo", "wno wmb", T.wsm[:, 3 * P:4 * P], T.wno[:, s:s + P], T.wmb[:], op_.mult)
     V("scan", "loc3", "loc2 r16", T.locr[:, 128:192], T.r16[:, 0:64], T.locr[:, 64:128], 0.0, op_.mult, op_.add)
     V("copy", "yl", "loc3", T.yl[:, 0:8:2], T.locr[:, 143:192:16])
     for k in range(4):
-        V("copy", "yb", "zb zbz yl", T.yb[:, k:64:4], T.zb[:].indirect(T.yl[:, 2 * k:2 * k + 1]))
+        S(Copy, "yb", "zb zbz yl", T.yb[:, k:64:4], T.zb[:].indirect(T.yl[:, 2 * k:2 * k + 1]))
     dma("s", "dy", T.y[:], T.yb[:], "yb", "y")
 
     tot["a_kls"] = sum(len(e_s[f]) for f in from_s)
     tot["a_klc"] = 4 * noff // 2
     wr_["lls"] = [("a_kls", tot["a_kls"])]
     wr_["llc"] = [("a_klc", tot["a_klc"])]
-    for q in sorted(same + [r], reverse=True):
-        off = T.lu[:] if q == r else T.ll[:, 4 * peers.index(q):4 * peers.index(q) + 4]
-        V("copy", "wns", "val " + ("lu" if q == r else "lls"), T.wns[:].indirect(off), T.val[:, 64 * q:64 * q + 64])
-    s = P * r + 1
-    V("tt", "wsm0", "wns wmb", T.wsm[:, 0:P], T.wns[:, s:s + P], T.wmb[:], op_.mult)
+    for q in sorted(same, reverse=True):
+        c = 4 * peers.index(q)
+        V("copy", "wns", "val lls", T.wns[:].indirect(T.ll[:, c:c + 4]), T.val[:, 64 * q:64 * q + 64])
+    V("tt", "wsm0", "wns wsmo", T.wsm[:, 0:P], T.wns[:, s:s + P], T.wsm[:, 3 * P:4 * P], op_.min)
     for q in sorted(cross, reverse=True):
         c = 4 * peers.index(q)
         V("copy", "wnc", "val llc", T.wnc[:].indirect(T.ll[:, c:c + 4]), T.val[:, 64 * q:64 * q + 64])

@@ -13,22 +13,24 @@ def _sb(name, n, d):
 
 for _n, _w, _d in [
     ("cdi", 16, I32), ("cpi", 2, I32), ("tbt", 512, BF), ("xt", 512, BF), ("xu", 512, BF), ("wt", 512, BF),
-    ("cdu", 32, U16), ("flg", 1024, BF), ("one", 128, BF), ("inc", 1024, BF), ("le", 1792, BF), ("cs", 1792, BF), ("rs", 512, BF),
+    ("cdu", 32, U16), ("fla", 1024, BF), ("flb", 1024, BF), ("mrg", 1024, BF), ("nam", 1024, BF), ("one", 128, BF),
+    ("inc", 1024, BF), ("le", 1792, BF), ("cs", 1792, BF), ("rs", 512, BF),
     ("sgo", 512, BF), ("sga", 16, F32), ("rq", 12, U16), ("rqx", 10, U16), ("rqr", 6, U16), ("rql", 22, U16),
     ("tbc", 128, X4), ("tbs", 128, U8), ("wc", 480, X4), ("ws", 480, U8), ("fwc", 256, X4), ("fws", 256, U8),
     ("xc", 128, X4), ("xs", 128, U8), ("wqc", 128, X4), ("wqs", 128, U8), ("pwc", 128, X4), ("pws", 128, U8),
+    ("xrc", 256, X4), ("xrs", 256, U8),
     ("dcc", 192, X4), ("dcs", 192, U8), ("dsc", 144, X4), ("dss", 144, U8), ("rlc", 96, X4), ("rls", 96, U8),
     ("rpc", 16, X4), ("rps", 16, U8), ("kc", 288, X4), ("ks", 288, U8), ("ppc", 128, X4), ("pps", 128, U8),
     ("foc", 128, X4), ("fos", 128, U8), ("ebt", 2048, BF), ("ec", 512, X4), ("es", 512, U8),
-    ("ii", 8, I32), ("fc", 40, F32), ("cj", 352, F32), ("idx", 1040, F32), ("c16", 256, F32), ("wm", 256, F32), ("wmb", 128, BF),
-    ("r16", 256, F32), ("r16b", 128, BF), ("r64", 256, BF), ("lm", 64, F32), ("r17", 34, F32), ("r8", 32, F32), ("c4", 32, F32),
-    ("zt", 512, F32), ("nrz", 32, F32), ("hid", 128, BF), ("val", 512, BF), ("lgs", 6, U16), ("low2", 2, U16), ("lrep", 2, U16),
-    ("loc", 1040, F32), ("cdk", 16, U16), ("posr", 256, F32), ("posm", 256, F32), ("posc", 256, F32), ("kpl", 16, U16),
+    ("ii", 8, I32), ("fc", 40, F32), ("cj", 96, F32), ("idx", 1040, F32), ("c16", 256, F32), ("wm", 256, F32), ("wmb", 128, BF),
+    ("r16", 256, F32), ("r16b", 128, BF), ("lm", 64, F32), ("r17", 34, F32), ("r8", 32, F32), ("c4", 32, F32),
+    ("zt", 512, F32), ("nrz", 32, F32), ("hid", 128, BF), ("val", 512, BF), ("lgs", 6, U16), ("lrep", 2, U16), ("xl", 16, U16),
+    ("loc", 1040, F32), ("cdk", 16, U16), ("posm", 256, F32), ("posc", 256, F32), ("kpl", 16, U16),
     ("cpu", 2, U16), ("nr", 32, F32), ("lw", 32, F32),
-    ("pb", 288, F32), ("gs", 64, F32), ("tr", 64, F32), ("qa", 128, F32), ("rku", 2, U16), ("ge2", 32, F32),
+    ("pb", 288, F32), ("pbx", 256, F32), ("gs", 32, F32), ("qa", 128, F32), ("rku", 2, U16), ("ge2", 32, F32),
     ("bsw", 40, F32), ("pk", 34, F32), ("pku", 2, U16), ("own", 32, F32), ("msw", 40, I32), ("ms", 8, I32), ("nsw", 40, F32),
-    ("ns", 8, F32), ("ui", 56, I32), ("fv", 8, F32), ("tmp", 16, F32), ("qb", 192, F32), ("klu", 4, U16),
-    ("kr", 4, F32), ("kru", 4, U16), ("rwm", 64, F32), ("eqd", 256, BF), ("scd", 256, BF), ("lf", 4, F32),
+    ("ui", 56, I32), ("fv", 8, F32), ("pn", 48, F32), ("qb", 96, F32), ("klu", 4, U16),
+    ("kr", 4, F32), ("kru", 4, U16), ("rwm", 64, F32), ("eqd", 256, BF), ("scf", 256, F32),
     ("lu", 4, U16), ("lr", 4, U16), ("ll", 28, U16), ("kpf", 64, F32), ("locr", 192, F32), ("yl", 8, U16), ("zb", 480, F32), ("yb", 64, F32),
     ("wns", 1552, BF), ("wnc", 1552, BF), ("wno", 1552, BF), ("wsm", 512, BF), ("wl", 8, F32), ("wu", 8, U16), ("fl", 8, U16), ("nt", 512, BF),
 ]:
@@ -37,7 +39,7 @@ for _n in ("pg0", "pg1", "pz", "pd0", "pd1", "pd2", "pd3"):
     SCRATCH[_n] = ("psum", [128, 512], F32)
 SEMAPHORES = ["cv", "ca", "ct", "cg", "dcd", "dcp", "dtb", "dx", "dxu", "dw", "dkx", "drep", "dy", "dkp", "doc", "ls",
               "a_rqc", "a_rqs", "a_dt", "a_pt", "a_klc", "a_kls", "r_pt", "r_rq", "r_dt", "r_kl"]
-PART = ("lerq", "lerqx", "csrq", "csrqx", "lgf", "low2", "lrep", "loc", "cdk", "eqd", "yb", "ebz", "ebt", "rs1", "idxs",
+PART = ("lerq", "lerqx", "csrq", "csrqx", "lgf", "lrep", "loc", "cdk", "yb", "ebz", "ebt", "rs1", "idxs",
         "rq", "rqx", "sgarq", "sgarqx")
 
 
@@ -159,7 +161,7 @@ def rank_program(g, core, T, topo):
     def V(name, wr, rd, *args):
         def fn(q):
             f = {"copy": q.tensor_copy, "tt": q.tensor_tensor, "ts": q.tensor_scalar, "set": q.memset,
-                 "scan": q.tensor_tensor_scan, "tr": q.transpose, "qz": q.quantize_mx}[name]
+                 "scan": q.tensor_tensor_scan, "qz": q.quantize_mx}[name]
             return f(*args)
         do("v", fn, rd.split(), wr.split())
 
@@ -214,16 +216,16 @@ def rank_program(g, core, T, topo):
         at_s.append(4 + sq.index(r))
         from_s.append(sq.index(r))
 
-    pin, ti, oi, o7 = [T.ii[:, 2 * k:2 * k + 2] for k in range(4)]
-    oi1 = T.ii[:, 4:5]
+    pin, ti, o7 = [T.ii[:, 2 * k:2 * k + 2] for k in range(3)]
     tf = T.fc[:, 0:1]
     sk = [T.fc[:, k:k + 1] for k in range(8)]
     trs = [T.fc[:, 16 + k:17 + k] for k in range(4)]
-    cpf, half2, pf2, n8, n8b = T.fc[:, 20:22], T.fc[:, 22:23], T.fc[:, 30:32], T.fc[:, 32:33], T.fc[:, 33:34]
+    cpf, half2, pf2, n8, n8b = T.fc[:, 20:22], T.fc[:, 22:23], T.fc[:, 30:31], T.fc[:, 32:33], T.fc[:, 33:34]
     lo, hi, half1 = T.fc[:, 36:37], T.fc[:, 37:38], T.fc[:, 38:39]
-    c8, c17, c64 = T.cj[:, 0:32], T.cj[:, 32:66], T.cj[:, 96:352]
+    c8, c17, xlf = T.cj[:, 0:32], T.cj[:, 32:66], T.cj[:, 72:88]
     eqt, gt, el = [T.qa[:, 32 * k:32 * k + 32] for k in range(3)]
-    k4, ps, kn, eq, v4, sc8 = [T.qb[:, 32 * k:32 * k + 32] for k in range(6)]
+    eq, v4, sc8 = [T.qb[:, 32 * k:32 * k + 32] for k in range(3)]
+    psn, nf, kn, ns = [T.pn[:, 8 * k:8 * k + 8] for k in range(4)]
 
     dma("a", "dx", T.xt[:, 0:64], T.x[:], "", "xt")
     for k in range(8):
@@ -238,49 +240,57 @@ def rank_program(g, core, T, topo):
     iota(T.fc[:, 8:16], "k16", [[16, 8]])
     iota(T.c16[:], "c16", [[0, 16], [1, 16]])
     iota(T.fc[:, 24:26], "lgf", [[128, 2]], 16, 1)
-    iota(pf2, "pf2", [[0, 2]], 0, 1)
+    iota(T.fc[:, 28:30], "lgf", [[128, 2]], 0, 1)
+    iota(pf2, "pf2", [[0, 1]], 0, 1)
 
     V("set", "xtz", "", T.xt[:, 64:512], 0.0)
     V("set", "one", "", T.one[:], 1.0)
-    V("set", "flg", "", T.flg[:], 0.0)
+    V("set", "fla", "", T.fla[:], -200.0)
 
+    for a in range(0, 1024, 448):
+        w = min(448, 1024 - a)
+        S(Copy, "flb%d" % (a // 448), "xtz", T.flb[:, a:a + w], T.xt[:, 64:64 + w])
     for k in range(4):
         S(Copy, "rs1", "one", T.rs[:, P * k:P * k + P], T.one[:])
     S(Copy, "rs", "rs1 xtz", T.rs[:, 0:512:128], T.xt[:, 64:68])
-    S(Sign, "r16", "c16", T.r16[:], T.c16[:])
-    S(Copy, "xuz", "xtz", T.xu[:, 0:448], T.xt[:, 64:512])
 
     V("qz", "xc xs", "xt xtz", T.xc[:], T.xs[:], T.xt[:])
     send([(u8(T.xc[:, 0:16]), [u8(T.rpc[:])] * 2, ids_r[0:2], e_h[0], "r_pt")], "xc")
     send([(T.xs[:, 0:16], [T.rps[:]] * 2, ids_r[2:4], e_h[1], "r_pt")], "xs")
     iota(T.idx[:, 0:256], "idx", [[1, 256]])
+    iota(xlf, "xlf", [[1, 2], [2, 8]])
 
     V("copy", "cdu", "cdi", T.cdu[:, 0:32:2], T.cdi[:])
     for i in range(A):
-        V("copy", "flg", "cdu one", T.flg[:].indirect(T.cdu[:, 2 * i:2 * i + 1]), T.one[:, 0:16])
+        f = "flb" if i % 2 else "fla"
+        V("copy", f, "cdu one flb0 flb1 flb2" if i % 2 else "cdu one", T[f][:].indirect(T.cdu[:, 2 * i:2 * i + 1]), T.one[:, 0:16])
         if i == 0:
             V("ts", "ti", "pin", ti, pin, 15, None, op_.bitwise_and)
-        elif i == 1:
+        elif i == 3:
             V("copy", "tf", "ti", T.fc[:, 34:36], ti)
-        elif i == 2:
+        elif i == 6:
             V("ts", "sk", "k16 tf", T.fc[:, 0:8], T.fc[:, 8:16], T.fc[:, 34:35], None, op_.add)
     S(Ident, "half2", "sk", half2, sk[2], bias=0.5)
     S(Ident, "half1", "sk", half1, sk[1], bias=0.5)
     S(Copy, "n8", "sk", n8, tf, scale=-0.125)
     S(Copy, "lhc", "sk", T.fc[:, 39:40], tf, scale=-1.0)
-    S(Ident, "hi", "sk", hi, tf, bias=-7.5)
+    S(Abs, "wm", "c16 sk", T.wm[:], T.c16[:], bias=tf, scale=-1.0)
     S(Ident, "n8b", "n8", n8b, n8, bias=273.0)
     S(Ident, "lo", "lhc", lo, T.fc[:, 39:40], bias=7.5)
-    S(Ident, "lgf", "pf2 n8", T.fc[:, 26:28], pf2, bias=n8, scale=0.125)
-    S(Ident, "lgf", "pf2 n8b", T.fc[:, 28:30], pf2, bias=n8b, scale=0.125)
+    S(Ident, "lgf", "pf2 n8", T.fc[:, 26:27], pf2, bias=n8, scale=0.125)
+    S(Relu, "wm", "wm", T.wm[:], T.wm[:], bias=1.0, scale=-1.0)
 
     def lists(qs, base, name, out, more):
         n = len(qs)
         h0 = base // P
         nk = [n, n - more]
         todo = [(x, half2, h0 + x) for x in range(n)] + [(x, half1, h0 + 4 + x) for x in range(n - more, n)]
-        for x, q in enumerate(qs):
-            V("scan", "inc%d" % q, "flg one", T.inc[:, P * q:P * q + P], T.one[:], T.flg[:, P * q:P * q + P], 0.0, op_.mult, op_.add)
+        for q in qs:
+            V("scan", "mrg%d" % q, "fla flb", T.mrg[:, P * q:P * q + P], T.fla[:, P * q:P * q + P], T.flb[:, P * q:P * q + P], 0.0, op_.add, op_.max)
+        for q in qs:
+            V("ts", "nam%d" % q, "mrg%d" % q, T.nam[:, P * q:P * q + P], T.mrg[:, P * q:P * q + P], 0.5, None, op_.is_ge)
+        for q in qs:
+            V("scan", "inc%d" % q, "nam%d one" % q, T.inc[:, P * q:P * q + P], T.one[:], T.nam[:, P * q:P * q + P], 0.0, op_.mult, op_.add)
         for y, (x, half, col) in enumerate(todo):
             b = P * (y % 4)
             S(Sign, "sgo%d sga%s" % (y % 4, name), "inc%d half1 half2" % qs[x], T.sgo[:, b:b + P - 1], T.inc[:, P * qs[x]:P * qs[x] + P - 1],
@@ -293,30 +303,29 @@ def rank_program(g, core, T, topo):
             a, e = base + P * n * k, base + P * (n * k + nk[k])
             V("scan", "cs" + name, "rs le" + name, T.cs[:, a:e], T.rs[:, 0:P * nk[k]], T.le[:, a:e], 0.0, op_.mult, op_.add)
         V("ts", name, "sga" + name, out[:, 2:3 * n:3], T.sga[:, h0:h0 + n], 0.5, 0.5 * (P - 1), op_.mult, op_.add)
-        if more:
-            V("ts", name, "sga" + name, out[:, 3 * (n - more) + 1:3 * n:3], T.sga[:, h0 + 4 + n - more:h0 + 4 + n], 0.5, 0.5 * (P - 1), op_.mult, op_.add)
+        V("ts", name, "sga" + name, out[:, 3 * (n - more) + 1:3 * n:3], T.sga[:, h0 + 4 + n - more:h0 + 4 + n], 0.5, 0.5 * (P - 1), op_.mult, op_.add)
         for k in range(2):
             V("copy", name, "cs" + name, out[:, k:3 * nk[k]:3], T.cs[:, base + P * n * k + P - 2:base + P * (n * k + nk[k]):P])
 
     lists(cross, 0, "rq", T.rq, 2)
     send([(T.rq[:, 6 * h:6 * h + 6], [T.rqr[:]], [ids_r[h]], e_h[h], "r_rq") for h in range(2)], "rq")
-    lists(same, 1024, "rqx", T.rqx, 0)
+    lists(same, 1024, "rqx", T.rqx, 1)
     send([(T.rqx[:, 3 * y:3 * y + 3], [T.rql[:, 3 * at_s[y]:3 * at_s[y] + 3]], [ids_s[y]], e_s[y], "a_rqs") for y in range(3)], "rqx")
 
     V("qz", "tbc tbs", "tbt", T.tbc[:], T.tbs[:], T.tbt[:])
     for x, q in enumerate(peers):
         S(Ident, "loc", "inc%d" % q, T.loc[:, 1 + P * q:1 + P * q + P], T.inc[:, P * q:P * q + P], bias=float(P + LC * x - 1))
+    S(Ident, "loc", "idx", T.loc[:, 1 + P * r:1 + P * r + P], T.idx[:, 0:P], bias=0.0)
+    S(Sign, "r16", "c16", T.r16[:], T.c16[:])
+    S(Ident, "lgf", "pf2 n8b", T.fc[:, 27:28], pf2, bias=n8b, scale=0.125)
     V("set", "locz", "", T.loc[:, 0:1], float(WCOLS))
     V("set", "locy", "", T.loc[:, 1025:1040], float(WCOLS))
-    V("ts", "oi", "pin", oi, pin, 31, None, op_.bitwise_and)
     V("ts", "o7", "pin", o7, pin, 7, None, op_.bitwise_and)
     V("ts", "cdk", "cdi", T.cdk[:, 0:8], T.cdi[:, 0:16:2], 1.0, None, op_.add)
     V("ts", "cdk", "cdi", T.cdk[:, 8:16], T.cdi[:, 1:16:2], 1.0, None, op_.add)
     V("copy", "cpf", "cpi", cpf, T.cpi[:])
     V("copy", "cpu", "cpi", T.cpu[:], T.cpi[:])
-    V("copy", "lgs", "lgf", T.lgs[:], T.fc[:, 24:30])
-    V("ts", "low2", "oi", T.low2[:, 0:1], oi1, 0.0, None, op_.add)
-    V("ts", "low2", "oi", T.low2[:, 1:2], oi1, 32.0, None, op_.add)
+    V("copy", "xl", "xlf", T.xl[:], xlf)
     V("ts", "lrep", "o7", T.lrep[:], o7, 0.0, None, op_.add)
 
     tot["a_rqc"] = 4 * noff // 2
@@ -337,37 +346,26 @@ def rank_program(g, core, T, topo):
     iota(T.c4[:], "c4", [[1, 4], [0, 8]], 1)
     send([(u8(T.xc[:, 0:16]), [u8(T.pwc[:, 16 * r:16 * r + 16])] * 3, ids_s, eoff, "a_pt")], "xc")
     send([(T.xs[:, 0:16], [T.pws[:, 16 * r:16 * r + 16]] * 3, ids_s, eoff, "a_pt")], "xs")
-    iota(c64, "c64", [[0, 4], [1, 64]])
     do("g", lambda q: q.affine_select(T.hid[:], T.one[:], [[-1, 128]], op_.is_equal, 0.0, 0, 1), ["one"], ["hid"])
     iota(T.val[:], "val", [[16, 8], [0, 4], [1, 16]])
 
-    S(Ident, "loc", "idx", T.loc[:, 1 + P * r:1 + P * r + P], T.idx[:, 0:P], bias=0.0)
-    S(Abs, "wm", "c16 sk", T.wm[:], T.c16[:], bias=tf, scale=-1.0)
+    S(Copy, "xuz", "xtz", T.xu[:, 0:448], T.xt[:, 64:512])
+    S(Copy, "xrs", "xs xl", T.xrs[:], T.xs[:].indirect(T.xl[:]))
     for k in range(1, 4):
         S(Ident, "idxs", "idx", T.idx[:, 256 * k:256 * k + 256], T.idx[:, 0:256], bias=float(256 * k))
     S(Ident, "idxs", "idx", T.idx[:, 1024:1040], T.idx[:, 0:16], bias=1024.0)
-    S(Relu, "wm", "wm", T.wm[:], T.wm[:], bias=1.0, scale=-1.0)
-    S(Sign, "lh", "lo hi", T.fc[:, 36:38], T.fc[:, 36:38])
-    S(Copy, "bsw", "c16", T.bsw[:, 0:34:17], T.c16[:, 0:2])
-    S(Relu, "lh", "lh", T.fc[:, 36:38], T.fc[:, 36:38])
-    S(Copy, "fv0", "c16", T.fv[:, 0:1], T.c16[:, 0:1])
-    S(Ident, "zt1", "idx lh", T.zt[:, 0:256], T.idx[:, 0:256], scale=lo)
-    S(Ident, "zt2", "idx lh", T.zt[:, 256:512], T.idx[:, 0:256], scale=hi)
-    S(Sign, "r17", "c17", T.r17[:], c17)
-    S(Sign, "r8", "c8", T.r8[:], c8)
-    S(Copy, "r17", "r17", T.r17[:], T.r17[:], scale=2.0)
     V("qz", "wco wso", "tbt", T.wc[:, 0:P], T.ws[:, 0:P], T.tbt[:])
-    V("copy", "posr", "loc locz locy cdk", T.posr[:], T.loc[:].indirect(T.cdk[:]))
     V("qz", "kcx ksx", "xt xtz", T.kc[:, 0:P], T.ks[:, 0:P], T.xt[:])
-    V("tt", "posm", "posr wm", T.posm[:], T.posr[:], T.wm[:], op_.mult)
+    V("tt", "posm", "loc locz locy cdk wm", T.posm[:], T.loc[:].indirect(T.cdk[:]), T.wm[:], op_.mult)
     V("qz", "kcx ksx", "xu xuz", T.kc[:, 160:288], T.ks[:, 160:288], T.xu[:])
     V("scan", "posc", "posm r16", T.posc[:], T.r16[:], T.posm[:], 0.0, op_.mult, op_.add)
-    V("copy", "nr", "idx idxs cpu", T.nr[:], T.idx[:].indirect(T.cpu[:]))
+    V("copy", "lgs", "lgf", T.lgs[:], T.fc[:, 24:30])
     V("copy", "kpl", "posc", T.kpl[:], T.posc[:, 15:256:16])
+    V("copy", "xrc", "xc xl", u32(T.xrc[:]), u32(T.xc[:]).indirect(T.xl[:]))
+    V("copy", "nr", "idx idxs cpu", T.nr[:], T.idx[:].indirect(T.cpu[:]))
+    V("qz", "wqc wqs", "wt", T.wqc[:], T.wqs[:], T.wt[:])
     for j in range(2):
         V("ts", "lw%d" % j, "nr cpf", T.lw[:, 16 * j:16 * j + 16], T.nr[:, 16 * j:16 * j + 16], T.fc[:, 20 + j:21 + j], None, op_.is_lt)
-        S(Ident, "nrz%d" % j, "nr lh", T.nrz[:, 16 * j:16 * j + 16], T.nr[:, 16 * j:16 * j + 16], bias=[lo, hi][j], scale=[lo, hi][j])
-    V("qz", "wqc wqs", "wt", T.wqc[:], T.wqs[:], T.wt[:])
     V("qz", "fwo fso", "tbt", T.fwc[:, 0:P], T.fws[:, 0:P], T.tbt[:])
 
     tot["a_dt"] = 4 * noff + sum(len(e_s[f]) + len(e_s2[f]) for f in from_s)
@@ -376,21 +374,36 @@ def rank_program(g, core, T, topo):
         a = 16 + P * j
         S(Copy, "ks%d" % j, "wso wca kpl ksx", T.ks[:, a:a + P], T.ws[:, 0:WCOLS].indirect(T.kpl[:, 8 * j:8 * j + 8]))
         V("copy", "kc%d" % j, "wco wca kpl kcx", u32(T.kc[:, a:a + P]), u32(T.wc[:, 0:WCOLS]).indirect(T.kpl[:, 8 * j:8 * j + 8]))
-    mm(T.pg0[:, 0:144], T.kc[:, 16:144], T.ks[:, 16:144], T.kc[:, 0:144], T.ks[:, 0:144], True, True, "kc0 ks0 kcx ksx", "pg0")
-    mm(T.pg1[:, 0:144], T.kc[:, 144:272], T.ks[:, 144:272], T.kc[:, 144:288], T.ks[:, 144:288], True, True, "kc1 ks1 kcx ksx", "pg1")
+    for j in range(2):
+        a, c = 16 + P * j, 144 * j
+        mm(T["pg%d" % j][:, 0:144], T.kc[:, a:a + P], T.ks[:, a:a + P], T.kc[:, c:c + 144], T.ks[:, c:c + 144], True, True,
+           "kc%d ks%d kcx ksx" % (j, j), "pg%d" % j)
+        mm(T["pd%d" % j][:, 0:P], T.xrc[:, P * j:P * j + P], T.xrs[:, P * j:P * j + P], T.kc[:, a:a + P], T.ks[:, a:a + P], True, True,
+           "kc%d ks%d xrc xrs" % (j, j), "pd%d" % j)
     mm(T.pz[:, 0:WCOLS], T.wqc[:], T.wqs[:], T.wc[:, 0:WCOLS], T.ws[:, 0:WCOLS], True, True, "wqc wqs wco wso wca", "pz")
+    S(Ident, "hi", "sk", hi, tf, bias=-7.5)
+    S(Copy, "bsw", "c16", T.bsw[:, 0:34:17], T.c16[:, 0:2])
+    S(Copy, "fv0", "c16", T.fv[:, 0:1], T.c16[:, 0:1])
+    S(Sign, "lh", "lo hi", T.fc[:, 36:38], T.fc[:, 36:38])
+    S(Sign, "r17", "c17", T.r17[:], c17)
+    S(Sign, "r8", "c8", T.r8[:], c8)
+    S(Relu, "lh", "lh", T.fc[:, 36:38], T.fc[:, 36:38])
+    S(Copy, "r17", "r17", T.r17[:], T.r17[:], scale=2.0)
     V("copy", "pb0", "pg0", T.pb[:, 0:144], T.pg0[:, 0:144])
     S(Copy, "pb1", "pg1", T.pb[:, 144:288], T.pg1[:, 0:144])
+    V("copy", "pbx0", "pd0", T.pbx[:, 0:P], T.pd0[:, 0:P])
+    S(Copy, "pbx1", "pd1", T.pbx[:, P:2 * P], T.pd1[:, 0:P])
+    for j in range(2):
+        S(Ident, "nrz%d" % j, "nr lh", T.nrz[:, 16 * j:16 * j + 16], T.nr[:, 16 * j:16 * j + 16], bias=[lo, hi][j], scale=[lo, hi][j])
+    S(Ident, "zt1", "idx lh", T.zt[:, 0:256], T.idx[:, 0:256], scale=lo)
+    S(Ident, "zt2", "idx lh", T.zt[:, 256:512], T.idx[:, 0:256], scale=hi)
     S(Copy, "zb", "pz", T.zb[:, 0:WCOLS], T.pz[:, 0:WCOLS])
     S(Sign, "lm", "c16 sk", T.lm[:], T.c16[:, 0:64], bias=tf, scale=-1.0)
     S(Ident, "trs", "sk", T.fc[:, 16:20], T.fc[:, 0:4], bias=1032.0, scale=8.0)
-    S(Relu, "lm", "lm", T.lm[:], T.lm[:])
-    S(Sign, "r64", "c64", T.r64[:], c64)
-    V("copy", "gs", "pb0 pb1 lgs", T.gs[:], T.pb[:].indirect(T.lgs[:, 2:6]))
-    V("tr", "tr", "gs", T.tr[:], T.gs[:])
-    V("tt", "ge2", "pb0 pb1 lgs gs", T.ge2[:], T.pb[:].indirect(T.lgs[:, 0:2]), T.gs[:, 16:48], op_.is_ge)
-    V("tt", "eqt", "tr low2 gs", eqt, T.tr[:].indirect(T.low2[:]), T.gs[:, 16:48], op_.is_equal)
-    V("tt", "gt", "tr low2 gs", gt, T.tr[:].indirect(T.low2[:]), T.gs[:, 16:48], op_.is_gt)
+    V("copy", "gs", "pb0 pb1 lgs", T.gs[:], T.pb[:].indirect(T.lgs[:, 2:4]))
+    V("tt", "eqt", "pbx0 pbx1 lgs gs", eqt, T.pbx[:].indirect(T.lgs[:, 4:6]), T.gs[:], op_.is_equal)
+    V("tt", "gt", "pbx0 pbx1 lgs gs", gt, T.pbx[:].indirect(T.lgs[:, 4:6]), T.gs[:], op_.is_gt)
+    V("tt", "ge2", "pb0 pb1 lgs gs", T.ge2[:], T.pb[:].indirect(T.lgs[:, 0:2]), T.gs[:], op_.is_ge)
     V("tt", "el", "eqt lw0 lw1", el, eqt, T.lw[:], op_.mult)
     for j in range(2):
         a = 16 * j
@@ -399,7 +412,7 @@ def rank_program(g, core, T, topo):
     V("copy", "bsw", "ge2 rku", T.bsw[:].indirect(T.rku[:]), T.ge2[:])
     V("copy", "nsw", "nrz0 nrz1 rku", T.nsw[:].indirect(T.rku[:]), T.nrz[:])
     V("scan", "pk", "bsw r17", T.pk[:], T.r17[:], T.bsw[:, 0:34], 0.0, op_.mult, op_.add)
-    V("tt", "ns", "nsw", T.ns[:], T.nsw[:, 1:9], T.nsw[:, 18:26], op_.add)
+    V("tt", "ns", "nsw", ns, T.nsw[:, 1:9], T.nsw[:, 18:26], op_.add)
     V("copy", "pku", "pk", T.pku[:], T.pk[:, 8:26:17])
     V("copy", "own", "zt1 zt2 pku", T.own[:], T.zt[:].indirect(T.pku[:]))
     V("copy", "msw", "own rku", T.msw[:].indirect(T.rku[:]), T.own[:])
@@ -414,16 +427,15 @@ def rank_program(g, core, T, topo):
 
     def far(m):
         a = m + 3
-        V("ts", "tmp%d" % m, "ui%d fv%d" % (m, m), T.tmp[:, 8 * m - 8 + a:8 * m], T.ui[:, 8 * m + a:8 * m + 8], T.fv[:, m:m + 1], None, op_.subtract)
+        V("ts", "tmp%d" % m, "ui%d fv%d" % (m, m), T.pn[:, 24 + 8 * m + a:32 + 8 * m], T.ui[:, 8 * m + a:8 * m + 8], T.fv[:, m:m + 1], None, op_.subtract)
 
     def far2(m):
         a = m + 3
         k = " ".join("fv%d" % j for j in range(a, 8))
-        V("tt", k, "tmp%d " % m + k, T.fv[:, a:8], T.fv[:, a:8], T.tmp[:, 8 * m - 8 + a:8 * m], op_.max)
+        V("tt", k, "tmp%d " % m + k, T.fv[:, a:8], T.fv[:, a:8], T.pn[:, 24 + 8 * m + a:32 + 8 * m], op_.max)
 
-    plane(0)
+    V("ts", "fv1 fv2 fv3 fv4 fv5 fv6 fv7", "ms", T.fv[:, 1:8], T.ms[:, 1:8], 128.0, None, op_.is_ge)
     plane(1)
-    V("copy", "fv1 fv2 fv3 fv4 fv5 fv6 fv7", "ui0", T.fv[:, 1:8], T.ui[:, 1:8])
     plane(2)
     pair(1, 2)
     pair(1, 3)
@@ -442,18 +454,20 @@ def rank_program(g, core, T, topo):
         for j in range(m + 1, 8):
             if (m, j) != (3, 4):
                 pair(m, j)
-    V("ts", "k4", "fv0 fv1 fv2 fv3 fv4 fv5 fv6 fv7 lrep", k4, T.fv[:].indirect(T.lrep[:]), 0.0, None, op_.is_equal)
-    V("scan", "ps", "k4 r8", ps, T.r8[:], k4, 0.0, op_.mult, op_.add)
-    V("tt", "kn", "ns k4 lrep", kn, T.ns[:].indirect(T.lrep[:]), k4, op_.mult)
-    V("tt", "eq", "ps c4", eq, ps, T.c4[:], op_.is_equal)
-    V("tt", "v4", "eq kn", v4, eq, kn, op_.mult)
+    fvs = "fv0 fv1 fv2 fv3 fv4 fv5 fv6 fv7"
+    V("ts", "nf", fvs, nf, T.fv[:], 0.0, None, op_.is_equal)
+    V("scan", "psn", fvs + " one", psn, T.one[:, 0:8], T.fv[:], 0.0, op_.add, op_.subtract)
+    V("tt", "kn", "ns nf", kn, ns, nf, op_.mult)
+    V("tt", "eq", "psn c4 lrep", eq, psn.indirect(T.lrep[:]), T.c4[:], op_.is_equal)
+    V("tt", "v4", "eq kn lrep", v4, kn.indirect(T.lrep[:]), eq, op_.mult)
     V("scan", "sc8", "v4 r8", sc8, T.r8[:], v4, 0.0, op_.mult, op_.add)
-    V("copy", "klu", "sc8", T.klu[:], T.qb[:, 167:192:8])
+    V("copy", "klu", "sc8", T.klu[:], T.qb[:, 71:96:8])
     for a in range(0, 2048, 448):
         w = min(448, 2048 - a)
         S(Copy, "ebz", "xtz", T.ebt[:, a:a + w], T.xt[:, 64:64 + w])
     for b in range(4):
         S(Copy, "ebt", "hid ebz", T.ebt[:, 512 * b + b:512 * b + 512:4], T.hid[:], scale=0.5)
+    S(Relu, "lm", "lm", T.lm[:], T.lm[:])
     for k in range(8):
         dma("s" if k % 2 == 0 else "a", "drep", T.kru[16 * k:16 * k + 16, :], T.klu[0:128:8, :], "klu", "kru")
     dma("s", "dkx", u8(T.pwc[:, 16 * r:16 * r + 16]), u8(T.xc[:, 0:16]), "xc", "pwo")
@@ -470,10 +484,10 @@ def rank_program(g, core, T, topo):
     V("copy", "kr", "kru", T.kr[:], T.kru[:])
     V("tt", "rwm", "idx idxs kru lm", T.rwm[:], T.idx[:].indirect(T.kru[:]), T.lm[:], op_.mult)
     for k in range(4):
-        V("ts", "eqd", "rwm kr trs", T.eqd[:, 64 * k:64 * k + 64], T.rwm[:], T.kr[:, k:k + 1], trs[k], op_.is_equal, op_.mult)
-    V("scan", "scd", "eqd r64", T.scd[:], T.r64[:], T.eqd[:], 0.0, op_.mult, op_.max)
-    V("tt", "lf", "scd kr", T.lf[:], T.scd[:, 63:256:64], T.kr[:], op_.max)
-    V("copy", "lu", "lf", T.lu[:], T.lf[:])
+        V("ts", "eqd%d" % k, "rwm kr trs", T.eqd[:, 64 * k:64 * k + 64], T.rwm[:], T.kr[:, k:k + 1], trs[k], op_.is_equal, op_.mult)
+    for k in range(4):
+        V("scan", "scf%d" % k, "eqd%d kr one" % k, T.scf[:, 64 * k:64 * k + 64], T.one[:, 0:64], T.eqd[:, 64 * k:64 * k + 64], T.kr[:, k:k + 1], op_.mult, op_.max)
+    V("copy", "lu", "scf0 scf1 scf2 scf3", T.lu[:], T.scf[:, 63:256:64])
     send([(T.lu[:], [T.lr[:]] * 2, ids_r[0:2], eon, "r_kl")], "lu")
     send([(T.lu[:], [T.ll[:, 4 * at_s[y]:4 * at_s[y] + 4]], [ids_s[y]], e_s[y], "a_kls") for y in range(3)], "lu")
 

from concourse.bass import DstId, RemoteDMATransfer
from concourse.mybir import dt, AluOpType, ActivationFunctionType

N, P, A, LC = 8, 128, 16, 48
F32, BF, I32, U16, U8, X4 = "float32", "bfloat16", "int32", "uint16", "uint8", "float8_e4m3fn_x4"
WCOLS = P + 7 * LC
SCRATCH = {}


def _sb(name, n, d):
    SCRATCH[name] = ("sbuf", [128, n], d)


for _n, _w, _d in [
    ("cdi", 16, I32), ("cpi", 2, I32), ("tbt", 512, BF), ("xt", 512, BF), ("xu", 512, BF), ("wt", 512, BF),
    ("cdu", 32, U16), ("fla", 1024, BF), ("flb", 1024, BF), ("mrg", 1024, BF), ("nam", 1024, BF), ("one", 128, BF),
    ("inc", 1024, BF), ("le", 1792, BF), ("cs", 1792, BF), ("rs", 512, BF),
    ("sgo", 512, BF), ("sga", 16, F32), ("rq", 12, U16), ("rqx", 10, U16), ("rqr", 6, U16), ("rql", 22, U16),
    ("tbc", 128, X4), ("tbs", 128, U8), ("wc", 480, X4), ("ws", 480, U8), ("fwc", 256, X4), ("fws", 256, U8),
    ("xc", 128, X4), ("xs", 128, U8), ("wqc", 128, X4), ("wqs", 128, U8), ("pwc", 128, X4), ("pws", 128, U8),
    ("xrc", 256, X4), ("xrs", 256, U8),
    ("dcc", 192, X4), ("dcs", 192, U8), ("dsc", 144, X4), ("dss", 144, U8), ("rlc", 96, X4), ("rls", 96, U8),
    ("rpc", 16, X4), ("rps", 16, U8), ("kc", 288, X4), ("ks", 288, U8), ("ppc", 128, X4), ("pps", 128, U8),
    ("foc", 128, X4), ("fos", 128, U8), ("ebt", 2048, BF), ("ec", 512, X4), ("es", 512, U8),
    ("ii", 8, I32), ("fc", 40, F32), ("cj", 96, F32), ("idx", 1040, F32), ("c16", 256, F32), ("wm", 256, F32), ("wmb", 128, BF),
    ("r16", 256, F32), ("r16b", 128, BF), ("lm", 64, F32), ("r17", 34, F32), ("r8", 32, F32), ("c4", 32, F32),
    ("zt", 512, F32), ("nrz", 32, F32), ("hid", 128, BF), ("val", 512, BF), ("lgs", 6, U16), ("lrep", 2, U16), ("xl", 16, U16),
    ("loc", 1040, F32), ("cdk", 16, U16), ("posm", 256, F32), ("posc", 256, F32), ("kpl", 16, U16),
    ("cpu", 2, U16), ("nr", 32, F32), ("lw", 32, F32),
    ("pb", 288, F32), ("pbx", 256, F32), ("gs", 32, F32), ("qa", 128, F32), ("rku", 2, U16), ("ge2", 32, F32),
    ("bsw", 40, F32), ("pk", 34, F32), ("pku", 2, U16), ("own", 32, F32), ("msw", 40, I32), ("ms", 8, I32), ("nsw", 40, F32),
    ("ui", 56, I32), ("fv", 8, F32), ("pn", 48, F32), ("qb", 96, F32), ("klu", 4, U16),
    ("kr", 4, F32), ("kru", 4, U16), ("rwm", 64, F32), ("eqd", 256, BF), ("scf", 256, F32),
    ("lu", 4, U16), ("lr", 4, U16), ("ll", 28, U16), ("kpf", 64, F32), ("locr", 192, F32), ("yl", 8, U16), ("zb", 480, F32), ("yb", 64, F32),
    ("wns", 1552, BF), ("wnc", 1552, BF), ("wno", 1552, BF), ("wsm", 512, BF), ("wl", 8, F32), ("wu", 8, U16), ("fl", 8, U16), ("nt", 512, BF),
]:
    _sb(_n, _w, _d)
for _n in ("pg0", "pg1", "pz", "pd0", "pd1", "pd2", "pd3"):
    SCRATCH[_n] = ("psum", [128, 512], F32)
SEMAPHORES = ["cv", "ca", "ct", "cg", "dcd", "dcp", "dtb", "dx", "dxu", "dw", "dkx", "drep", "dy", "dkp", "doc", "ls",
              "a_rqc", "a_rqs", "a_dt", "a_pt", "a_klc", "a_kls", "r_pt", "r_rq", "r_dt", "r_kl"]
PART = ("lerq", "lerqx", "csrq", "csrqx", "lgf", "lrep", "loc", "cdk", "yb", "ebz", "ebt", "rs1", "idxs",
        "rq", "rqx", "sgarq", "sgarqx")


def _bits(es):
    m = 0
    for e in es:
        m |= 1 << e
    return m


def _peers(topo, cores, r):
    cross = [q for q in range(N) if q != r and not topo.may_write(cores[r], cores[q])]
    same = [q for q in range(N) if q != r and topo.may_write(cores[r], cores[q])]
    return cross, same


def _relays(topo, cores, r):
    cross, _ = _peers(topo, cores, r)
    ok = [c for c in topo.cores_of(cores[r]) if c != cores[r] and topo.may_write(c, cores[cross[0]])]
    d0 = [c for c in ok if topo.die(c) == topo.die(cores[r])]
    d1 = [c for c in ok if topo.die(c) != topo.die(cores[r])]
    return cross, [d0[0], d1[0], d0[1], d1[1]]


def _dst(topo, d, s):
    rid, pid = topo.addr(d, s)
    return DstId(rid=rid, pnc=pid)


def _same_engines(es):
    return [es[0:4], es[4:6], es[6:8]], [es[0:2], es[2:4], es[4:8]]


def _relay_program(g, core, T, topo, cores, r, x):
    cross, _ = _peers(topo, cores, r)
    h = x % 2
    pair = cross[2 * h:2 * h + 2]
    ids = [_dst(topo, cores[q], core) for q in pair]
    es = topo.engines(core, cores[pair[0]])
    half = [es[0:4], es[4:8]]
    at = [_peers(topo, cores, q)[0].index(r) for q in pair]
    n = [0]

    def fwd(ts):
        out = []
        for src, dsts, to, e, sem in ts:
            out.append(RemoteDMATransfer(dst_ids=to, dma_engine_mask=_bits(e), remote_sem=T.sem[sem], srcs=[src], dsts=dsts))
            n[0] += len(e)
        g.remote_dma_fused(out, local_sem=T.sem.ls)

    non = len(topo.engines(cores[r], core))
    a = 16 * r
    w = [P + LC * at[0], P + LC * at[1]]
    g.wait_ge(T.sem.r_pt, non // 2)
    if x < 2:
        fwd([(T.rpc[:].bitcast(dt.uint8), [T.pwc[:, a:a + 16].bitcast(dt.uint8)] * 2, ids, es, "a_pt")])
        g.wait_ge(T.sem.r_rq, non // 2)
        fwd([(T.rqr[:, 3 * k:3 * k + 3], [T.rql[:, 3 * at[k]:3 * at[k] + 3]], [ids[k]], half[k], "a_rqc") for k in range(2)])
        g.wait_ge(T.sem.r_dt, non // 2)
        fwd([(T.rlc[:, LC * k:LC * k + LC].bitcast(dt.uint8), [T.wc[:, w[k]:w[k] + LC].bitcast(dt.uint8)], [ids[k]], half[k], "a_dt") for k in range(2)])
        g.wait_ge(T.sem.r_kl, non)
        fwd([(T.lr[:], [T.ll[:, 4 * at[k]:4 * at[k] + 4]], [ids[k]], half[k], "a_klc") for k in range(2)])
    else:
        fwd([(T.rps[:], [T.pws[:, a:a + 16]] * 2, ids, es, "a_pt")])
        g.wait_ge(T.sem.r_dt, non // 2)
        fwd([(T.rls[:, LC * k:LC * k + LC], [T.ws[:, w[k]:w[k] + LC]], [ids[k]], half[k], "a_dt") for k in range(2)])
    g.wait_ge(T.sem.ls, n[0])


def rank_program(g, core, T, topo):
    cores = T.cores
    r = T.rank_of(core)
    if r is None:
        for k in range(N):
            if cores[k] in topo.cores_of(core):
                _, rel = _relays(topo, cores, k)
                if core in rel:
                    _relay_program(g, core, T, topo, cores, k, rel.index(core))
        return

    op_ = AluOpType
    AF = ActivationFunctionType
    Copy, Sign, Ident, Abs, Relu = AF.Copy, AF.Sign, AF.Identity, AF.Abs, AF.Relu
    cross, rel = _relays(topo, cores, r)
    _, same = _peers(topo, cores, r)
    peers = cross + same

    eng = {"v": g.vector, "a": g.scalar, "t": g.tensor, "g": g, "s": g.sync}
    csem = {"v": "cv", "a": "ca", "t": "ct", "g": "cg"}
    tot, seen, wr_, rd_ = {}, {e: {} for e in eng}, {}, {}

    def need(e, toks):
        want = {}
        for s, c in toks:
            c = tot[s] if c is None else c
            want[s] = max(want.get(s, 0), c)
        for s in want:
            if seen[e].get(s, 0) < want[s]:
                eng[e].wait_ge(T.sem[s], want[s])
                seen[e][s] = want[s]

    def do(e, fn, rd, wr):
        mine = csem[e]
        toks = []
        for k in rd:
            toks += wr_.get(k, [])
        for k in wr:
            toks += [t for t in wr_.get(k, []) + rd_.get(k, []) if k not in PART or t[0] != mine]
        need(e, toks)
        fn(eng[e]).then_inc(T.sem[mine], 1)
        tot[mine] = tot.get(mine, 0) + 1
        tok = (mine, tot[mine])
        for k in wr:
            wr_[k] = [t for t in wr_.get(k, []) if t[0] != mine] + [tok] if k in PART else [tok]
            rd_[k] = []
        for k in rd:
            rd_[k] = [t for t in rd_.get(k, []) if t[0] != mine] + [tok]

    def V(name, wr, rd, *args):
        def fn(q):
            f = {"copy": q.tensor_copy, "tt": q.tensor_tensor, "ts": q.tensor_scalar, "set": q.memset,
                 "scan": q.tensor_tensor_scan, "qz": q.quantize_mx}[name]
            return f(*args)
        do("v", fn, rd.split(), wr.split())

    def S(f, wr, rd, out, in_, **k):
        do("a", lambda q: q.activation(out, in_, f, **k), rd.split(), wr.split())

    def iota(out, wr, pattern, base=0, cm=0):
        do("g", lambda q: q.iota(out, pattern, base, cm, allow_small_or_imprecise_dtypes=True), [], [wr])

    def dma(e, sem, out, in_, rd, wr):
        toks = []
        for k in rd.split():
            toks += wr_.get(k, [])
        for k in wr.split():
            toks += [t for t in wr_.get(k, []) + rd_.get(k, []) if t[0] != sem]
        need(e, toks)
        eng[e].dma_start(out, in_).then_inc(T.sem[sem], 16)
        tot[sem] = tot.get(sem, 0) + 16
        for k in wr.split():
            wr_[k] = [(sem, None)]
        for k in rd.split():
            rd_[k] = rd_.get(k, []) + [(sem, None)]

    def mm(out, l, ls, m, ms, start, stop, rd, wr):
        do("t", lambda q: q.matmul_mx(out, l, ls, m, ms, start, stop), rd.split(), wr.split())

    def u8(v):
        return v.bitcast(dt.uint8)

    def u32(v):
        return v.bitcast(dt.uint32)

    def send(transfers, rd):
        need("g", wr_.get(rd, []))
        ts = []
        for src, dsts, ids, es, sem in transfers:
            ts.append(RemoteDMATransfer(dst_ids=ids, dma_engine_mask=_bits(es), remote_sem=T.sem[sem], srcs=[src], dsts=dsts))
            tot["ls"] = tot.get("ls", 0) + len(es)
        g.remote_dma_fused(ts, local_sem=T.sem.ls)

    ids_r = [_dst(topo, c, core) for c in rel]
    ids_s = [_dst(topo, cores[q], core) for q in same]
    eon = topo.engines(core, rel[0])
    eoff = topo.engines(core, cores[same[0]])
    noff = len(eoff)
    e_h = [eon[0:len(eon) // 2], eon[len(eon) // 2:]]
    e_s, e_s2 = _same_engines(eoff)
    at_s = []
    from_s = []
    for q in same:
        cq, sq = _peers(topo, cores, q)
        at_s.append(4 + sq.index(r))
        from_s.append(sq.index(r))

    pin, ti, o7 = [T.ii[:, 2 * k:2 * k + 2] for k in range(3)]
    tf = T.fc[:, 0:1]
    sk = [T.fc[:, k:k + 1] for k in range(8)]
    trs = [T.fc[:, 16 + k:17 + k] for k in range(4)]
    cpf, half2, pf2, n8, n8b = T.fc[:, 20:22], T.fc[:, 22:23], T.fc[:, 30:31], T.fc[:, 32:33], T.fc[:, 33:34]
    lo, hi, half1 = T.fc[:, 36:37], T.fc[:, 37:38], T.fc[:, 38:39]
    c8, c17, xlf = T.cj[:, 0:32], T.cj[:, 32:66], T.cj[:, 72:88]
    eqt, gt, el = [T.qa[:, 32 * k:32 * k + 32] for k in range(3)]
    eq, v4, sc8 = [T.qb[:, 32 * k:32 * k + 32] for k in range(3)]
    psn, nf, kn, ns = [T.pn[:, 8 * k:8 * k + 8] for k in range(4)]

    dma("a", "dx", T.xt[:, 0:64], T.x[:], "", "xt")
    for k in range(8):
        dma("s" if k % 2 == 0 else "a", "dcd", T.cdi[16 * k:16 * k + 16, :], T.cd[:], "", "cdi")
    dma("s", "dtb", T.tbt[:], T.tb[:], "", "tbt")
    dma("s", "dxu", T.xu[:, 448:512], T.x[:], "", "xu")
    dma("s", "dw", T.wt[:], T.w[:], "", "wt")
    for k in range(8):
        dma("s", "dcp", T.cpi[16 * k:16 * k + 16, :], T.cd[:, 2 * k:2 * k + 2], "", "cpi")

    do("g", lambda q: q.iota(pin, [[0, 2]], 0, 1), [], ["pin"])
    iota(T.fc[:, 8:16], "k16", [[16, 8]])
    iota(T.c16[:], "c16", [[0, 16], [1, 16]])
    iota(T.fc[:, 24:26], "lgf", [[128, 2]], 16, 1)
    iota(T.fc[:, 28:30], "lgf", [[128, 2]], 0, 1)
    iota(pf2, "pf2", [[0, 1]], 0, 1)

    V("set", "xtz", "", T.xt[:, 64:512], 0.0)
    V("set", "one", "", T.one[:], 1.0)
    V("set", "fla", "", T.fla[:], -200.0)

    for a in range(0, 1024, 448):
        w = min(448, 1024 - a)
        S(Copy, "flb%d" % (a // 448), "xtz", T.flb[:, a:a + w], T.xt[:, 64:64 + w])
    for k in range(4):
        S(Copy, "rs1", "one", T.rs[:, P * k:P * k + P], T.one[:])
    S(Copy, "rs", "rs1 xtz", T.rs[:, 0:512:128], T.xt[:, 64:68])

    V("qz", "xc xs", "xt xtz", T.xc[:], T.xs[:], T.xt[:])
    send([(u8(T.xc[:, 0:16]), [u8(T.rpc[:])] * 2, ids_r[0:2], e_h[0], "r_pt")], "xc")
    send([(T.xs[:, 0:16], [T.rps[:]] * 2, ids_r[2:4], e_h[1], "r_pt")], "xs")
    iota(T.idx[:, 0:256], "idx", [[1, 256]])
    iota(xlf, "xlf", [[1, 2], [2, 8]])

    V("copy", "cdu", "cdi", T.cdu[:, 0:32:2], T.cdi[:])
    for i in range(A):
        f = "flb" if i % 2 else "fla"
        V("copy", f, "cdu one flb0 flb1 flb2" if i % 2 else "cdu one", T[f][:].indirect(T.cdu[:, 2 * i:2 * i + 1]), T.one[:, 0:16])
        if i == 0:
            V("ts", "ti", "pin", ti, pin, 15, None, op_.bitwise_and)
        elif i == 3:
            V("copy", "tf", "ti", T.fc[:, 34:36], ti)
        elif i == 6:
            V("ts", "sk", "k16 tf", T.fc[:, 0:8], T.fc[:, 8:16], T.fc[:, 34:35], None, op_.add)
    S(Ident, "half2", "sk", half2, sk[2], bias=0.5)
    S(Ident, "half1", "sk", half1, sk[1], bias=0.5)
    S(Copy, "n8", "sk", n8, tf, scale=-0.125)
    S(Copy, "lhc", "sk", T.fc[:, 39:40], tf, scale=-1.0)
    S(Abs, "wm", "c16 sk", T.wm[:], T.c16[:], bias=tf, scale=-1.0)
    S(Ident, "n8b", "n8", n8b, n8, bias=273.0)
    S(Ident, "lo", "lhc", lo, T.fc[:, 39:40], bias=7.5)
    S(Ident, "lgf", "pf2 n8", T.fc[:, 26:27], pf2, bias=n8, scale=0.125)
    S(Relu, "wm", "wm", T.wm[:], T.wm[:], bias=1.0, scale=-1.0)

    def lists(qs, base, name, out, more):
        n = len(qs)
        h0 = base // P
        nk = [n, n - more]
        todo = [(x, half2, h0 + x) for x in range(n)] + [(x, half1, h0 + 4 + x) for x in range(n - more, n)]
        for q in qs:
            V("scan", "mrg%d" % q, "fla flb", T.mrg[:, P * q:P * q + P], T.fla[:, P * q:P * q + P], T.flb[:, P * q:P * q + P], 0.0, op_.add, op_.max)
        for q in qs:
            V("ts", "nam%d" % q, "mrg%d" % q, T.nam[:, P * q:P * q + P], T.mrg[:, P * q:P * q + P], 0.5, None, op_.is_ge)
        for q in qs:
            V("scan", "inc%d" % q, "nam%d one" % q, T.inc[:, P * q:P * q + P], T.one[:], T.nam[:, P * q:P * q + P], 0.0, op_.mult, op_.add)
        for y, (x, half, col) in enumerate(todo):
            b = P * (y % 4)
            S(Sign, "sgo%d sga%s" % (y % 4, name), "inc%d half1 half2" % qs[x], T.sgo[:, b:b + P - 1], T.inc[:, P * qs[x]:P * qs[x] + P - 1],
              bias=half, scale=-1.0, accum_out=T.sga[:, col:col + 1])
        for k in range(2):
            for x in range(nk[k]):
                a = base + P * (n * k + x)
                V("ts", "le" + name, "inc%d sk" % qs[x], T.le[:, a:a + P], T.inc[:, P * qs[x]:P * qs[x] + P], sk[k], None, op_.is_le)
        for k in range(2):
            a, e = base + P * n * k, base + P * (n * k + nk[k])
            V("scan", "cs" + name, "rs le" + name, T.cs[:, a:e], T.rs[:, 0:P * nk[k]], T.le[:, a:e], 0.0, op_.mult, op_.add)
        V("ts", name, "sga" + name, out[:, 2:3 * n:3], T.sga[:, h0:h0 + n], 0.5, 0.5 * (P - 1), op_.mult, op_.add)
        V("ts", name, "sga" + name, out[:, 3 * (n - more) + 1:3 * n:3], T.sga[:, h0 + 4 + n - more:h0 + 4 + n], 0.5, 0.5 * (P - 1), op_.mult, op_.add)
        for k in range(2):
            V("copy", name, "cs" + name, out[:, k:3 * nk[k]:3], T.cs[:, base + P * n * k + P - 2:base + P * (n * k + nk[k]):P])

    lists(cross, 0, "rq", T.rq, 2)
    send([(T.rq[:, 6 * h:6 * h + 6], [T.rqr[:]], [ids_r[h]], e_h[h], "r_rq") for h in range(2)], "rq")
    lists(same, 1024, "rqx", T.rqx, 1)
    send([(T.rqx[:, 3 * y:3 * y + 3], [T.rql[:, 3 * at_s[y]:3 * at_s[y] + 3]], [ids_s[y]], e_s[y], "a_rqs") for y in range(3)], "rqx")

    V("qz", "tbc tbs", "tbt", T.tbc[:], T.tbs[:], T.tbt[:])
    for x, q in enumerate(peers):
        S(Ident, "loc", "inc%d" % q, T.loc[:, 1 + P * q:1 + P * q + P], T.inc[:, P * q:P * q + P], bias=float(P + LC * x - 1))
    S(Ident, "loc", "idx", T.loc[:, 1 + P * r:1 + P * r + P], T.idx[:, 0:P], bias=0.0)
    S(Sign, "r16", "c16", T.r16[:], T.c16[:])
    S(Ident, "lgf", "pf2 n8b", T.fc[:, 27:28], pf2, bias=n8b, scale=0.125)
    V("set", "locz", "", T.loc[:, 0:1], float(WCOLS))
    V("set", "locy", "", T.loc[:, 1025:1040], float(WCOLS))
    V("ts", "o7", "pin", o7, pin, 7, None, op_.bitwise_and)
    V("ts", "cdk", "cdi", T.cdk[:, 0:8], T.cdi[:, 0:16:2], 1.0, None, op_.add)
    V("ts", "cdk", "cdi", T.cdk[:, 8:16], T.cdi[:, 1:16:2], 1.0, None, op_.add)
    V("copy", "cpf", "cpi", cpf, T.cpi[:])
    V("copy", "cpu", "cpi", T.cpu[:], T.cpi[:])
    V("copy", "xl", "xlf", T.xl[:], xlf)
    V("ts", "lrep", "o7", T.lrep[:], o7, 0.0, None, op_.add)

    tot["a_rqc"] = 4 * noff // 2
    tot["a_rqs"] = sum(len(e_s[f]) for f in from_s)
    wr_["rqlc"] = [("a_rqc", tot["a_rqc"])]
    wr_["rqls"] = [("a_rqs", tot["a_rqs"])]
    S(Copy, "dcs", "tbs rqlc", T.dcs[:], T.tbs[:].indirect(T.rql[:, 0:12]))
    V("copy", "dcc", "tbc rqlc", u32(T.dcc[:]), u32(T.tbc[:]).indirect(T.rql[:, 0:12]))
    S(Copy, "dss", "tbs rqls", T.dss[:], T.tbs[:].indirect(T.rql[:, 12:21]))
    V("copy", "dsc", "tbc rqls", u32(T.dsc[:]), u32(T.tbc[:]).indirect(T.rql[:, 12:21]))
    send([(u8(T.dcc[:, 96 * h:96 * h + 96]), [u8(T.rlc[:])], [ids_r[h]], e_h[h], "r_dt") for h in range(2)], "dcc")
    send([(T.dcs[:, 96 * h:96 * h + 96], [T.rls[:]], [ids_r[2 + h]], e_h[h], "r_dt") for h in range(2)], "dcs")
    ws_ = [P + LC * at_s[y] for y in range(3)]
    send([(u8(T.dsc[:, LC * y:LC * y + LC]), [u8(T.wc[:, ws_[y]:ws_[y] + LC])], [ids_s[y]], e_s[y], "a_dt") for y in range(3)], "dsc")
    send([(T.dss[:, LC * y:LC * y + LC], [T.ws[:, ws_[y]:ws_[y] + LC]], [ids_s[y]], e_s2[y], "a_dt") for y in range(3)], "dss")
    iota(c17, "c17", [[0, 2], [1, 17]])
    iota(c8, "c8", [[0, 4], [1, 8]])
    iota(T.c4[:], "c4", [[1, 4], [0, 8]], 1)
    send([(u8(T.xc[:, 0:16]), [u8(T.pwc[:, 16 * r:16 * r + 16])] * 3, ids_s, eoff, "a_pt")], "xc")
    send([(T.xs[:, 0:16], [T.pws[:, 16 * r:16 * r + 16]] * 3, ids_s, eoff, "a_pt")], "xs")
    do("g", lambda q: q.affine_select(T.hid[:], T.one[:], [[-1, 128]], op_.is_equal, 0.0, 0, 1), ["one"], ["hid"])
    iota(T.val[:], "val", [[16, 8], [0, 4], [1, 16]])

    S(Copy, "xuz", "xtz", T.xu[:, 0:448], T.xt[:, 64:512])
    S(Copy, "xrs", "xs xl", T.xrs[:], T.xs[:].indirect(T.xl[:]))
    for k in range(1, 4):
        S(Ident, "idxs", "idx", T.idx[:, 256 * k:256 * k + 256], T.idx[:, 0:256], bias=float(256 * k))
    S(Ident, "idxs", "idx", T.idx[:, 1024:1040], T.idx[:, 0:16], bias=1024.0)
    V("qz", "wco wso", "tbt", T.wc[:, 0:P], T.ws[:, 0:P], T.tbt[:])
    V("qz", "kcx ksx", "xt xtz", T.kc[:, 0:P], T.ks[:, 0:P], T.xt[:])
    V("tt", "posm", "loc locz locy cdk wm", T.posm[:], T.loc[:].indirect(T.cdk[:]), T.wm[:], op_.mult)
    V("qz", "kcx ksx", "xu xuz", T.kc[:, 160:288], T.ks[:, 160:288], T.xu[:])
    V("scan", "posc", "posm r16", T.posc[:], T.r16[:], T.posm[:], 0.0, op_.mult, op_.add)
    V("copy", "lgs", "lgf", T.lgs[:], T.fc[:, 24:30])
    V("copy", "kpl", "posc", T.kpl[:], T.posc[:, 15:256:16])
    V("copy", "xrc", "xc xl", u32(T.xrc[:]), u32(T.xc[:]).indirect(T.xl[:]))
    V("copy", "nr", "idx idxs cpu", T.nr[:], T.idx[:].indirect(T.cpu[:]))
    V("qz", "wqc wqs", "wt", T.wqc[:], T.wqs[:], T.wt[:])
    for j in range(2):
        V("ts", "lw%d" % j, "nr cpf", T.lw[:, 16 * j:16 * j + 16], T.nr[:, 16 * j:16 * j + 16], T.fc[:, 20 + j:21 + j], None, op_.is_lt)
    V("qz", "fwo fso", "tbt", T.fwc[:, 0:P], T.fws[:, 0:P], T.tbt[:])

    tot["a_dt"] = 4 * noff + sum(len(e_s[f]) + len(e_s2[f]) for f in from_s)
    wr_["wca"] = [("a_dt", tot["a_dt"])]
    for j in range(2):
        a = 16 + P * j
        S(Copy, "ks%d" % j, "wso wca kpl ksx", T.ks[:, a:a + P], T.ws[:, 0:WCOLS].indirect(T.kpl[:, 8 * j:8 * j + 8]))
        V("copy", "kc%d" % j, "wco wca kpl kcx", u32(T.kc[:, a:a + P]), u32(T.wc[:, 0:WCOLS]).indirect(T.kpl[:, 8 * j:8 * j + 8]))
    for j in range(2):
        a, c = 16 + P * j, 144 * j
        mm(T["pg%d" % j][:, 0:144], T.kc[:, a:a + P], T.ks[:, a:a + P], T.kc[:, c:c + 144], T.ks[:, c:c + 144], True, True,
           "kc%d ks%d kcx ksx" % (j, j), "pg%d" % j)
        mm(T["pd%d" % j][:, 0:P], T.xrc[:, P * j:P * j + P], T.xrs[:, P * j:P * j + P], T.kc[:, a:a + P], T.ks[:, a:a + P], True, True,
           "kc%d ks%d xrc xrs" % (j, j), "pd%d" % j)
    mm(T.pz[:, 0:WCOLS], T.wqc[:], T.wqs[:], T.wc[:, 0:WCOLS], T.ws[:, 0:WCOLS], True, True, "wqc wqs wco wso wca", "pz")
    S(Ident, "hi", "sk", hi, tf, bias=-7.5)
    S(Copy, "bsw", "c16", T.bsw[:, 0:34:17], T.c16[:, 0:2])
    S(Copy, "fv0", "c16", T.fv[:, 0:1], T.c16[:, 0:1])
    S(Sign, "lh", "lo hi", T.fc[:, 36:38], T.fc[:, 36:38])
    S(Sign, "r17", "c17", T.r17[:], c17)
    S(Sign, "r8", "c8", T.r8[:], c8)
    S(Relu, "lh", "lh", T.fc[:, 36:38], T.fc[:, 36:38])
    S(Copy, "r17", "r17", T.r17[:], T.r17[:], scale=2.0)
    V("copy", "pb0", "pg0", T.pb[:, 0:144], T.pg0[:, 0:144])
    S(Copy, "pb1", "pg1", T.pb[:, 144:288], T.pg1[:, 0:144])
    V("copy", "pbx0", "pd0", T.pbx[:, 0:P], T.pd0[:, 0:P])
    S(Copy, "pbx1", "pd1", T.pbx[:, P:2 * P], T.pd1[:, 0:P])
    for j in range(2):
        S(Ident, "nrz%d" % j, "nr lh", T.nrz[:, 16 * j:16 * j + 16], T.nr[:, 16 * j:16 * j + 16], bias=[lo, hi][j], scale=[lo, hi][j])
    S(Ident, "zt1", "idx lh", T.zt[:, 0:256], T.idx[:, 0:256], scale=lo)
    S(Ident, "zt2", "idx lh", T.zt[:, 256:512], T.idx[:, 0:256], scale=hi)
    S(Copy, "zb", "pz", T.zb[:, 0:WCOLS], T.pz[:, 0:WCOLS])
    S(Sign, "lm", "c16 sk", T.lm[:], T.c16[:, 0:64], bias=tf, scale=-1.0)
    S(Ident, "trs", "sk", T.fc[:, 16:20], T.fc[:, 0:4], bias=1032.0, scale=8.0)
    V("copy", "gs", "pb0 pb1 lgs", T.gs[:], T.pb[:].indirect(T.lgs[:, 2:4]))
    V("tt", "eqt", "pbx0 pbx1 lgs gs", eqt, T.pbx[:].indirect(T.lgs[:, 4:6]), T.gs[:], op_.is_equal)
    V("tt", "gt", "pbx0 pbx1 lgs gs", gt, T.pbx[:].indirect(T.lgs[:, 4:6]), T.gs[:], op_.is_gt)
    V("tt", "ge2", "pb0 pb1 lgs gs", T.ge2[:], T.pb[:].indirect(T.lgs[:, 0:2]), T.gs[:], op_.is_ge)
    V("tt", "el", "eqt lw0 lw1", el, eqt, T.lw[:], op_.mult)
    for j in range(2):
        a = 16 * j
        V("scan", "sc%d" % j, "gt el", T.qa[:, 96 + a:112 + a], T.qa[:, 32 + a:48 + a], T.qa[:, 64 + a:80 + a], float(1 + 17 * j), op_.add, op_.add)
    V("copy", "rku", "sc0 sc1", T.rku[:], T.qa[:, 111:128:16])
    V("copy", "bsw", "ge2 rku", T.bsw[:].indirect(T.rku[:]), T.ge2[:])
    V("copy", "nsw", "nrz0 nrz1 rku", T.nsw[:].indirect(T.rku[:]), T.nrz[:])
    V("scan", "pk", "bsw r17", T.pk[:], T.r17[:], T.bsw[:, 0:34], 0.0, op_.mult, op_.add)
    V("tt", "ns", "nsw", ns, T.nsw[:, 1:9], T.nsw[:, 18:26], op_.add)
    V("copy", "pku", "pk", T.pku[:], T.pk[:, 8:26:17])
    V("copy", "own", "zt1 zt2 pku", T.own[:], T.zt[:].indirect(T.pku[:]))
    V("copy", "msw", "own rku", T.msw[:].indirect(T.rku[:]), T.own[:])
    V("tt", "ms", "msw", T.ms[:], T.msw[:, 1:9], T.msw[:, 18:26], op_.add)

    def plane(m):
        V("ts", "ui%d" % m, "ms", T.ui[:, 8 * m:8 * m + 8], T.ms[:], 7 - m, 1, op_.logical_shift_right, op_.bitwise_and)

    def pair(m, j):
        V("ts", "fv%d" % j, "ui%d fv%d fv%d" % (m, m, j), T.fv[:, j:j + 1], T.ui[:, 8 * m + j:8 * m + j + 1], T.fv[:, m:m + 1],
          T.fv[:, j:j + 1], op_.subtract, op_.max)

    def far(m):
        a = m + 3
        V("ts", "tmp%d" % m, "ui%d fv%d" % (m, m), T.pn[:, 24 + 8 * m + a:32 + 8 * m], T.ui[:, 8 * m + a:8 * m + 8], T.fv[:, m:m + 1], None, op_.subtract)

    def far2(m):
        a = m + 3
        k = " ".join("fv%d" % j for j in range(a, 8))
        V("tt", k, "tmp%d " % m + k, T.fv[:, a:8], T.fv[:, a:8], T.pn[:, 24 + 8 * m + a:32 + 8 * m], op_.max)

    V("ts", "fv1 fv2 fv3 fv4 fv5 fv6 fv7", "ms", T.fv[:, 1:8], T.ms[:, 1:8], 128.0, None, op_.is_ge)
    plane(1)
    plane(2)
    pair(1, 2)
    pair(1, 3)
    far(1)
    plane(3)
    pair(2, 3)
    far2(1)
    plane(4)
    pair(2, 4)
    far(2)
    plane(5)
    pair(3, 4)
    far2(2)
    plane(6)
    for m in range(3, 7):
        for j in range(m + 1, 8):
            if (m, j) != (3, 4):
                pair(m, j)
    fvs = "fv0 fv1 fv2 fv3 fv4 fv5 fv6 fv7"
    V("ts", "nf", fvs, nf, T.fv[:], 0.0, None, op_.is_equal)
    V("scan", "psn", fvs + " one", psn, T.one[:, 0:8], T.fv[:], 0.0, op_.add, op_.subtract)
    V("tt", "kn", "ns nf", kn, ns, nf, op_.mult)
    V("tt", "eq", "psn c4 lrep", eq, psn.indirect(T.lrep[:]), T.c4[:], op_.is_equal)
    V("tt", "v4", "eq kn lrep", v4, kn.indirect(T.lrep[:]), eq, op_.mult)
    V("scan", "sc8", "v4 r8", sc8, T.r8[:], v4, 0.0, op_.mult, op_.add)
    V("copy", "klu", "sc8", T.klu[:], T.qb[:, 71:96:8])
    for a in range(0, 2048, 448):
        w = min(448, 2048 - a)
        S(Copy, "ebz", "xtz", T.ebt[:, a:a + w], T.xt[:, 64:64 + w])
    for b in range(4):
        S(Copy, "ebt", "hid ebz", T.ebt[:, 512 * b + b:512 * b + 512:4], T.hid[:], scale=0.5)
    S(Relu, "lm", "lm", T.lm[:], T.lm[:])
    for k in range(8):
        dma("s" if k % 2 == 0 else "a", "drep", T.kru[16 * k:16 * k + 16, :], T.klu[0:128:8, :], "klu", "kru")
    dma("s", "dkx", u8(T.pwc[:, 16 * r:16 * r + 16]), u8(T.xc[:, 0:16]), "xc", "pwo")
    dma("s", "dkx", T.pws[:, 16 * r:16 * r + 16], T.xs[:, 0:16], "xs", "pwo")
    V("qz", "ec es", "ebt ebz", T.ec[:], T.es[:], T.ebt[:])
    for b in range(4):
        mm(T["pd%d" % b][:, 0:P], T.ec[:, P * b:P * b + P], T.es[:, P * b:P * b + P], T.tbc[:], T.tbs[:], True, False, "ec es tbc tbs", "pd%d" % b)
    S(Copy, "zbz", "xtz", T.zb[:, WCOLS:480], T.xt[:, 64:80])
    for k in ("wno", "wns", "wnc"):
        S(Copy, k, "one", T[k][:, P * r + 1:P * r + 1 + P], T.one[:], scale=float(P))
    S(Copy, "wmb", "wm", T.wmb[:], T.wm[:, 0:P])
    S(Sign, "r16b", "c16", T.r16b[:], T.c16[:, 0:P])

    V("copy", "kr", "kru", T.kr[:], T.kru[:])
    V("tt", "rwm", "idx idxs kru lm", T.rwm[:], T.idx[:].indirect(T.kru[:]), T.lm[:], op_.mult)
    for k in range(4):
        V("ts", "eqd%d" % k, "rwm kr trs", T.eqd[:, 64 * k:64 * k + 64], T.rwm[:], T.kr[:, k:k + 1], trs[k], op_.is_equal, op_.mult)
    for k in range(4):
        V("scan", "scf%d" % k, "eqd%d kr one" % k, T.scf[:, 64 * k:64 * k + 64], T.one[:, 0:64], T.eqd[:, 64 * k:64 * k + 64], T.kr[:, k:k + 1], op_.mult, op_.max)
    V("copy", "lu", "scf0 scf1 scf2 scf3", T.lu[:], T.scf[:, 63:256:64])
    send([(T.lu[:], [T.lr[:]] * 2, ids_r[0:2], eon, "r_kl")], "lu")
    send([(T.lu[:], [T.ll[:, 4 * at_s[y]:4 * at_s[y] + 4]], [ids_s[y]], e_s[y], "a_kls") for y in range(3)], "lu")

    S(Copy, "locr", "loc locz locy kru", T.locr[:, 0:64], T.loc[:].indirect(T.kru[:]))
    S(Ident, "kpf", "idx idxs kru", T.kpf[:], T.idx[:].indirect(T.kru[:]), bias=-1.0)
    dma("s", "dkp", T.kp[:], T.kpf[0:1, :], "kpf", "kp")
    s = P * r + 1
    V("copy", "wno", "val lu", T.wno[:].indirect(T.lu[:]), T.val[:, 64 * r:64 * r + 64])
    V("tt", "loc2", "locr wm", T.locr[:, 64:128], T.locr[:, 0:64], T.wm[:, 0:64], op_.mult)
    V("tt", "wsmo", "wno wmb", T.wsm[:, 3 * P:4 * P], T.wno[:, s:s + P], T.wmb[:], op_.mult)
    V("scan", "loc3", "loc2 r16", T.locr[:, 128:192], T.r16[:, 0:64], T.locr[:, 64:128], 0.0, op_.mult, op_.add)
    V("copy", "yl", "loc3", T.yl[:, 0:8:2], T.locr[:, 143:192:16])
    for k in range(4):
        S(Copy, "yb", "zb zbz yl", T.yb[:, k:64:4], T.zb[:].indirect(T.yl[:, 2 * k:2 * k + 1]))
    dma("s", "dy", T.y[:], T.yb[:], "yb", "y")

    tot["a_kls"] = sum(len(e_s[f]) for f in from_s)
    tot["a_klc"] = 4 * noff // 2
    wr_["lls"] = [("a_kls", tot["a_kls"])]
    wr_["llc"] = [("a_klc", tot["a_klc"])]
    for q in sorted(same, reverse=True):
        c = 4 * peers.index(q)
        V("copy", "wns", "val lls", T.wns[:].indirect(T.ll[:, c:c + 4]), T.val[:, 64 * q:64 * q + 64])
    V("tt", "wsm0", "wns wsmo", T.wsm[:, 0:P], T.wns[:, s:s + P], T.wsm[:, 3 * P:4 * P], op_.min)
    for q in sorted(cross, reverse=True):
        c = 4 * peers.index(q)
        V("copy", "wnc", "val llc", T.wnc[:].indirect(T.ll[:, c:c + 4]), T.val[:, 64 * q:64 * q + 64])
    V("tt", "wsm1", "wsm0 wnc", T.wsm[:, P:2 * P], T.wsm[:, 0:P], T.wnc[:, s:s + P], op_.min)
    V("scan", "wsm2", "wsm1 r16b", T.wsm[:, 2 * P:3 * P], T.r16b[:], T.wsm[:, P:2 * P], 0.0, op_.mult, op_.add)
    won = T.wsm[:, 2 * P + 15:3 * P:16]
    V("ts", "wu", "wsm2", T.wu[:], won, float(P - 1), None, op_.min)
    tot["a_pt"] = 7 * 2 * noff
    wr_["pwa"] = [("a_pt", tot["a_pt"])]
    S(Copy, "pps", "pwa pwo wu", T.pps[:], T.pws[:].indirect(T.wu[:]))
    V("copy", "ppc", "pwa pwo wu", u32(T.ppc[:]), u32(T.pwc[:]).indirect(T.wu[:]))
    for b in range(4):
        mm(T["pd%d" % b][:, 0:P], T.ec[:, P * b:P * b + P], T.es[:, P * b:P * b + P], T.ppc[:], T.pps[:], False, True, "ec es ppc pps", "pd%d" % b)
    V("ts", "wl", "wsm2", T.wl[:], won, float(P), float(P), op_.is_lt, op_.mult)
    V("tt", "wl", "wl sk", T.wl[:], T.wl[:], T.fc[:, 0:8], op_.add)
    V("copy", "fl", "wl", T.fl[:], T.wl[:])
    for b in range(4):
        o, i = T.nt[:, b:512:4], T["pd%d" % b][:, 0:P]
        if b % 2 == 0:
            V("copy", "nt%d" % b, "pd%d" % b, o, i)
        else:
            S(Copy, "nt%d" % b, "pd%d" % b, o, i)
    V("qz", "fwn fsn", "nt0 nt1 nt2 nt3", T.fwc[:, P:2 * P], T.fws[:, P:2 * P], T.nt[:])
    S(Copy, "fos", "fso fsn fl", T.fos[:], T.fws[:].indirect(T.fl[:]))
    V("copy", "foc", "fwo fwn fl", u32(T.foc[:]), u32(T.fwc[:]).indirect(T.fl[:]))
    dma("s", "doc", T.oc[:], u8(T.foc[:]), "foc", "oc")
    for k in range(4):
        dma("a" if k < 3 else "s", "doc", T.osc[4 * k:4 * k + 4, :], T.fos[32 * k:32 * k + 4, :], "fos", "osc")
    need("g", [(x, tot[x]) for x in tot])
